import numpy as np, ml_dtypes
CORES = [113,118,241,246]
N = 4
BF = ml_dtypes.bfloat16
M, C, W, RO = 96, 32, 4096, 6
TOP = 255 * N * C
def settle(rng, e):
    x = np.add.accumulate(e, axis=3); x = x - np.min(x, axis=3, keepdims=True); top = np.max(x, axis=3, keepdims=True)
    return x + 32 + (rng.random(top.shape) * (169 - top)).astype(np.int64)
def parts(rng):
    e = rng.integers(-3, 4, (8, 16, M, 8)); x = settle(rng, rng.permuted(np.concatenate([e, -e], axis=3), axis=3))
    s = np.argsort(rng.random((8, 16, M)), axis=1); miss = rng.integers(0, 16, (8, M))
    u = N * C * 127 + rng.integers(-600, 601, (8, 16, M))
    return x, s, miss, u, rng.integers(0, 256, (N, 8, 16, W)), rng.integers(0, 128, (N, 8, 16, C))
def pack(x, s, miss, u, d, a):
    n = np.where(np.arange(16)[:, None] == miss[:, None, :], -1, s)
    def same(y): return np.repeat(np.ascontiguousarray(y).reshape(1, 128, -1), N, axis=0)
    return {"v": same(x).astype(np.float32).astype(BF), "inv": same(n).astype(np.int32), "sup": same(u).astype(np.int32),
            "dem": d.reshape(N, 128, W).astype(np.float32).astype(BF), "wt": np.ascontiguousarray(a).reshape(N, 128, C).astype(np.float32).astype(BF)}
def newcomer(s, miss):
    return np.take_along_axis(s, miss[:, None, :], 1)[:, 0]
def climb(rng, x, s, miss, u, d, a, g):
    o = rng.permutation(16); turn = rng.integers(0, 16, M); j = (np.arange(16) - turn[:, None]) % 16
    key = int(rng.integers(0, 16)); b = int(rng.integers(32, 177))
    far = np.where(rng.random((16, M, 1)) < 0.5, 32 + 3 * (j & 1), 200 - 3 * (j & 1))
    x[g] = np.where(rng.random((16, M, 1)) < 0.5, far, x[g]); x[g, key] = b + 3 * np.minimum(j, 16 - j)
    t = np.zeros((16, M), np.int64); t[o[:5]] = np.arange(1, 6)[:, None]
    t[o[5:]] = rng.permuted(np.repeat(np.array([0, 6, 7, 8, 9, 10, 11, 12, 13, 14, 15])[:, None], M, axis=1), axis=0)
    s[g] = (t + turn) % 16; miss[g] = np.argmax(t == 8, axis=0)
    u[g] = rng.integers(0, 128 * N * C, (16, M)); d[:, g] = rng.integers(0, 64, (N, 16, W)); a[:, g] = 0; a[:, g, key] = 1
    at = [-1] + [int(y) for y in o[:5]] + [-1] * 10; c = 8
    for w in [int(y) for y in rng.permutation(np.array([1, 3, 5]))] + [int(y) for y in rng.permutation(np.array([2, 4]))] + [3]:
        d[:, g, at[w], b + 3 * c] = 255; at[c] = at[w]; c = w
def setup_inputs(rng):
    return pack(*parts(rng))
def setup_inputs_alike(rng):
    x, s, miss, u, d, a = parts(rng)
    for g in (0, 2, 5, 7): x[g] = x[g][:, :1]; s[g] = s[g][:, :1]; miss[g] = miss[g, 0]; u[g] = u[g][:, :1]
    for g in (1, 2, 6, 7): a[:, g] = a[:, g, :, :1]
    for y in (d, a): y[:, 3] = y[:1, 3].copy(); y[1, 4] = y[0, 4]
    return pack(x, s, miss, u, d, a)
def setup_inputs_ends(rng):
    x, s, miss, u, d, a = parts(rng)
    e = rng.permuted(np.broadcast_to(np.repeat(np.array([3, -3]), 8), (8, 16, M, 16)).copy(), axis=3); e[:, ::2] = np.sort(e[:, ::2], axis=3)
    x = np.add.accumulate(e, axis=3); x = x - np.min(x, axis=3, keepdims=True); top = np.max(x, axis=3, keepdims=True)
    low = rng.random(top.shape) < 0.5; low[3] = False
    x = x + np.where(low, 32, 200 - top); c = newcomer(s, miss)
    for g in range(8):
        for i in (14, 15): x[g, i, 0] += 50 + i - x[g, i, 0, c[g, 0]]
    a = 127 * rng.integers(0, 2, a.shape); a[..., 0] = 0; a[..., 3] = 0; a[:, :, 5, 3] = 1
    a[:, 3, :, 4:] = 127 - rng.integers(0, 16, (N, 16, C - 4)); a[:, 3, :, 4] = 127
    for r in range(N):
        for g in range(8):
            p = x[g, :, 0, c[g, 0]]
            for j, t in ((1, W - 1), (2, 0)):
                b = rng.integers(0, 128, 16); k = int(t - np.sum(b[:14] * p[:14])) % W
                b[15] = k % 64; b[14] = (k // 64 - k % 64) % (W // 64); a[r, g, :, j] = b
    d[..., 0] = 255 * rng.integers(0, 2, (N, 8, 16)); d[..., W - 1] = 255 * rng.integers(0, 2, (N, 8, 16))
    m = rng.integers(0, 600, (8, 16, M)); u = np.where(rng.random((8, 1, M)) < 0.5, m, TOP - m)
    few = rng.integers(0, 3, (2, 16, M)) * (rng.random((2, 1, M)) < 0.5)
    d[:, 1, :, :W - 1] = 255 - (rng.random((N, 16, W - 1)) < 1.0 / C); u[1] = few[0]
    d[:, 4, :, :W - 1] = rng.integers(200, 256, (N, 16, W - 1)); u[4] = rng.integers(0, 256, (16, M))
    d[:, 6, :, :W - 1] = rng.random((N, 16, W - 1)) < 1.0 / C; u[6] = TOP - few[1]
    climb(rng, x, s, miss, u, d, a, 7)
    return pack(x, s, miss, u, d, a)
def setup_inputs_rest(rng):
    x, s, miss, u, d, a = parts(rng); d = rng.integers(1, 255, d.shape); c = newcomer(s, miss)
    kind = rng.integers(0, 4, (8, M)); kind[0] = 0; kind[1] = rng.integers(1, 3, M)
    end = np.where(rng.random((8, M)) < 0.5, 0, 15); end = np.where(end == c, 15 - end, end)
    near = (c + np.where(rng.random((8, M)) < 0.5, 1, 15)) % 16
    want = np.where(kind == 0, c, np.where(kind == 1, end, near))
    fav = np.take_along_axis(np.argsort(s, axis=1), want[:, None, :], 1)
    lab = rng.integers(0, 16, (8, 1, M)); lab[1:] = int(rng.integers(0, 16))
    s = np.take_along_axis(s, (np.arange(16)[:, None] + fav - lab) % 16, 1); miss = (miss - (fav - lab)[:, 0]) % 16
    u = np.where((kind == 3)[:, None, :], u, np.where(np.arange(16)[:, None] == lab, 0, TOP))
    return pack(x, s, miss, u, d, a)
def setup_inputs_ties(rng):
    x, s, miss, u, d, a = parts(rng)
    d = 255 * (rng.random(d.shape) < 1.0 / (N * C)).astype(np.int64); d[:, 3] = 0
    u = np.repeat(255 * rng.choice(np.array([0, 1, N * C // 2, N * C - 1]), (8, 1, M)), 16, axis=1)
    u[::2] = u[::2] + 255 * rng.integers(0, 2, u[::2].shape)
    u[3] = 255 * rng.choice(np.array([0, 1, N * C // 2, N * C]), (1, M))
    return pack(x, s, miss, u, d, a)
def setup_inputs_spread(rng):
    x, s, miss, u, d, a = parts(rng)
    d = (np.exp2(8 * rng.random((N, 8, 1, W))) * rng.random(d.shape)).astype(np.int64)
    a = np.exp2(7 * rng.random(a.shape)).astype(np.int64) * (rng.random(a.shape) > 0.0625)
    return pack(x, s, miss, rng.integers(0, 2 * N * C, u.shape), d, a)
def check_inputs(d):
    bad = []
    for k, lo, hi in (("v", 32, 200), ("sup", 0, TOP), ("dem", 0, 255), ("wt", 0, 127)):
        y = np.asarray(d[k]).astype(np.float64)
        if not np.all((y >= lo) & (y <= hi) & (y == np.floor(y))): bad.append("range of " + k)
    x = np.asarray(d["v"]).astype(np.float64).reshape(N, 8, 16, M, 16)
    if not np.all(np.abs(np.roll(x, -1, axis=4) - x) <= 3): bad.append("ring neighbours in v")
    s = np.sort(np.asarray(d["inv"]).astype(np.int64).reshape(N, 8, 16, M), axis=2)
    if not (np.all(s[:, :, 0] == -1) and np.all(s[:, :, 1] >= 0) and np.all(s[:, :, 15] <= 15) and np.all(s[:, :, 1:] > s[:, :, :-1])): bad.append("slots in inv")
    for k in ("v", "inv", "sup"):
        y = np.asarray(d[k]).astype(np.float64)
        if not np.all(y == y[:1]): bad.append(k + " is not the same on all ranks")
    return bad
def reference(v, inv, sup, dem, wt):
    x = v[0].astype(np.float32).astype(np.int64).reshape(8, 16, M, 16); n = inv[0].astype(np.int64).reshape(8, 16, M); u = sup[0].astype(np.int64).reshape(8, 16, M)
    d = dem.astype(np.float32).astype(np.int64).reshape(N, 8, 16, W); a = wt.astype(np.float32).astype(np.int64).reshape(N, 8, 16, C).transpose(0, 1, 3, 2)
    row = np.arange(16)[:, None]; slot = np.arange(16)
    def pick(k): return np.take_along_axis(x, (k & 15)[:, None, :, None], 3)[..., 0]
    c = 119 - np.add.reduce(n, axis=1)
    for step in range(RO):
        p = pick(c)
        h = np.matmul(a, p[None]) & (W - 1)
        z = np.add.reduce(np.take_along_axis(d, h.reshape(N, 8, 1, C * M), 3).reshape(N, 8, 16, C, M), axis=(0, 3)) - u
        l = np.argmax(z, axis=1)
        s = np.take_along_axis(n, l[:, None, :], 1)[:, 0]; go = s >= 0
        new = pick(s - 1) + pick(s + 1) - pick(s)
        x = np.where((slot == s[:, None, :, None]) & go[:, None, :, None], new[..., None], x)
        n = np.where((row == l[:, None, :]) & go[:, None, :], c[:, None, :], n)
        c = np.where(go, s, c)
    return {"yv": np.repeat(x.reshape(1, 128, 16 * M), N, axis=0).astype(np.float32).astype(BF), "yi": np.repeat(n.reshape(1, 128, M), N, axis=0).astype(np.float32)}

@@ -1,0 +1,512 @@
+from concourse.bass import DstId, RemoteDMATransfer
+from concourse.mybir import AluOpType as ALU, AxisListType as AX, ActivationFunctionType as AF
+
+N, Q, NC, RO = 4, 48, 2, 6
+ROWS = 19
+CR = 402653184.0
+CH = 526336.5
+CO = 528384.0
+PIECES = [("dve", 0, 24), ("act", 24, 48), ("dve", 48, 56), ("dve", 56, 64), ("act", 64, 96)]
+PIECES2 = [("dve", 0, 24), ("act", 24, 48), ("dve", 48, 54), ("dve", 54, 60), ("act", 60, 96)]
+PIECES_END = [("dve", 0, 24), ("act", 24, 48), ("dve", 48, 72), ("act", 72, 96)]
+T2 = 6
+BATCH = [(1, 3), (4, 2), (6, 1)]
+HOP, BIAS, WIN, JIT, SEED = 130.0, 1500.0, 60.0, 0.0, 1
+GAM, SIG, CYC, PEC = 1.7, 3.8, 1.0, 0.6
+
+SCRATCH = {
+    "stg": ("dram", [8, 128, 512], "bfloat16"), "lnd": ("dram", [8, 128, 512], "bfloat16"),
+}
+for _d, _l in (("bfloat16", "TB 4096 VN 3072 VR 1536 VO 1536 RP 128 WS 32 WA 128 WK 256 KS 96 RS 32 CN 96 AT 768 SM 256 SG 128 "
+                            "SR 32 NI 128 IQ 48 SO 34 N1 64 RN 256 ZR 96 RA 96 RB 96 RC 96"),
+               ("int32", "IV 96 SU 96 SU2 96 PI 1 PJ 4 I1 76 I2 76 I3 76 BS 60 BS2 60 DF 30 DB 30 DX 90 DY 90 DZ 90"),
+               ("float32", "CA 96 CB 96 CAP 96 YI 96 PF 16 J128 128 JJ 128 JX 128 PA 6"),
+               ("uint16", "IU 76 OG 36 R0 120 R1 120 R2 120 R3 120 DU0 90 DU1 90 DU2 90 DU3 90")):
+    _l = _l.split()
+    for _k in range(0, len(_l), 2):
+        SCRATCH[_l[_k]] = ("sbuf", [128, int(_l[_k + 1])], _d)
+for _c in range(NC):
+    for _n, _s, _d in (("X", ROWS * 64, "bfloat16"), ("G", 1536, "bfloat16"), ("O", 96, "uint16"), ("OS", 4, "uint16"),
+                       ("G3", 64, "bfloat16"), ("RR", 96, "bfloat16"), ("NV", 48, "bfloat16"), ("E", 14, "bfloat16"),
+                       ("MX", 2, "float32"), ("RQ", 2, "float32"), ("F", 2, "float32"), ("D", 2, "float32"),
+                       ("DL", 192, "bfloat16")):
+        SCRATCH["%s%d" % (_n, _c)] = ("sbuf", [128, _s], _d)
+    for _n in ("pK", "pT", "pH", "pG"):
+        SCRATCH["%s%d" % (_n, _c)] = ("psum", [128, 512], "float32")
+
+SEMAPHORES = (["q_pe", "q_dve", "q_act", "q_g", "ls"] + ["d%d" % k for k in range(32)]
+              + ["a%s%d" % (n, r) for n in ("w", "t0", "t1", "t2", "t3", "o0", "o1", "o2", "o3", "n") for r in range(N)])
+
+
+def _engine_sets(topo, cores, src):
+    peers = [c for c in cores if c != src]
+    every = {c: list(topo.engines(src, c)) for c in peers}
+    few = min(len(e) for e in every.values())
+    far = [c for c in peers if len(every[c]) == few]
+    near = [c for c in peers if c not in far]
+    out, used = {}, []
+    share = few // len(far)
+    for k, c in enumerate(far):
+        out[c] = every[c][k * share:(k + 1) * share]
+        used += out[c]
+    for c in near:
+        out[c] = [e for e in every[c] if e not in used]
+        used += out[c]
+    return far, near, out
+
+
+def build(g, core, T, topo):
+    rho = T.rank_of(core)
+    cores = list(T.cores)
+    far, near, eng = _engine_sets(topo, cores, core)
+    rk = {c: T.rank_of(c) for c in cores}
+    ops = []
+    last_w, readers, bank = {}, {}, {}
+    prev_fixed = {}
+    ndma = [0]
+    cur = [None]
+
+    def add(q, fn, r, w, dur, lat=0.0, kind="c", sem=None, cnt=0, fixed=False):
+        i = len(ops)
+        deps = set()
+        for x in list(r) + list(w):
+            if x[0] == "p":
+                for j in bank.get(x, []):
+                    if ops[j]["q"] != q:
+                        deps.add(j)
+        for x in r:
+            if x in last_w:
+                deps.add(last_w[x])
+        for x in w:
+            if x in last_w:
+                deps.add(last_w[x])
+            deps.update(readers.get(x, []))
+        for x in r:
+            readers.setdefault(x, []).append(i)
+        for x in w:
+            last_w[x] = i
+            readers[x] = []
+        for x in set(list(r) + list(w)):
+            if x[0] == "p":
+                old = bank.get(x, [])
+                bank[x] = (old if old and ops[old[0]]["q"] == q else []) + [i]
+        deps.discard(i)
+        order = set()
+        if q == "pe":
+            order = {j for j in deps if ops[j]["q"] == "pe"}
+            deps -= order
+        if fixed:
+            if q in prev_fixed:
+                order.add(prev_fixed[q])
+            prev_fixed[q] = i
+        if kind == "dma":
+            sem, cnt = "d%d" % ndma[0], 16
+            ndma[0] += 1
+        ops.append(dict(ch=cur[0], q=q, fn=fn, deps=deps, order=order, dur=dur, lat=lat, kind=kind, sem=sem, cnt=cnt))
+        return i
+
+    V_, S_, P_ = g.vector, g.scalar, g.tensor
+
+    def vcost(n, f=1.0):
+        return 15.0 + max(64.0, n * f) * CYC
+
+    def ga(n):
+        return 60.0 + GAM * n
+
+    def sc(n):
+        return 60.0 + SIG * n
+
+    def ts(out, in0, s1, s2, o0, o1, r, w, n=1):
+        if o1 is None:
+            add("dve", lambda: V_.tensor_scalar(out, in0, s1, None, o0), r, w, vcost(n))
+        else:
+            add("dve", lambda: V_.tensor_scalar(out, in0, s1, s2, o0, o1), r, w, vcost(n))
+
+    def tt(out, a, b, op, r, w, n=1, dur=None):
+        add("dve", lambda: V_.tensor_tensor(out, a, b, op), r, w, dur or vcost(n, 2.0))
+
+    def cp(out, a, r, w, n=1, dur=None):
+        add("dve", lambda: V_.tensor_copy(out, a), r, w, dur or vcost(n))
+
+    def ms(ap, val, w, n=1):
+        add("dve", lambda: V_.memset(ap, val), [], w, vcost(n, 0.5))
+
+    def act(out, a, r, w, n=1, dur=None, bias=None):
+        if bias is None:
+            add("act", lambda: S_.activation(out, a, AF.Identity), r, w, dur or vcost(n))
+        else:
+            add("act", lambda: S_.activation(out, a, AF.Identity, bias=bias), r, w, dur or vcost(n))
+
+    def mm(out, l, rr, st, sp, r, w, m, n):
+        add("pe", lambda: P_.matmul(out, l, rr, st, sp), r, w, 5.0 + max(min(64, m), n) * PEC)
+
+    def dma(q, out, a, r, w, nbytes):
+        e = {"sync": g.sync, "act": g.scalar}[q]
+        add(q, lambda: e.dma_start(out, a), r, w, 100.0, lat=1800.0 + nbytes / 200.0, kind="dma", fixed=True)
+
+    def iota(out, pat, base, cm, w, n, flt):
+        if flt:
+            add("g", lambda: g.iota(out, pat, base, cm, allow_small_or_imprecise_dtypes=True), [], w, 150.0 + 2 * n, fixed=True)
+        else:
+            add("g", lambda: g.iota(out, pat, base, cm), [], w, 150.0 + 2 * n, fixed=True)
+
+    def gcp(out, a, r, w):
+        add("g", lambda: g.affine_select(out, a, [[0, Q]], ALU.is_ge, 0.0, 0, 0), r, w, 200.0 + 2 * Q * CYC)
+
+    def send(name, src, dst, r, w_in, lat):
+        def fn():
+            trs = []
+            for c in far + near:
+                rid, pid = topo.addr(c, core)
+                trs.append(RemoteDMATransfer(dst_ids=[DstId(rid=rid, pnc=pid)], dma_engine_mask=sum(1 << e for e in eng[c]),
+                                             remote_sem=T.sem["a%s%d" % (name, rho)], src=src(rk[c]), dst=dst))
+            return g.remote_dma_fused(trs, local_sem=T.sem["ls"])
+        i = add("g", fn, r, [], 700.0, kind="send", cnt=sum(len(e) for e in eng.values()), fixed=True)
+        for c in near + far:
+            k = len(_engine_sets(topo, cores, c)[2][core])
+            j = add("rx", None, [], [w_in(rk[c])], 0.0, lat=lat * (0.6 if c in near else 1.0), kind="rx",
+                    sem="a%s%d" % (name, rk[c]), cnt=k)
+            ops[j]["order"].add(i)
+
+    o32 = 32 * rho
+    dma("act", T.WS[:], T.wt[:], [], ["WS"], 8192)
+    order_ = [rk[c] for c in far + near]
+    for m in range(2):
+        for k, r in enumerate(order_):
+            gq = 2 * r + m
+            dma("act" if k == 1 else "sync", T.stg[gq], T.dem[16 * gq:16 * gq + 16, :], [], ["stg%d" % gq], 131072 * 3)
+    dma("act", T.IV[:], T.inv[:], [], ["IV"], 49152)
+    dma("act", T.VO[0:32, :], T.v[o32:o32 + 32, :], [], ["VO"], 400000)
+    dma("act", T.SU[0:32, :], T.sup[o32:o32 + 32, :], [], ["SUa"], 12288)
+    dma("act", T.SU[32:64, :], T.sup[o32:o32 + 32, :], [], ["SUb"], 12288)
+    dma("act", T.WA[:, o32:o32 + 32], T.wt[:], [], ["WA%d" % rho], 8192)
+    iota(T.PI[:], [[0, 1]], 0, 1, ["PI"], 1, False)
+    iota(T.JJ[:], [[0, 4], [1, 32]], 0, 0, ["JJ"], 128, True)
+    iota(T.I1[:], [[1, ROWS], [0, 4]], 15, 0, ["I1"], 76, False)
+    iota(T.I2[:], [[0, ROWS], [256, 4]], 0, 0, ["I2"], 76, False)
+    iota(T.JX[:], [[0, 4], [1000, 2], [1, 16]], 0, 0, ["JX"], 128, True)
+    iota(T.PA[:], [[-16, 3], [1000, 2]], 0, 1, ["PA"], 6, True)
+    send("w", lambda r: T.WS[:], T.WA[:, o32:o32 + 32], ["WS"], lambda r: "WA%d" % r, 4000.0)
+    for m in range(2):
+        send("t%d" % m, lambda r, m=m: T.stg[2 * r + m], T.lnd[2 * rho + m],
+             ["stg%d" % (2 * r + m) for r in order_], lambda r, m=m: "lnd%d" % (2 * r + m), 5000.0 + 3000.0 * m)
+    iota(T.J128[:], [[1, 128]], 0, 0, ["J128"], 128, True)
+    iota(T.BS[:], [[0, 10], [256, 6]], 0, 0, ["BS"], 60, False)
+    for m in range(2):
+        for c in near + far:
+            gq = 2 * rk[c] + m
+            dma("sync", T.TB[16 * gq:16 * gq + 16, :], T.lnd[gq], ["lnd%d" % gq], ["TB%d" % gq], 131072)
+            if m == 0 and c == near[0]:
+                dma("sync", T.TB[o32:o32 + 32, :], T.dem[o32:o32 + 32, :], [], ["TB%d" % (2 * rho)], 262144)
+    dma("sync", T.VN[:, 0:1536], T.v[:], [], ["V"], 393216)
+    TBall = ["TB%d" % k for k in range(8) if k != 2 * rho + 1]
+
+    PF = lambda k, a=0, b=128: T.PF[a:b, k:k + 1]
+    cp(PF(0), T.PI[:], ["PI"], ["F0"])
+    ts(T.PJ[:, 0:1], T.PI[:], 31, None, ALU.bitwise_and, None, ["PI"], ["J0"])
+    ts(T.PJ[:, 1:2], T.PI[:], 15, None, ALU.bitwise_and, None, ["PI"], ["J1"])
+    ts(T.PJ[:, 2:3], T.PI[:], 4, None, ALU.arith_shift_right, None, ["PI"], ["J2"])
+    cp(T.PF[:, 1:4], T.PJ[:, 0:3], ["J0", "J1", "J2"], ["F1"])
+    ts(PF(4), PF(0), float(-o32), None, ALU.add, None, ["F0"], ["F4"])
+    ms(PF(5, 0, 32), 1.0, ["F5a"]); ms(PF(5, 32, 64), -1.0, ["F5b"]); ms(PF(5, 64, 128), 0.0, ["F5c"])
+    F5 = ["F5a", "F5b", "F5c"]
+    ms(PF(6, 0, 64), 1.0, ["F6a"]); ms(PF(6, 64, 128), -1.0, ["F6b"])
+    F6 = ["F6a", "F6b"]
+    ts(PF(7), PF(5), -64.0, PF(2), ALU.mult, ALU.add, F5 + ["F1"], ["F7"])
+    ts(PF(8), PF(2), 16.0, None, ALU.mult, None, ["F1"], ["F8"])
+    for m in range(2):
+        ts(PF(9 + m), PF(3), float(2 * rho + m), None, ALU.is_equal, None, ["F1"], ["F9%d" % m])
+    ms(PF(11, 0, 32), -65536.0, ["F11a"]); ms(PF(11, 32, 64), -512.0, ["F11b"])
+    for qh in range(3):
+        for m in range(2):
+            k = 2 * qh + m
+            ts(T.AT[0:64, 128 * k:128 * k + 128], T.JX[0:64, :], T.PA[0:64, k:k + 1], 64.0, ALU.is_equal, ALU.mult, ["JX", "PA"], ["A%d" % k], 128)
+        ms(T.AT[64:65, 256 * qh:256 * qh + 128], 576.0 + 16 * qh, ["Ac%d" % qh])
+    for m in range(2):
+        ts(T.SM[:, 128 * m:128 * m + 128], T.JJ[:], PF(4), PF(9 + m), ALU.is_equal, ALU.mult, ["JJ", "F4", "F9%d" % m], ["SM%d" % m], 128)
+        ts(T.SO[:, 32 + m:33 + m], PF(9 + m), -1.0, None, ALU.mult, None, ["F9%d" % m], ["SO%d" % m])
+        ts(T.RS[64:65, 16 * m:16 * m + 16], T.JX[64:65, 0:16], -32.0, 480.0, ALU.mult, ALU.add, ["JX"], ["RSc%d" % m])
+    ts(T.SO[:, 0:32], T.JJ[:, 0:32], PF(4), None, ALU.is_equal, None, ["JJ", "F4"], ["SO"])
+    ts(T.SG[:], T.JJ[:], PF(1), PF(6), ALU.is_equal, ALU.mult, ["JJ", "F1"] + F6, ["SG"], 128)
+    ts(T.SR[:], T.JJ[:, 0:32], PF(1), 512.0, ALU.is_equal, ALU.mult, ["JJ", "F1"], ["SR"])
+    ts(T.RS[0:64, :], T.JJ[0:64, 0:32], PF(1, 0, 64), PF(11, 0, 64), ALU.is_equal, ALU.mult, ["JJ", "F1", "F11a", "F11b"], ["RS"])
+    ts(T.NI[:], T.J128[:], PF(0), -1.0, ALU.is_equal, ALU.mult, ["J128", "F0"], ["NI"], 128)
+    ts(T.IQ[0:64, :], T.J128[0:64, 0:48], PF(0, 0, 64), None, ALU.is_equal, None, ["J128", "F0"], ["IQ"])
+    ms(T.ZR[:], 0.0, ["ZR"])
+    ms(T.IQ[64:65, :], 1.0, ["IQc"])
+    ms(T.N1[0:64, :], 0.0, ["N10", "N11"]); ms(T.N1[64:128, :], 8.0, ["N1c"])
+    for c in range(NC):
+        ms(T["E%d" % c][0:64, :], 0.0, ["E%d_%d_%d" % (c, t, m) for t in range(RO + 1) for m in range(2)])
+        ms(T["E%d" % c][64:65, :], 1.0, ["Ec%d" % c])
+    ms(T.VN[:, 1536:3072], 0.0, ["Vj"], 1536)
+    ts(T.SU2[0:32, :], T.SU[0:32, :], 7, None, ALU.arith_shift_right, None, ["SUa"], ["S2a"], 96)
+    ts(T.SU2[32:64, :], T.SU[32:64, :], 127, None, ALU.bitwise_and, None, ["SUb"], ["S2b"], 96)
+    cp(T.KS[0:64, :], T.SU2[0:64, :], ["S2a", "S2b"], ["KS"], 96)
+    ms(T.KS[64:65, :], 1.0, ["KSc"])
+    ts(T.CA[:], T.IV[:], 0.0, 17.0, ALU.is_lt, ALU.mult, ["IV"], ["CA"], 96)
+    ts(T.CB[:], T.IV[:], -8.0, None, ALU.add, None, ["IV"], ["CB"], 96)
+    tt(T.CN[:], T.CA[:], T.CB[:], ALU.add, ["CA", "CB"], ["CN"], 96)
+    ts(T.CAP[:], T.CA[:], -6.0, 101.0, ALU.mult, ALU.add, ["CA"], ["CAP"], 96)
+    ts(T.I3[:], T.I1[:], PF(5), None, ALU.add, None, ["I1"] + F5, ["I3"], 76)
+    ts(T.I1[:], T.I3[:], 15, None, ALU.bitwise_and, None, ["I3"], ["I1"], 76)
+    tt(T.I3[:], T.I1[:], T.I2[:], ALU.add, ["I1", "I2"], ["I3"], 76)
+    ts(T.IU[:], T.I3[:], PF(8), 767.0, ALU.add, ALU.min, ["I3", "F8"], ["IU"], 76)
+    ts(T.BS2[:], T.BS[:], PF(8), None, ALU.add, None, ["BS", "F8"], ["BS2"])
+    ts(T.RP[0:32, :], T.JJ[0:32, :], PF(1, 0, 32), None, ALU.is_equal, None, ["JJ", "F1"], ["RP"], 128)
+    for k, bk in enumerate(("pH0", "pG0", "pH1", "pT1")):
+        mm(T[bk][:, 0:384], T.RP[0:32, :], T.VO[0:32, 384 * k:384 * k + 384], True, True, ["RP", "VO"], [bk], 128, 384)
+        act(T.VR[:, 384 * k:384 * k + 384], T[bk][:, 0:384], [bk], ["VR%d" % k], 384)
+    act(T.X0[:], T.VR[:, 0:768].indirect(T.IU[:]), ["VR0", "VR1", "IU"], ["X0"], dur=ga(1216))
+    cp(T.X1[:], T.VR[:, 768:1536].indirect(T.IU[:]), ["VR2", "VR3", "IU"], ["X1"], dur=ga(1216))
+    for eh in range(2):
+        for r in range(N):
+            for m in range(2):
+                o = 128 * eh + 32 * r + 16 * m
+                mm(T.pG1[0:96, o:o + 16], T.SM[:, 128 * m:128 * m + 96], T.WA[:, 32 * r + 16 * eh:32 * r + 16 * eh + 16],
+                   True, True, ["SM%d" % m, "WA%d" % r], ["pG1"], 96, 16)
+    ts(T.WK[0:96, :], T.pG1[0:96, 0:256], PF(6, 0, 96), None, ALU.mult, None, ["pG1"] + F6, ["WK"], 256)
+
+    def B(n, c):
+        return T["%s%d" % (n, c)]
+
+    def after_decision(c, t):
+        s = str(c)
+        cur[0] = c
+        E, X, pT, pH, pG = B("E", c), B("X", c), B("pT", c), B("pH", c), B("pG", c)
+        for qh in range(3):
+            for m in range(2):
+                k, K = 2 * qh + m, (65 if m == 0 else 48)
+                mm(pT[:, qh:qh + 1], T.AT[0:K, 128 * k:128 * k + 128], E[0:K, 2 * t + m:2 * t + m + 1], m == 0, m == 1,
+                   ["A%d" % k, "Ac%d" % qh, "Ec" + s, "E%d_%d_%d" % (c, t, m)], ["pT" + s], 128, 1)
+        if t > 0:
+            o = 6 * (t - 1) + 3 * c
+            ts(T.OG[:, o:o + 3], pT[:, 0:3], PF(2), None, ALU.add, None, ["pT" + s, "F1"], ["OG%d_%d" % (t, c)])
+        if t == RO:
+            return
+        if t < RO - 1:
+            ts(B("OS", c)[:, 0:3], pT[:, 0:3], PF(7), None, ALU.add, None, ["pT" + s, "F7"], ["OS" + s])
+        ts(B("F", c)[0:Q, :], E[0:Q, 2 * t:2 * t + 2], -7.5, 16.0, ALU.add, ALU.mult,
+           ["E%d_%d_%d" % (c, t, m) for m in range(2)], ["F" + s + "_"])
+        Xr = ["X" + s, "Xa" + s, "Xb" + s]
+        if t == 0:
+            off, lo, rd = B("OS", c)[:, 0:3], 0, ["OS" + s]
+        elif c == 0:
+            off, lo, rd = T.OG[:, o:o + 3], 0, ["OG%d_0" % t]
+        else:
+            off, lo, rd = T.OG[:, o - 1:o + 3], 16, ["OG%d_0" % t, "OG%d_1" % t]
+        cp(B("G3", c)[:, 0:lo + Q], X[:].indirect(off), Xr + rd, ["G3" + s], dur=ga(lo + Q))
+        g3 = B("G3", c)[0:96, lo:lo + Q]
+        for eh in range(2):
+            mm(pH[:, Q * eh:Q * eh + Q], T.WK[0:96, 128 * eh:128 * eh + 128], g3, True, True, ["WK", "G3" + s], ["pH" + s], 128, Q)
+        act(B("RR", c)[:], pH[:, 0:2 * Q], ["pH" + s], ["RR" + s], 2 * Q, bias=CH)
+        mm(pG[:, 0:2 * Q], T.NI[:], T.ZR[:], True, False, ["NI", "ZR"], ["pG" + s], 128, 2 * Q)
+        for eh in range(2):
+            mm(pG[:, Q * eh:Q * eh + Q], T.WK[0:96, 128 * eh:128 * eh + 128], g3, False, False, ["WK", "G3" + s], ["pG" + s], 128, Q)
+        mm(pG[:, 0:2 * Q], T.NI[:], B("RR", c)[:], False, True, ["NI", "RR" + s], ["pG" + s], 128, 2 * Q)
+        ts(B("O", c)[:], pG[:, 0:2 * Q], CO, 4095.0, ALU.add, ALU.min, ["pG" + s], ["O" + s], 2 * Q)
+        if 0 < t < RO - 1:
+            mm(pH[:, 128:128 + Q], T.SG[0:96, :], g3, True, True, ["SG", "G3" + s], ["pH" + s], 128, Q)
+            act(B("NV", c)[:], pH[:, 128:128 + Q], ["pH" + s], ["NV" + s], Q)
+            cp(X[:].indirect(B("OS", c)[:, 0:3]), B("NV", c)[:], ["NV" + s, "OS" + s], Xr, dur=sc(Q))
+            gcp(X[0:32, 1024:1024 + Q], X[0:32, 0:Q], ["X" + s], ["Xa" + s])
+            gcp(X[32:64, 64:64 + Q], X[32:64, 1088:1088 + Q], ["X" + s], ["Xb" + s])
+
+    def step(c, t):
+        s = str(c)
+        cur[0] = c
+        E, G, pK, MX, DL = B("E", c), B("G", c), B("pK", c), B("MX", c), B("DL", c)
+        n1 = T.N1[0:Q, 32 * c:32 * c + 32]
+        pieces = PIECES_END if (t == 1 and c == 0) or (t == RO and c == NC - 1) else PIECES if t < T2 else PIECES2
+        prevp = {}
+        for q, a, b in pieces:
+            (cp if q == "dve" else act)(G[:, 16 * a:16 * b], T.TB[:].indirect(B("O", c)[:, a:b]), TBall + ["O" + s],
+                                        ["G%s_%d" % (s, x) for x in range(a, b, 2)], dur=ga(16 * (b - a)))
+            if q in prevp:
+                ops[-1]["order"].add(prevp[q])
+            prevp[q] = len(ops) - 1
+
+        def codes(bk, upto, st, sp):
+            mm(T[bk][0:Q, 0:32], T.IQ[0:Q, :], n1, st, False, ["IQ", "N1" + s], [bk], Q, 32)
+            for u in range(1, upto + 1):
+                mm(T[bk][0:Q, 0:32], T.IQ[0:Q, :], DL[0:Q, 32 * u - 32:32 * u], False, sp and u == upto,
+                   ["IQ", "DL%s_%d0" % (s, u), "DL%s_%d1" % (s, u)], [bk], Q, 32)
+        mm(pK[0:Q, 0:32], T.KS[0:65, Q * c:Q * c + Q], T.RS[0:65, :], True, False, ["KS", "KSc", "RS", "RSc0", "RSc1"], ["pK" + s], Q, 32)
+        codes("pK" + s, t - 1, False, False)
+        for eh in range(2):
+            for el in range(16):
+                mm(pK[0:Q, 0:32], G[:, 16 * Q * eh + el:16 * Q * (eh + 1):16], T.SR[:], False, eh == 1 and el == 15,
+                   ["SR"] + ["G%s_%d" % (s, x) for x in range(Q * eh, Q * eh + Q, 2)], ["pK" + s], Q, 32)
+        for m in range(2):
+            add("dve", lambda m=m: V_.tensor_reduce(MX[0:Q, m:m + 1], pK[0:Q, 16 * m:16 * m + 16], AX.X, ALU.max),
+                ["pK" + s], ["MX%s_%d" % (s, m)], vcost(16))
+        mx = ["MX%s_%d" % (s, m) for m in range(2)]
+        ts(B("RQ", c)[0:Q, :], MX[0:Q, :], CR, CR, ALU.add, ALU.subtract, mx, ["RQ" + s])
+        for m in range(2):
+            ts(E[0:Q, 2 * t + m:2 * t + m + 1], MX[0:Q, m:m + 1], B("RQ", c)[0:Q, m:m + 1], B("F", c)[0:Q, m:m + 1],
+               ALU.subtract, ALU.max, [mx[m], "RQ" + s, "F" + s + "_"], ["E%d_%d_%d" % (c, t, m)])
+        tt(B("D", c)[0:Q, :], E[0:Q, 2 * t - 2:2 * t], E[0:Q, 2 * t:2 * t + 2], ALU.subtract,
+           ["E%d_%d_%d" % (c, u, m) for u in (t - 1, t) for m in range(2)], ["D" + s])
+        for m in range(2):
+            ts(DL[0:Q, 32 * t - 32 + 16 * m:32 * t - 16 + 16 * m], pK[0:Q, 16 * m:16 * m + 16], MX[0:Q, m:m + 1],
+               B("D", c)[0:Q, m:m + 1], ALU.is_equal, ALU.mult, ["pK" + s, mx[m], "D" + s], ["DL%s_%d%d" % (s, t, m)])
+        after_decision(c, t)
+        if t == RO:
+            codes("pG" + s, RO, True, True)
+            act(n1, B("pG", c)[0:Q, 0:32], ["pG" + s], ["N1" + s])
+
+    for c in range(NC):
+        s = str(c)
+        pK = B("pK", c)
+        mm(pK[0:Q, 0:34], T.CN[:, Q * c:Q * c + Q], T.SO[:], True, True, ["CN", "SO", "SO0", "SO1"], ["pK" + s], Q, 34)
+        cp(T.N1[0:Q, 32 * c:32 * c + 32], pK[0:Q, 0:32], ["pK" + s], ["N1" + s])
+        cp(B("E", c)[0:Q, 0:2], pK[0:Q, 32:34], ["pK" + s], ["E%d_0_0" % c, "E%d_0_1" % c])
+        after_decision(c, 0)
+
+    def og(t0, n):
+        return ["OG%d_%d" % (u, c) for u in range(t0, t0 + n) for c in range(NC)]
+
+    def replay(nm, t0, n):
+        w = 6 * n
+        cur[0] = None
+        R, DU, V = T["R" + nm], T["DU" + nm], T.VN[:]
+        DF, DB, DX, DY, DZ = T.DF, T.DB, T.DX, T.DY, T.DZ
+        DO = DX[:, 2 * w:3 * w]
+        for r in range(N):
+            a, b = 32 * r, 32 * r + 32
+            if r == rho:
+                cp(DX[a:b, 2 * w:3 * w], T.OG[a:b, 6 * t0 - 6:6 * t0 - 6 + w], og(t0, n), ["DO%d" % r])
+            else:
+                cp(DX[a:b, 2 * w:3 * w], R[a:b, w * r:w * r + w], ["R%s%d" % (nm, r)], ["DO%d" % r])
+        do = ["DO%d" % r for r in range(N)]
+        for k, v in enumerate((960.0, 896.0)):
+            ts(DX[:, k * w:k * w + w], DO, v, None, ALU.add, None, do, ["DX%d" % k])
+        ts(DF[:, 0:w], DO, 1088.0, 1536.0, ALU.is_ge, ALU.mult, do, ["DF"])
+        tt(DB[:, 0:w], DF[:, 0:w], T.BS2[:, 0:w], ALU.add, ["DF", "BS2"], ["DB"])
+        ts(DY[:, 0:3 * w], DX[:, 0:3 * w], 6, 15, ALU.arith_shift_right, ALU.bitwise_and, ["DX0", "DX1"] + do, ["DY"], 3 * w)
+        tt(DZ[:, 0:w], DY[:, 0:w], DB[:, 0:w], ALU.add, ["DY", "DB"], ["DZ0"])
+        tt(DZ[:, w:3 * w], DY[:, w:3 * w], T.BS2[:, 0:2 * w], ALU.add, ["DY", "BS2"], ["DZ1"], w)
+        cp(DU[:, 0:3 * w], DZ[:, 0:3 * w], ["DZ0", "DZ1"], ["DU" + nm], 3 * w)
+        for u in range(n):
+            o = [DU[:, k * w + 6 * u:k * w + 6 * u + 6] for k in range(3)]
+            rd = ["V", "Vj", "DU" + nm]
+            (act if t0 < RO else cp)(T.RA[:], V.indirect(o[0]), rd, ["RA"], dur=ga(96))
+            act(T.RC[:], V.indirect(o[2]), rd, ["RC"], dur=ga(96))
+            tt(T.RB[:], V.indirect(o[1]), T.RA[:], ALU.subtract, rd + ["RA"], ["RB"], dur=ga(96))
+            tt(V.indirect(o[0]), T.RB[:], T.RC[:], ALU.add, ["RB", "RC", "DU" + nm], ["V", "Vj"], dur=sc(96))
+
+    for t in range(1, RO + 1):
+        for c in range(NC):
+            step(c, t)
+        for k, (t0, n) in enumerate(BATCH):
+            if t == t0 + n - 1:
+                send("o%d" % k, lambda r, t0=t0, n=n: T.OG[:, 6 * t0 - 6:6 * (t0 + n) - 6],
+                     T["R%d" % k][:, 6 * n * rho:6 * n * rho + 6 * n], og(t0, n), lambda r, k=k: "R%d%d" % (k, r),
+                     5000.0 if t < RO else 3000.0)
+    send("n", lambda r: T.N1[:], T.RN[:, 64 * rho:64 * rho + 64], ["N10", "N11", "N1c"], lambda r: "RN%d" % r, 3000.0)
+    for k, (t0, n) in enumerate(BATCH):
+        replay(str(k), t0, n)
+    dma("sync", T.yv[:], T.VN[:, 0:1536], ["V"], [], 393216)
+    for r in range(N):
+        for c in range(NC):
+            src = T.N1[0:65, 32 * c:32 * c + 32] if r == rho else T.RN[0:65, 64 * r + 32 * c:64 * r + 32 * c + 32]
+            mm(T.pH0[32 * r:32 * r + 32, Q * c:Q * c + Q], src, T.IQ[0:65, :], True, True,
+               ["IQ", "IQc"] + (["N10", "N11", "N1c"] if r == rho else ["RN%d" % r]), ["pH0"], 32, Q)
+    tt(T.YI[:], T.pH0[:, 0:96], T.CAP[:], ALU.min, ["pH0", "CAP"], ["YI"], 96)
+    dma("act", T.yi[:], T.YI[:], ["YI"], [], 49152)
+    return ops
+
+
+def schedule(ops):
+    n = len(ops)
+    succ = [[] for _ in range(n)]
+    for i, o in enumerate(ops):
+        for j in o["deps"] | o["order"]:
+            succ[j].append(i)
+    prio = [0.0] * n
+    for i in range(n - 1, -1, -1):
+        o = ops[i]
+        best = 0.0
+        for j in succ[i]:
+            best = max(best, prio[j] + (o["lat"] + HOP if i in ops[j]["deps"] else 0.0))
+        prio[i] = max(best, o["lat"]) + o["dur"]
+    x = SEED
+    for i, o in enumerate(ops):
+        x = (x * 1103515245 + 12345) % 2147483648
+        prio[i] += (BIAS if o["ch"] == 0 else 0.0) + JIT * x / 2147483648.0
+    left = [len(o["deps"] | o["order"]) for o in ops]
+    ready_at = [0.0] * n
+    pool = [i for i in range(n) if left[i] == 0]
+    free, order, end = {}, [], [0.0] * n
+    while pool:
+        start = {i: max(ready_at[i], free.get(ops[i]["q"], 0.0)) for i in pool}
+        first = min(pool, key=lambda i: (start[i], -prio[i]))
+        cand = [i for i in pool if ops[i]["q"] == ops[first]["q"] and start[i] <= start[first] + WIN]
+        i = max(cand, key=lambda k: (prio[k], -k))
+        pool.remove(i)
+        o = ops[i]
+        free[o["q"]] = start[i] + o["dur"]
+        end[i] = start[i] + o["dur"] + o["lat"]
+        o["t"] = start[i]
+        order.append(i)
+        for j in succ[i]:
+            ready_at[j] = max(ready_at[j], end[i] + HOP if i in ops[j]["deps"] else start[i] + o["dur"])
+            left[j] -= 1
+            if left[j] == 0:
+                pool.append(j)
+    return order, max(end)
+
+
+def emit(g, T, ops, order):
+    queue = {"pe": g.tensor, "dve": g.vector, "act": g.scalar, "g": g, "sync": g.sync}
+    pos = {i: k for k, i in enumerate(order)}
+    needed = set()
+    for o in ops:
+        last = {}
+        for j in o["deps"]:
+            key = ops[j]["q"] if ops[j]["kind"] == "c" else j
+            if key not in last or pos[j] > pos[last[key]]:
+                last[key] = j
+        o["deps"] = set(last.values())
+        needed |= o["deps"]
+    known = {q: {} for q in queue}
+    count, total, done = {}, {}, {}
+    for i in order:
+        o = ops[i]
+        q = o["q"]
+        if o["kind"] == "rx":
+            done[i] = (o["sem"], o["cnt"], {})
+            total[o["sem"]] = o["cnt"]
+            continue
+        kn = known[q]
+        for j in sorted(o["deps"], key=lambda j: -pos[j]):
+            s, v, clock = done[j]
+            if kn.get(s, 0) < v:
+                queue[q].wait_ge(T.sem[s], v)
+                kn[s] = v
+            for s2, v2 in clock.items():
+                if kn.get(s2, 0) < v2:
+                    kn[s2] = v2
+        ins = o["fn"]()
+        if o["kind"] == "send":
+            total["ls"] = total.get("ls", 0) + o["cnt"]
+        elif o["kind"] == "dma":
+            ins.then_inc(T.sem[o["sem"]], 16)
+            done[i] = (o["sem"], 16, dict(kn))
+            total[o["sem"]] = 16
+        elif i in needed:
+            s = "q_" + q
+            count[s] = count.get(s, 0) + 1
+            ins.then_inc(T.sem[s], 1)
+            done[i] = (s, count[s], dict(kn))
+            total[s] = count[s]
+    for s, v in total.items():
+        if max(k.get(s, 0) for k in known.values()) < v:
+            g.wait_ge(T.sem[s], v)
+
+
+def rank_program(g, core, T, topo):
+    if T.rank_of(core) is None:
+        return
+    ops = build(g, core, T, topo)
+    order, _ = schedule(ops)
+    emit(g, T, ops, order)

@@ -1,41 +1,50 @@
 from concourse.bass import DstId, RemoteDMATransfer
 from concourse.mybir import AluOpType as ALU, AxisListType as AX, ActivationFunctionType as AF
 
-N, Q, NC, RO = 4, 48, 2, 6
+N, Q, NC, RO = 4, 32, 3, 6
+QH = Q // 16
 ROWS = 19
 CR = 402653184.0
-CH = 526336.5
-CO = 528384.0
-PIECES = [("dve", 0, 24), ("act", 24, 48), ("dve", 48, 56), ("dve", 56, 64), ("act", 64, 96)]
-PIECES2 = [("dve", 0, 24), ("act", 24, 48), ("dve", 48, 54), ("dve", 54, 60), ("act", 60, 96)]
-PIECES_END = [("dve", 0, 24), ("act", 24, 48), ("dve", 48, 72), ("act", 72, 96)]
-T2 = 6
-BATCH = [(1, 3), (4, 2), (6, 1)]
-HOP, BIAS, WIN, JIT, SEED = 130.0, 1500.0, 60.0, 0.0, 1
-GAM, SIG, CYC, PEC = 1.7, 3.8, 1.0, 0.6
-
-SCRATCH = {
-    "stg": ("dram", [8, 128, 512], "bfloat16"), "lnd": ("dram", [8, 128, 512], "bfloat16"),
+LOW = -67108864.0
+VW, VS = 16 * Q, 32 * Q + 16
+CUT = [0, 768, 1024]
+PIECES = [("A1", 0, 24), ("g1", 24, 32), ("g2", 32, 40), ("A2", 40, 64)]
+PIECES_END = [("A1", 0, 16), ("g1", 16, 32), ("g2", 32, 48), ("A2", 48, 64)]
+ROUND = {
+    "dve": [("OG", -2), ("g1", 0), ("G3", -2), ("SC", -1), ("g2", 0), ("E", -1), ("O", -2), ("X", -3), ("DL", -2)],
+    "act": [("A1", 0), ("NV", -3), ("A2", 0)],
+    "pe": [("k3", -1), ("k4", -1), ("SG", -3), ("D", -2), ("H", -2), ("z", -2), ("k0", 0), ("pH", -2), ("k1", 0), ("pT", -1),
+           ("k2", 0)],
 }
-for _d, _l in (("bfloat16", "TB 4096 VN 3072 VR 1536 VO 1536 RP 128 WS 32 WA 128 WK 256 KS 96 RS 32 CN 96 AT 768 SM 256 SG 128 "
-                            "SR 32 NI 128 IQ 48 SO 34 N1 64 RN 256 ZR 96 RA 96 RB 96 RC 96"),
-               ("int32", "IV 96 SU 96 SU2 96 PI 1 PJ 4 I1 76 I2 76 I3 76 BS 60 BS2 60 DF 30 DB 30 DX 90 DY 90 DZ 90"),
-               ("float32", "CA 96 CB 96 CAP 96 YI 96 PF 16 J128 128 JJ 128 JX 128 PA 6"),
-               ("uint16", "IU 76 OG 36 R0 120 R1 120 R2 120 R3 120 DU0 90 DU1 90 DU2 90 DU3 90")):
+BATCH = [(1, 2), (3, 2), (5, 1)]
+NB = len(BATCH)
+LB = [4000.0, 4000.0, 3500.0, 3500.0, 3500.0]
+HOP, WIN, YF, BIAS = 210.0, 60.0, 8, 0.0
+GAM, SIG, CYC, PEC = 1.35, 3.3, 0.86, 0.47
+LAT, RATE = 1200.0, 250.0
+LW, LF, LN = 5000.0, [8000.0, 9000.0], 5000.0
+ACTC = [1, 1, 1]
+
+SCRATCH = {}
+for _d, _l in (("bfloat16", "TB 4096 SB 3072 LD 4096 VN 3120 VO 1536 VR 1536 G 3072 RP 128 RN 36 WS 32 WA 128 WK 512 KS 96 CN 96 "
+                            "AT 256 SM 192 SG 128 SR 36 ID 128 NI 128 IS 128 FQ 96 SO 2 ON 1024 CK 64 CW 216 "
+                            "RA0 96 RA1 96 RB 96 RC 96 M0 18 M1 18 M2 18 M3 40 M4 40 R0 72 R1 72 R2 72 R3 160 R4 160"),
+               ("int32", "IV 96 SU 96 SU2 96 PI 1 PJ 6 I1 38 I2 38 I3 38 J128 128 JK 36 JJ 128"),
+               ("float32", "CA 96 CB 96 CAP 96 YI 96 PF 26 JX 128 RZ 36"),
+               ("uint16", "IU 38 DU0 54 DU1 54 DU2 54 DU3 54 DU4 54")):
     _l = _l.split()
     for _k in range(0, len(_l), 2):
         SCRATCH[_l[_k]] = ("sbuf", [128, int(_l[_k + 1])], _d)
 for _c in range(NC):
-    for _n, _s, _d in (("X", ROWS * 64, "bfloat16"), ("G", 1536, "bfloat16"), ("O", 96, "uint16"), ("OS", 4, "uint16"),
-                       ("G3", 64, "bfloat16"), ("RR", 96, "bfloat16"), ("NV", 48, "bfloat16"), ("E", 14, "bfloat16"),
-                       ("MX", 2, "float32"), ("RQ", 2, "float32"), ("F", 2, "float32"), ("D", 2, "float32"),
-                       ("DL", 192, "bfloat16")):
+    for _n, _s, _d in (("X", ROWS * Q, "bfloat16"), ("O", 2 * Q, "uint16"), ("OG", 2 * QH, "uint16"),
+                       ("G3", Q, "bfloat16"), ("NV", Q, "bfloat16"), ("E", 8, "bfloat16"),
+                       ("SC", 36, "float32"), ("DL", 36 * RO, "bfloat16"), ("NR", 36, "bfloat16")):
         SCRATCH["%s%d" % (_n, _c)] = ("sbuf", [128, _s], _d)
-    for _n in ("pK", "pT", "pH", "pG"):
-        SCRATCH["%s%d" % (_n, _c)] = ("psum", [128, 512], "float32")
+for _n in ("pK0", "pK1", "pK2", "pH0", "pH1", "pH2", "pT", "pY"):
+    SCRATCH[_n] = ("psum", [128, 512], "float32")
 
 SEMAPHORES = (["q_pe", "q_dve", "q_act", "q_g", "ls"] + ["d%d" % k for k in range(32)]
-              + ["a%s%d" % (n, r) for n in ("w", "t0", "t1", "t2", "t3", "o0", "o1", "o2", "o3", "n") for r in range(N)])
+              + ["a%s%d" % (n, r) for n in ("w", "t0", "t1", "t2", "tn", "o0", "o1", "o2", "o3", "o4") for r in range(N)])
 
 
 def _engine_sets(topo, cores, src):
@@ -60,10 +69,11 @@ def build(g, core, T, topo):
     cores = list(T.cores)
     far, near, eng = _engine_sets(topo, cores, core)
     rk = {c: T.rank_of(c) for c in cores}
+    rfar, rnear = [rk[c] for c in far], rk[near[0]]
     ops = []
     last_w, readers, bank = {}, {}, {}
     prev_fixed = {}
-    ndma = [0]
+    ndma, load = [0], [0.0]
     cur = [None]
 
     def add(q, fn, r, w, dur, lat=0.0, kind="c", sem=None, cnt=0, fixed=False):
@@ -108,13 +118,13 @@ def build(g, core, T, topo):
     V_, S_, P_ = g.vector, g.scalar, g.tensor
 
     def vcost(n, f=1.0):
-        return 15.0 + max(64.0, n * f) * CYC
+        return max(64.0, n * f) * CYC
 
     def ga(n):
-        return 60.0 + GAM * n
+        return 55.0 + GAM * n
 
     def sc(n):
-        return 60.0 + SIG * n
+        return 55.0 + SIG * n
 
     def ts(out, in0, s1, s2, o0, o1, r, w, n=1):
         if o1 is None:
@@ -123,7 +133,7 @@ def build(g, core, T, topo):
             add("dve", lambda: V_.tensor_scalar(out, in0, s1, s2, o0, o1), r, w, vcost(n))
 
     def tt(out, a, b, op, r, w, n=1, dur=None):
-        add("dve", lambda: V_.tensor_tensor(out, a, b, op), r, w, dur or vcost(n, 2.0))
+        add("dve", lambda: V_.tensor_tensor(out, a, b, op), r, w, dur or vcost(n))
 
     def cp(out, a, r, w, n=1, dur=None):
         add("dve", lambda: V_.tensor_copy(out, a), r, w, dur or vcost(n))
@@ -131,308 +141,393 @@ def build(g, core, T, topo):
     def ms(ap, val, w, n=1):
         add("dve", lambda: V_.memset(ap, val), [], w, vcost(n, 0.5))
 
-    def act(out, a, r, w, n=1, dur=None, bias=None):
-        if bias is None:
-            add("act", lambda: S_.activation(out, a, AF.Identity), r, w, dur or vcost(n))
-        else:
-            add("act", lambda: S_.activation(out, a, AF.Identity, bias=bias), r, w, dur or vcost(n))
+    def act(out, a, r, w, n=1, dur=None, bias=0.0, scale=1.0):
+        add("act", lambda: S_.activation(out, a, AF.Identity, bias=bias, scale=scale), r, w, dur or vcost(n))
 
     def mm(out, l, rr, st, sp, r, w, m, n):
-        add("pe", lambda: P_.matmul(out, l, rr, st, sp), r, w, 5.0 + max(min(64, m), n) * PEC)
+        add("pe", lambda: P_.matmul(out, l, rr, st, sp), r, w, max(min(64, m), n) * PEC)
 
-    def dma(q, out, a, r, w, nbytes):
+    def dma(q, out, a, r, w, nbytes, first=False):
         e = {"sync": g.sync, "act": g.scalar}[q]
-        add(q, lambda: e.dma_start(out, a), r, w, 100.0, lat=1800.0 + nbytes / 200.0, kind="dma", fixed=True)
+        load[0] = (load[0] if first else 0.0) + nbytes / RATE
+        add(q, lambda: e.dma_start(out, a), r, w, 60.0, lat=LAT + load[0], kind="dma", fixed=True)
 
     def iota(out, pat, base, cm, w, n, flt):
         if flt:
-            add("g", lambda: g.iota(out, pat, base, cm, allow_small_or_imprecise_dtypes=True), [], w, 150.0 + 2 * n, fixed=True)
+            add("g", lambda: g.iota(out, pat, base, cm, allow_small_or_imprecise_dtypes=True), [], w, 130.0 + 2 * n * CYC, fixed=True)
         else:
-            add("g", lambda: g.iota(out, pat, base, cm), [], w, 150.0 + 2 * n, fixed=True)
+            add("g", lambda: g.iota(out, pat, base, cm), [], w, 130.0 + 2 * n * CYC, fixed=True)
 
     def gcp(out, a, r, w):
-        add("g", lambda: g.affine_select(out, a, [[0, Q]], ALU.is_ge, 0.0, 0, 0), r, w, 200.0 + 2 * Q * CYC)
+        add("g", lambda: g.affine_select(out, a, [[0, Q]], ALU.is_ge, 0.0, 0, 0), r, w, 170.0 + 2 * Q * CYC)
 
-    def send(name, src, dst, r, w_in, lat):
+    def send(name, peers, src, dst, r, w_in, lat):
         def fn():
             trs = []
-            for c in far + near:
+            for c in peers:
                 rid, pid = topo.addr(c, core)
                 trs.append(RemoteDMATransfer(dst_ids=[DstId(rid=rid, pnc=pid)], dma_engine_mask=sum(1 << e for e in eng[c]),
                                              remote_sem=T.sem["a%s%d" % (name, rho)], src=src(rk[c]), dst=dst))
             return g.remote_dma_fused(trs, local_sem=T.sem["ls"])
-        i = add("g", fn, r, [], 700.0, kind="send", cnt=sum(len(e) for e in eng.values()), fixed=True)
-        for c in near + far:
+        i = add("g", fn, r, [], 800.0, kind="send", cnt=sum(len(eng[c]) for c in peers), fixed=True)
+        for c in sorted(peers, key=lambda c: c in far):
             k = len(_engine_sets(topo, cores, c)[2][core])
-            j = add("rx", None, [], [w_in(rk[c])], 0.0, lat=lat * (0.6 if c in near else 1.0), kind="rx",
+            j = add("rx", None, [], [w_in(rk[c])], 0.0, lat=lat * (0.8 if c in near else 1.0), kind="rx",
                     sem="a%s%d" % (name, rk[c]), cnt=k)
             ops[j]["order"].add(i)
 
-    o32 = 32 * rho
-    dma("act", T.WS[:], T.wt[:], [], ["WS"], 8192)
-    order_ = [rk[c] for c in far + near]
-    for m in range(2):
-        for k, r in enumerate(order_):
-            gq = 2 * r + m
-            dma("act" if k == 1 else "sync", T.stg[gq], T.dem[16 * gq:16 * gq + 16, :], [], ["stg%d" % gq], 131072 * 3)
-    dma("act", T.IV[:], T.inv[:], [], ["IV"], 49152)
-    dma("act", T.VO[0:32, :], T.v[o32:o32 + 32, :], [], ["VO"], 400000)
-    dma("act", T.SU[0:32, :], T.sup[o32:o32 + 32, :], [], ["SUa"], 12288)
-    dma("act", T.SU[32:64, :], T.sup[o32:o32 + 32, :], [], ["SUb"], 12288)
-    dma("act", T.WA[:, o32:o32 + 32], T.wt[:], [], ["WA%d" % rho], 8192)
+    def blk(r, n=32):
+        return slice(n * r, n * r + n)
+
+    NP = len(CUT) - 1
+    peers = rfar + [rnear]
+    TBall = ["TB%d_%d_%d" % (r, k, j) for r in peers for k in range(4) for j in range(NP)] + ["TBo"]
+    SBn = lambda r: ["SB%d_%d" % (r, k) for k in range(4)]
+
+    def stage(r):
+        for k in range(4):
+            dma(("sync", "act")[k % 2], T.SB[blk(k), blk(peers.index(r), 1024)], T.dem[blk(r), blk(k, 1024)], [],
+                [SBn(r)[k]], 65536, True)
+
+    dma("act", T.WS[:], T.wt[:], [], ["WS"], 8192, True)
+    for r in rfar:
+        stage(r)
+    dma("sync", T.VO[0:32, :], T.v[blk(rho), :], [], ["VO"], 98304, True)
+    dma("act", T.IV[:], T.inv[:], [], ["IV"], 49152, True)
+    stage(rnear)
+    dma("act", T.SU[0:32, :], T.sup[blk(rho), :], [], ["SUa"], 12288, True)
+    dma("act", T.SU[32:64, :], T.sup[blk(rho), :], [], ["SUb"], 12288, True)
+    dma("sync", T.TB[blk(rho), :], T.dem[blk(rho), :], SBn(rnear), ["TBo"], 262144 * 5)
     iota(T.PI[:], [[0, 1]], 0, 1, ["PI"], 1, False)
-    iota(T.JJ[:], [[0, 4], [1, 32]], 0, 0, ["JJ"], 128, True)
-    iota(T.I1[:], [[1, ROWS], [0, 4]], 15, 0, ["I1"], 76, False)
-    iota(T.I2[:], [[0, ROWS], [256, 4]], 0, 0, ["I2"], 76, False)
+    iota(T.J128[:], [[1, 128]], 0, 0, ["J128"], 128, False)
+    iota(T.I1[:], [[1, ROWS], [0, QH]], 15, 0, ["I1"], ROWS * QH, False)
+    iota(T.I2[:], [[0, ROWS], [256, QH]], 0, 0, ["I2"], ROWS * QH, False)
+    iota(T.JK[:], [[32, 2], [1, 18]], 0, 0, ["JK"], 36, False)
+    send("w", far + near, lambda r: T.WS[:], T.WA[:, blk(rho)], ["WS"], lambda r: "WA%d" % r, LW)
     iota(T.JX[:], [[0, 4], [1000, 2], [1, 16]], 0, 0, ["JX"], 128, True)
-    iota(T.PA[:], [[-16, 3], [1000, 2]], 0, 1, ["PA"], 6, True)
-    send("w", lambda r: T.WS[:], T.WA[:, o32:o32 + 32], ["WS"], lambda r: "WA%d" % r, 4000.0)
-    for m in range(2):
-        send("t%d" % m, lambda r, m=m: T.stg[2 * r + m], T.lnd[2 * rho + m],
-             ["stg%d" % (2 * r + m) for r in order_], lambda r, m=m: "lnd%d" % (2 * r + m), 5000.0 + 3000.0 * m)
-    iota(T.J128[:], [[1, 128]], 0, 0, ["J128"], 128, True)
-    iota(T.BS[:], [[0, 10], [256, 6]], 0, 0, ["BS"], 60, False)
-    for m in range(2):
-        for c in near + far:
-            gq = 2 * rk[c] + m
-            dma("sync", T.TB[16 * gq:16 * gq + 16, :], T.lnd[gq], ["lnd%d" % gq], ["TB%d" % gq], 131072)
-            if m == 0 and c == near[0]:
-                dma("sync", T.TB[o32:o32 + 32, :], T.dem[o32:o32 + 32, :], [], ["TB%d" % (2 * rho)], 262144)
-    dma("sync", T.VN[:, 0:1536], T.v[:], [], ["V"], 393216)
-    TBall = ["TB%d" % k for k in range(8) if k != 2 * rho + 1]
+    for j in range(NP):
+        a, b = CUT[j], CUT[j + 1]
+        send("t%d" % j, far, lambda r, a=a, b=b: T.SB[:, 1024 * peers.index(r) + a:1024 * peers.index(r) + b],
+             T.LD[:, 1024 * rho + a:1024 * rho + b], SBn(rfar[0]) + SBn(rfar[1]), lambda r, j=j: "LD%d_%d" % (r, j), LF[j])
+    send("tn", near, lambda r: T.SB[:, 2048:3072], T.LD[:, blk(rho, 1024)], SBn(rnear), lambda r: "LDn", LN)
+    u4 = 64 // Q
+    for ty, (st, b) in enumerate(((u4, 38), (-64, -34 * Q), (u4, 30))):
+        iota(T.CW[0:1, blk(ty, 18)], [[0, 18 // QH], [st, QH]], b, 0, ["CW"], 18, True)
+    iota(T.CW[0:1, 54:108], [[4, 3], [0, 18 // QH], [-u4, QH]], -8, 0, ["CW"], 54, True)
+    iota(T.CW[0:1, 108:162], [[0, 9], [VS // 16, NC], [16, QH]], 0, 0, ["CW"], 54, True)
+    iota(T.CW[0:1, 162:216], [[0, 54]], 1, 0, ["CW"], 54, True)
+    iota(T.CW[0:1, 180:198], [[0, 18]], Q, 0, ["CW"], 18, True)
+    for c in range(NC):
+        dma("sync", T.VN[:, VS * c:VS * c + VW], T.v[:, blk(c, VW)], ["LD%d_%d" % (r, NP - 1) for r in rfar], ["V%d" % c], 256 * VW * (c + 1))
+
+    def unfold(r, a, b, src, names, nact):
+        for k in range(4):
+            f, n = (act, b - a) if k < nact else (cp, (b - a) // 2)
+            f(T.TB[blk(r), 1024 * k + a:1024 * k + b], T.LD[blk(k), 1024 * r + a:1024 * r + b], [src], names(k), n)
+
+    unfold(rnear, 0, 1024, "LDn", lambda k: ["TB%d_%d_%d" % (rnear, k, j) for j in range(NP)], ACTC[0])
+    for j in range(NP):
+        for r in rfar:
+            unfold(r, CUT[j], CUT[j + 1], "LD%d_%d" % (r, j), lambda k: ["TB%d_%d_%d" % (r, k, j)], ACTC[1 + j])
 
     PF = lambda k, a=0, b=128: T.PF[a:b, k:k + 1]
     cp(PF(0), T.PI[:], ["PI"], ["F0"])
-    ts(T.PJ[:, 0:1], T.PI[:], 31, None, ALU.bitwise_and, None, ["PI"], ["J0"])
-    ts(T.PJ[:, 1:2], T.PI[:], 15, None, ALU.bitwise_and, None, ["PI"], ["J1"])
-    ts(T.PJ[:, 2:3], T.PI[:], 4, None, ALU.arith_shift_right, None, ["PI"], ["J2"])
-    cp(T.PF[:, 1:4], T.PJ[:, 0:3], ["J0", "J1", "J2"], ["F1"])
-    ts(PF(4), PF(0), float(-o32), None, ALU.add, None, ["F0"], ["F4"])
-    ms(PF(5, 0, 32), 1.0, ["F5a"]); ms(PF(5, 32, 64), -1.0, ["F5b"]); ms(PF(5, 64, 128), 0.0, ["F5c"])
+    for k, (v, op) in enumerate(((31, ALU.bitwise_and), (15, ALU.bitwise_and), (4, ALU.arith_shift_right), (63, ALU.bitwise_and),
+                                 (6, ALU.arith_shift_right), (16, ALU.bitwise_and))):
+        ts(T.PJ[:, k:k + 1], T.PI[:], v, None, op, None, ["PI"], ["J%d" % k])
+    cp(T.PF[:, 1:7], T.PJ[:], ["J%d" % k for k in range(6)], ["F1"])
+    ts(T.JJ[:], T.J128[:], 31, None, ALU.bitwise_and, None, ["J128"], ["JJ"], 128)
+    ts(PF(24), PF(1), PF(6), None, ALU.add, None, ["F1"], ["F24"])
+    ts(PF(7), PF(0), float(-32 * rho), None, ALU.add, None, ["F0"], ["F4"])
+    ms(PF(8, 0, 32), 1.0, ["F5a"]); ms(PF(8, 32, 64), -1.0, ["F5b"]); ms(PF(8, 64, 128), 0.0, ["F5c"])
     F5 = ["F5a", "F5b", "F5c"]
-    ms(PF(6, 0, 64), 1.0, ["F6a"]); ms(PF(6, 64, 128), -1.0, ["F6b"])
+    ms(PF(9, 0, 64), 1.0, ["F6a"]); ms(PF(9, 64, 128), -1.0, ["F6b"])
     F6 = ["F6a", "F6b"]
-    ts(PF(7), PF(5), -64.0, PF(2), ALU.mult, ALU.add, F5 + ["F1"], ["F7"])
-    ts(PF(8), PF(2), 16.0, None, ALU.mult, None, ["F1"], ["F8"])
+    ts(PF(10), PF(0), 113.0, float(Q), ALU.is_equal, ALU.mult, ["F0"], ["F7"])
+    ts(PF(11), PF(2), 16.0, None, ALU.mult, None, ["F1"], ["F8"])
+    ms(PF(14, 0, 32), -65536.0, ["F11a"]); ms(PF(14, 32, 64), -512.0, ["F11b"])
+    ts(PF(15), PF(0), -64.0, None, ALU.add, None, ["F0"], ["F15"])
+    ts(PF(16), PF(0), 112.0, None, ALU.is_equal, None, ["F0"], ["F16"])
+    for nm, v in (("ID", 1.0), ("NI", -1.0), ("IS", float(Q))):
+        ts(T[nm][:], T.J128[:], PF(0), v, ALU.is_equal, ALU.mult, ["J128", "F0"], [nm], 128)
+    for k, v in enumerate((0.25, 16.0, 31.5, 2.0 ** 29, -2.0 ** 29, 0.0, 1.5 * 2.0 ** 27, -1.5 * 2.0 ** 27)):
+        ms(T.ON[0:1, blk(k, 128)], v, ["ONc" if 1 < k < 6 else "ONa"])
+    ms(T.CK[0:1, :], 65.0, ["CK"])
+    ms(T.RZ[:], 0.0, ["RZ"])
+    for a, v in ((slice(16, 36, 18), CR), (slice(17, 36, 18), -CR), (slice(18, 19), 4 * LOW)):
+        ms(T.RZ[:, a], v, ["RZ"])
+    ts(PF(23), PF(5), 1000.0, PF(4), ALU.mult, ALU.add, ["F1"], ["F23"])
+    for qh in range(QH):
+        ts(PF(17 + qh), PF(23), -16.0 * qh, None, ALU.add, None, ["F23"], ["F17%d" % qh])
+        ts(PF(20 + qh), PF(16), 9.0 * Q + 16 * qh, None, ALU.mult, None, ["F16"], ["F20%d" % qh])
+        ts(T.AT[:, blk(qh, 128)], T.JX[:], PF(17 + qh), float(Q), ALU.is_equal, ALU.mult, ["JX", "F17%d" % qh], ["A%d" % qh], 128)
+        ts(T.AT[96:128, blk(qh, 128)], T.AT[96:128, blk(qh, 128)], PF(20 + qh, 96), None, ALU.add, None,
+           ["A%d" % qh, "F20%d" % qh], ["A%d" % qh], 64)
+        for k in range(2):
+            a = slice(128 * qh + 32 * k, 128 * qh + 32 * k + 32)
+            ts(T.AT[96:128, a], T.AT[96:128, a], PF(10, 96), None, (ALU.subtract, ALU.add)[k], None, ["A%d" % qh, "F7"], ["A%d" % qh])
+    ts(T.FQ[:], T.J128[:, 0:96], PF(0), 16.0, ALU.is_equal, ALU.mult, ["J128", "F0"], ["FQ"], 96)
+    ts(PF(22), PF(16), -120.0, None, ALU.mult, None, ["F16"], ["F22"])
+    ts(T.FQ[96:128, :], T.FQ[96:128, :], PF(22, 96), None, ALU.add, None, ["FQ", "F22"], ["FQ"])
     for m in range(2):
-        ts(PF(9 + m), PF(3), float(2 * rho + m), None, ALU.is_equal, None, ["F1"], ["F9%d" % m])
-    ms(PF(11, 0, 32), -65536.0, ["F11a"]); ms(PF(11, 32, 64), -512.0, ["F11b"])
-    for qh in range(3):
-        for m in range(2):
-            k = 2 * qh + m
-            ts(T.AT[0:64, 128 * k:128 * k + 128], T.JX[0:64, :], T.PA[0:64, k:k + 1], 64.0, ALU.is_equal, ALU.mult, ["JX", "PA"], ["A%d" % k], 128)
-        ms(T.AT[64:65, 256 * qh:256 * qh + 128], 576.0 + 16 * qh, ["Ac%d" % qh])
-    for m in range(2):
-        ts(T.SM[:, 128 * m:128 * m + 128], T.JJ[:], PF(4), PF(9 + m), ALU.is_equal, ALU.mult, ["JJ", "F4", "F9%d" % m], ["SM%d" % m], 128)
-        ts(T.SO[:, 32 + m:33 + m], PF(9 + m), -1.0, None, ALU.mult, None, ["F9%d" % m], ["SO%d" % m])
-        ts(T.RS[64:65, 16 * m:16 * m + 16], T.JX[64:65, 0:16], -32.0, 480.0, ALU.mult, ALU.add, ["JX"], ["RSc%d" % m])
-    ts(T.SO[:, 0:32], T.JJ[:, 0:32], PF(4), None, ALU.is_equal, None, ["JJ", "F4"], ["SO"])
-    ts(T.SG[:], T.JJ[:], PF(1), PF(6), ALU.is_equal, ALU.mult, ["JJ", "F1"] + F6, ["SG"], 128)
-    ts(T.SR[:], T.JJ[:, 0:32], PF(1), 512.0, ALU.is_equal, ALU.mult, ["JJ", "F1"], ["SR"])
-    ts(T.RS[0:64, :], T.JJ[0:64, 0:32], PF(1, 0, 64), PF(11, 0, 64), ALU.is_equal, ALU.mult, ["JJ", "F1", "F11a", "F11b"], ["RS"])
-    ts(T.NI[:], T.J128[:], PF(0), -1.0, ALU.is_equal, ALU.mult, ["J128", "F0"], ["NI"], 128)
-    ts(T.IQ[0:64, :], T.J128[0:64, 0:48], PF(0, 0, 64), None, ALU.is_equal, None, ["J128", "F0"], ["IQ"])
-    ms(T.ZR[:], 0.0, ["ZR"])
-    ms(T.IQ[64:65, :], 1.0, ["IQc"])
-    ms(T.N1[0:64, :], 0.0, ["N10", "N11"]); ms(T.N1[64:128, :], 8.0, ["N1c"])
+        ts(PF(12 + m), PF(3), float(2 * rho + m), None, ALU.is_equal, None, ["F1"], ["F9%d" % m])
+        ts(T.SO[:, m:m + 1], PF(12 + m), -1.0, None, ALU.mult, None, ["F9%d" % m], ["SO%d" % m])
+        ts(T.SM[:, blk(m, 96)], T.JJ[:, 0:96], PF(7), PF(12 + m), ALU.is_equal, ALU.mult, ["JJ", "F4", "F9%d" % m], ["SM%d" % m], 96)
+    ts(T.RP[0:32, :], T.JJ[0:32, :], PF(1, 0, 32), None, ALU.is_equal, None, ["JJ", "F1"], ["RP"], 128)
+    ts(PF(25), PF(12), PF(13), None, ALU.add, None, ["F90", "F91"], ["F25"])
+    ts(T.RN[:], T.JK[:], PF(24), PF(25), ALU.is_equal, ALU.mult, ["JK", "F24", "F25"], ["RN"])
+    ts(T.SG[:], T.JJ[:], PF(1), PF(9), ALU.is_equal, ALU.mult, ["JJ", "F1"] + F6, ["SG"], 128)
+    ts(T.SR[:], T.JK[:], PF(24), 512.0, ALU.is_equal, ALU.mult, ["JK", "F24"], ["SR"])
+    for k in (NB, NB + 1):
+        ms(T["M%d" % k][:], 0.0, ["M%d" % k] + ["L%d_%d%d" % (k, c, m) for c in range(NC) for m in range(2)])
     for c in range(NC):
-        ms(T["E%d" % c][0:64, :], 0.0, ["E%d_%d_%d" % (c, t, m) for t in range(RO + 1) for m in range(2)])
-        ms(T["E%d" % c][64:65, :], 1.0, ["Ec%d" % c])
-    ms(T.VN[:, 1536:3072], 0.0, ["Vj"], 1536)
+        s = str(c)
+        E, NR = T["E" + s], T["NR" + s]
+        ms(E[0:64, :], 0.0, ["E%d_%d_0" % (c, t) for t in range(RO + 1)])
+        ms(E[64:128, :], 1.0, ["Ec" + s] + ["E%d_%d_1" % (c, t) for t in range(RO + 1)])
+        ms(T["DL" + s][0:Q, :], 0.0, ["DL%s_%d%d" % (s, t, m) for t in range(1, RO + 1) for m in range(2)], 36 * RO)
+        ts(NR[0:64, :], T.JK[0:64, :], PF(24, 0, 64), PF(14, 0, 64), ALU.is_equal, ALU.mult, ["JK", "F24", "F11a", "F11b"], ["NRa" + s])
+        for m in range(2):
+            ts(NR[96:128, blk(m, 18)], T.JK[96:128, 0:18], -32.0, 472.0, ALU.mult, ALU.add, ["JK"], ["NRb" + s])
+            ms(NR[96:128, 18 * m + 16:18 * m + 18], LOW, ["NRb" + s])
+        ts(T.KS[64:128, blk(c, Q)], T.J128[64:128, 0:Q], PF(15, 64), PF(16, 64), ALU.is_equal, ALU.max, ["J128", "F15", "F16"], ["KSc" + s])
+        ms(T.VN[:, VS * c + VW:VS * c + VS], 0.0, ["Vj" + s], VW)
+    Vall = ["V%d" % c for c in range(NC)] + ["Vj%d" % c for c in range(NC)]
     ts(T.SU2[0:32, :], T.SU[0:32, :], 7, None, ALU.arith_shift_right, None, ["SUa"], ["S2a"], 96)
     ts(T.SU2[32:64, :], T.SU[32:64, :], 127, None, ALU.bitwise_and, None, ["SUb"], ["S2b"], 96)
     cp(T.KS[0:64, :], T.SU2[0:64, :], ["S2a", "S2b"], ["KS"], 96)
-    ms(T.KS[64:65, :], 1.0, ["KSc"])
     ts(T.CA[:], T.IV[:], 0.0, 17.0, ALU.is_lt, ALU.mult, ["IV"], ["CA"], 96)
     ts(T.CB[:], T.IV[:], -8.0, None, ALU.add, None, ["IV"], ["CB"], 96)
-    tt(T.CN[:], T.CA[:], T.CB[:], ALU.add, ["CA", "CB"], ["CN"], 96)
+    tt(T.CN[:], T.CA[:], T.CB[:], ALU.add, ["CA", "CB"], ["CN"], 192)
     ts(T.CAP[:], T.CA[:], -6.0, 101.0, ALU.mult, ALU.add, ["CA"], ["CAP"], 96)
-    ts(T.I3[:], T.I1[:], PF(5), None, ALU.add, None, ["I1"] + F5, ["I3"], 76)
-    ts(T.I1[:], T.I3[:], 15, None, ALU.bitwise_and, None, ["I3"], ["I1"], 76)
-    tt(T.I3[:], T.I1[:], T.I2[:], ALU.add, ["I1", "I2"], ["I3"], 76)
-    ts(T.IU[:], T.I3[:], PF(8), 767.0, ALU.add, ALU.min, ["I3", "F8"], ["IU"], 76)
-    ts(T.BS2[:], T.BS[:], PF(8), None, ALU.add, None, ["BS", "F8"], ["BS2"])
-    ts(T.RP[0:32, :], T.JJ[0:32, :], PF(1, 0, 32), None, ALU.is_equal, None, ["JJ", "F1"], ["RP"], 128)
-    for k, bk in enumerate(("pH0", "pG0", "pH1", "pT1")):
-        mm(T[bk][:, 0:384], T.RP[0:32, :], T.VO[0:32, 384 * k:384 * k + 384], True, True, ["RP", "VO"], [bk], 128, 384)
-        act(T.VR[:, 384 * k:384 * k + 384], T[bk][:, 0:384], [bk], ["VR%d" % k], 384)
-    act(T.X0[:], T.VR[:, 0:768].indirect(T.IU[:]), ["VR0", "VR1", "IU"], ["X0"], dur=ga(1216))
-    cp(T.X1[:], T.VR[:, 768:1536].indirect(T.IU[:]), ["VR2", "VR3", "IU"], ["X1"], dur=ga(1216))
-    for eh in range(2):
-        for r in range(N):
-            for m in range(2):
-                o = 128 * eh + 32 * r + 16 * m
-                mm(T.pG1[0:96, o:o + 16], T.SM[:, 128 * m:128 * m + 96], T.WA[:, 32 * r + 16 * eh:32 * r + 16 * eh + 16],
-                   True, True, ["SM%d" % m, "WA%d" % r], ["pG1"], 96, 16)
-    ts(T.WK[0:96, :], T.pG1[0:96, 0:256], PF(6, 0, 96), None, ALU.mult, None, ["pG1"] + F6, ["WK"], 256)
+    ts(T.I3[:], T.I1[:], PF(8), None, ALU.add, None, ["I1"] + F5, ["I3"])
+    ts(T.I1[:], T.I3[:], 15, None, ALU.bitwise_and, None, ["I3"], ["I1"])
+    tt(T.I3[:], T.I1[:], T.I2[:], ALU.add, ["I1", "I2"], ["I3"])
+    ts(T.IU[:], T.I3[:], PF(11), None, ALU.add, None, ["I3", "F8"], ["IU"])
+    for c in range(NC):
+        s, f = str(c), (act, cp, act)[c]
+        mm(T["pH" + s][:], T.RP[0:32, :], T.VO[0:32, blk(c, VW)], True, True, ["RP", "VO"], ["pH" + s], 128, VW)
+        f(T.VR[:, blk(c, VW)], T["pH" + s][:], ["pH" + s], ["VR" + s], VW)
+        f(T["X" + s][:], T.VR[:, blk(c, VW)].indirect(T.IU[:]), ["VR" + s, "IU"], ["X" + s], dur=ga(ROWS * Q))
+    for r in [rho, rnear] + rfar:
+        src, nm = (T.WS[:], "WS") if r == rho else (T.WA[:, blk(r)], "WA%d" % r)
+        for m in range(2):
+            mm(T.pY[0:96, blk(2 * r + m)], T.SM[:, blk(m, 96)], src, True, True, ["SM%d" % m, nm], ["pY"], 96, 32)
+    act(T.WK[0:96, 0:256], T.pY[0:96, 0:256], ["pY"] + F6, ["WK"], 256, scale=PF(9, 0, 96))
+    ts(T.WK[0:96, 256:512], T.pY[0:96, 0:256], PF(9, 0, 96), -1.0, ALU.mult, ALU.mult, ["pY"] + F6, ["WN"], 256)
+
+    def const(out, k, n, st, sp, bk):
+        mm(out, T.ON[0:1, blk(2 + k, 128)], T.CK[0:1, 0:n], st, sp, ["ONc", "CK"], [bk], 128, n)
 
     def B(n, c):
         return T["%s%d" % (n, c)]
 
-    def after_decision(c, t):
-        s = str(c)
-        cur[0] = c
-        E, X, pT, pH, pG = B("E", c), B("X", c), B("pT", c), B("pH", c), B("pG", c)
-        for qh in range(3):
-            for m in range(2):
-                k, K = 2 * qh + m, (65 if m == 0 else 48)
-                mm(pT[:, qh:qh + 1], T.AT[0:K, 128 * k:128 * k + 128], E[0:K, 2 * t + m:2 * t + m + 1], m == 0, m == 1,
-                   ["A%d" % k, "Ac%d" % qh, "Ec" + s, "E%d_%d_%d" % (c, t, m)], ["pT" + s], 128, 1)
-        if t > 0:
-            o = 6 * (t - 1) + 3 * c
-            ts(T.OG[:, o:o + 3], pT[:, 0:3], PF(2), None, ALU.add, None, ["pT" + s, "F1"], ["OG%d_%d" % (t, c)])
-        if t == RO:
-            return
-        if t < RO - 1:
-            ts(B("OS", c)[:, 0:3], pT[:, 0:3], PF(7), None, ALU.add, None, ["pT" + s, "F7"], ["OS" + s])
-        ts(B("F", c)[0:Q, :], E[0:Q, 2 * t:2 * t + 2], -7.5, 16.0, ALU.add, ALU.mult,
-           ["E%d_%d_%d" % (c, t, m) for m in range(2)], ["F" + s + "_"])
-        Xr = ["X" + s, "Xa" + s, "Xb" + s]
-        if t == 0:
-            off, lo, rd = B("OS", c)[:, 0:3], 0, ["OS" + s]
-        elif c == 0:
-            off, lo, rd = T.OG[:, o:o + 3], 0, ["OG%d_0" % t]
-        else:
-            off, lo, rd = T.OG[:, o - 1:o + 3], 16, ["OG%d_0" % t, "OG%d_1" % t]
-        cp(B("G3", c)[:, 0:lo + Q], X[:].indirect(off), Xr + rd, ["G3" + s], dur=ga(lo + Q))
-        g3 = B("G3", c)[0:96, lo:lo + Q]
-        for eh in range(2):
-            mm(pH[:, Q * eh:Q * eh + Q], T.WK[0:96, 128 * eh:128 * eh + 128], g3, True, True, ["WK", "G3" + s], ["pH" + s], 128, Q)
-        act(B("RR", c)[:], pH[:, 0:2 * Q], ["pH" + s], ["RR" + s], 2 * Q, bias=CH)
-        mm(pG[:, 0:2 * Q], T.NI[:], T.ZR[:], True, False, ["NI", "ZR"], ["pG" + s], 128, 2 * Q)
-        for eh in range(2):
-            mm(pG[:, Q * eh:Q * eh + Q], T.WK[0:96, 128 * eh:128 * eh + 128], g3, False, False, ["WK", "G3" + s], ["pG" + s], 128, Q)
-        mm(pG[:, 0:2 * Q], T.NI[:], B("RR", c)[:], False, True, ["NI", "RR" + s], ["pG" + s], 128, 2 * Q)
-        ts(B("O", c)[:], pG[:, 0:2 * Q], CO, 4095.0, ALU.add, ALU.min, ["pG" + s], ["O" + s], 2 * Q)
-        if 0 < t < RO - 1:
-            mm(pH[:, 128:128 + Q], T.SG[0:96, :], g3, True, True, ["SG", "G3" + s], ["pH" + s], 128, Q)
-            act(B("NV", c)[:], pH[:, 128:128 + Q], ["pH" + s], ["NV" + s], Q)
-            cp(X[:].indirect(B("OS", c)[:, 0:3]), B("NV", c)[:], ["NV" + s, "OS" + s], Xr, dur=sc(Q))
-            gcp(X[0:32, 1024:1024 + Q], X[0:32, 0:Q], ["X" + s], ["Xa" + s])
-            gcp(X[32:64, 64:64 + Q], X[32:64, 1088:1088 + Q], ["X" + s], ["Xb" + s])
-
     def step(c, t):
         s = str(c)
-        cur[0] = c
-        E, G, pK, MX, DL = B("E", c), B("G", c), B("pK", c), B("MX", c), B("DL", c)
-        n1 = T.N1[0:Q, 32 * c:32 * c + 32]
-        pieces = PIECES_END if (t == 1 and c == 0) or (t == RO and c == NC - 1) else PIECES if t < T2 else PIECES2
-        prevp = {}
-        for q, a, b in pieces:
-            (cp if q == "dve" else act)(G[:, 16 * a:16 * b], T.TB[:].indirect(B("O", c)[:, a:b]), TBall + ["O" + s],
-                                        ["G%s_%d" % (s, x) for x in range(a, b, 2)], dur=ga(16 * (b - a)))
-            if q in prevp:
-                ops[-1]["order"].add(prevp[q])
-            prevp[q] = len(ops) - 1
 
-        def codes(bk, upto, st, sp):
-            mm(T[bk][0:Q, 0:32], T.IQ[0:Q, :], n1, st, False, ["IQ", "N1" + s], [bk], Q, 32)
+        def tag(nm):
+            cur[0] = (nm, NC * t + c) if t else None
+        E, X, SC, DL, OG, NR = B("E", c), B("X", c), B("SC", c), B("DL", c), B("OG", c), B("NR", c)
+        pK, pH = B("pK", c), B("pH", c)
+        En = lambda u: ["E%d_%d_%d" % (c, u, m) for m in range(2)]
+        mk = lambda m: slice(64 * m, 64 * m + Q)
+        gd = lambda m: slice(18 * m, 18 * m + 16)
+        key, g0 = pK[0:Q, 0:36], 32 * Q * c
+
+        def changes(out, bk, upto, sp):
             for u in range(1, upto + 1):
-                mm(T[bk][0:Q, 0:32], T.IQ[0:Q, :], DL[0:Q, 32 * u - 32:32 * u], False, sp and u == upto,
-                   ["IQ", "DL%s_%d0" % (s, u), "DL%s_%d1" % (s, u)], [bk], Q, 32)
-        mm(pK[0:Q, 0:32], T.KS[0:65, Q * c:Q * c + Q], T.RS[0:65, :], True, False, ["KS", "KSc", "RS", "RSc0", "RSc1"], ["pK" + s], Q, 32)
-        codes("pK" + s, t - 1, False, False)
-        for eh in range(2):
-            for el in range(16):
-                mm(pK[0:Q, 0:32], G[:, 16 * Q * eh + el:16 * Q * (eh + 1):16], T.SR[:], False, eh == 1 and el == 15,
-                   ["SR"] + ["G%s_%d" % (s, x) for x in range(Q * eh, Q * eh + Q, 2)], ["pK" + s], Q, 32)
-        for m in range(2):
-            add("dve", lambda m=m: V_.tensor_reduce(MX[0:Q, m:m + 1], pK[0:Q, 16 * m:16 * m + 16], AX.X, ALU.max),
-                ["pK" + s], ["MX%s_%d" % (s, m)], vcost(16))
-        mx = ["MX%s_%d" % (s, m) for m in range(2)]
-        ts(B("RQ", c)[0:Q, :], MX[0:Q, :], CR, CR, ALU.add, ALU.subtract, mx, ["RQ" + s])
-        for m in range(2):
-            ts(E[0:Q, 2 * t + m:2 * t + m + 1], MX[0:Q, m:m + 1], B("RQ", c)[0:Q, m:m + 1], B("F", c)[0:Q, m:m + 1],
-               ALU.subtract, ALU.max, [mx[m], "RQ" + s, "F" + s + "_"], ["E%d_%d_%d" % (c, t, m)])
-        tt(B("D", c)[0:Q, :], E[0:Q, 2 * t - 2:2 * t], E[0:Q, 2 * t:2 * t + 2], ALU.subtract,
-           ["E%d_%d_%d" % (c, u, m) for u in (t - 1, t) for m in range(2)], ["D" + s])
-        for m in range(2):
-            ts(DL[0:Q, 32 * t - 32 + 16 * m:32 * t - 16 + 16 * m], pK[0:Q, 16 * m:16 * m + 16], MX[0:Q, m:m + 1],
-               B("D", c)[0:Q, m:m + 1], ALU.is_equal, ALU.mult, ["pK" + s, mx[m], "D" + s], ["DL%s_%d%d" % (s, t, m)])
-        after_decision(c, t)
-        if t == RO:
-            codes("pG" + s, RO, True, True)
-            act(n1, B("pG", c)[0:Q, 0:32], ["pG" + s], ["N1" + s])
+                mm(out, T.ID[0:Q, 0:Q], DL[0:Q, blk(u - 1, 36)], False, sp and u == upto,
+                   ["ID", "DL%s_%d0" % (s, u), "DL%s_%d1" % (s, u)], [bk], Q, 36)
+        if t == 0:
+            mm(key, T.CN[:, blk(c, Q)], T.RN[:], True, True, ["CN", "RN"], ["pK" + s], Q, 36)
+            mm(pK[0:Q, 64:66], T.CN[:, blk(c, Q)], T.SO[:], True, True, ["CN", "SO0", "SO1"], ["pK" + s], Q, 2)
+            for m in range(2):
+                act(E[mk(m), 0:1], pK[0:Q, 64 + m:65 + m], ["pK" + s], [En(0)[m]])
+            act(NR[mk(1), :], key, ["pK" + s], ["N" + s], bias=8.0)
+        else:
+            for nm, a, b in PIECES_END if (t == 1 and c == 0) or (t == RO and c == NC - 1) else PIECES:
+                tag(nm)
+                (cp if nm[0] == "g" else act)(T.G[:, g0 + 16 * a:g0 + 16 * b], T.TB[:].indirect(B("O", c)[:, a:b]),
+                                              TBall + ["O" + s], ["G%s_%d" % (s, x) for x in range(a, b, 2)], dur=ga(16 * (b - a)))
+            tag("k0")
+            mm(key, T.KS[0:113, blk(c, Q)], NR[0:113, :], True, False, ["KS", "KSc" + s, "NRa" + s, "NRb" + s, "N" + s], ["pK" + s], Q, 36)
+            changes(key, "pK" + s, t - 1, False)
+            for eh in range(2):
+                a = g0 + 16 * Q * eh
+                for el in range(16):
+                    tag("k%d" % (2 * eh + el // 8 + 1))
+                    mm(key, T.G[:, a + el:a + 16 * Q:16], T.SR[:], False, eh == 1 and el == 15,
+                       ["SR"] + ["G%s_%d" % (s, x) for x in range(Q * eh, Q * eh + Q, 2)], ["pK" + s], Q, 36)
+            tag("SC")
+            add("dve", lambda: V_.tensor_tensor_scan(SC[0:Q, :], T.RZ[0:Q, :], key, LOW, ALU.add, ALU.max),
+                ["RZ", "pK" + s], ["SC" + s], vcost(36))
+            tag("E")
+            for m in range(2):
+                ts(E[mk(m), t:t + 1], SC[0:Q, 18 * m + 15:18 * m + 16], SC[0:Q, 18 * m + 17:18 * m + 18],
+                   -8.0 if t == 1 else pK[mk(m), 65:66], ALU.subtract, ALU.max, ["SC" + s, "pK" + s], [En(t)[m]])
 
-    for c in range(NC):
-        s = str(c)
-        pK = B("pK", c)
-        mm(pK[0:Q, 0:34], T.CN[:, Q * c:Q * c + Q], T.SO[:], True, True, ["CN", "SO", "SO0", "SO1"], ["pK" + s], Q, 34)
-        cp(T.N1[0:Q, 32 * c:32 * c + 32], pK[0:Q, 0:32], ["pK" + s], ["N1" + s])
-        cp(B("E", c)[0:Q, 0:2], pK[0:Q, 32:34], ["pK" + s], ["E%d_0_0" % c, "E%d_0_1" % c])
-        after_decision(c, 0)
-
-    def og(t0, n):
-        return ["OG%d_%d" % (u, c) for u in range(t0, t0 + n) for c in range(NC)]
-
-    def replay(nm, t0, n):
-        w = 6 * n
+        def rows(out, a, K, bk):
+            for qh in range(QH):
+                mm(out[:, a + qh:a + qh + 1], T.AT[0:K, blk(qh, 128)], E[0:K, t:t + 1], True, True,
+                   ["A%d" % qh, "Ec" + s] + En(t), [bk], 128, 1)
+        if t < RO:
+            tag("pT")
+            rows(pK, 72, 113, "pK" + s)
+            if t < RO - 1:
+                rows(pK, 72 + QH, 114, "pK" + s)
+            tag("OG")
+            w = 2 * QH if t < RO - 1 else QH
+            ts(OG[:, 0:w], pK[:, 72:72 + w], PF(2), None, ALU.add, None, ["pK" + s, "F1"], ["OG" + s])
+        if t > 0:
+            tag("H")
+            rows(T.pT, 6 * (t - 1) + QH * c, 113, "pT")
+            tag("D")
+            mm(pK[0:96, 64:65], T.ID[0:96, 0:96], E[0:96, t - 1:t], True, False, ["ID"] + En(t - 1), ["pK" + s], 96, 1)
+            mm(pK[0:96, 64:65], T.NI[0:96, 0:96], E[0:96, t:t + 1], False, True, ["NI"] + En(t), ["pK" + s], 96, 1)
+            if t < RO:
+                mm(pK[0:96, 65:66], T.FQ[0:113, :], E[0:113, t:t + 1], True, True, ["FQ", "Ec" + s] + En(t), ["pK" + s], 96, 1)
+            tag("DL")
+            lab = lambda k, m: (B("M", k)[blk(c), 8 + 16 * m:24 + 16 * m], "L%d_%d%d" % (k, c, m))
+            for m in range(2):
+                a = 36 * (t - 1) + 18 * m
+                out, nm = (DL[0:Q, a:a + 16], "DL%s_%d%d" % (s, t, m)) if t < RO else lab(NB + 1, m)
+                ts(out, pK[0:Q, gd(m)], SC[0:Q, 18 * m + 15:18 * m + 16], pK[mk(m), 64:65],
+                   ALU.is_equal, ALU.mult, ["pK" + s, "SC" + s], [nm])
+        if t == RO and c >= NC - 2:
+            tag("M")
+            k, a = (NB, 0) if c == NC - 2 else (NB + 1, QH * c)
+            act(B("M", k)[:, 0:QH * (c + 1) - a], T.pT[:, 30 + a:30 + QH * (c + 1)], ["pT"], ["M%d" % k], scale=1.0 / Q)
+        if t < RO:
+            Xr = ["X" + s, "Xa" + s, "Xb" + s]
+            tag("G3")
+            cp(B("G3", c)[:], X[:].indirect(OG[:, blk(0 if t else 1, QH)]), Xr + ["OG" + s], ["G3" + s], dur=ga(Q))
+            g3, rd, h = B("G3", c)[0:96, :], ["WK", "WN", "G3" + s], pH[:, 0:2 * Q]
+            tag("z")
+            const(h, 0, 2 * Q, True, False, "pH" + s)
+            tag("pH")
+            for eh in range(2):
+                mm(pH[:, blk(eh, Q)], T.WK[0:96, 256 + eh:512:2], g3, False, False, rd, ["pH" + s], 128, Q)
+            const(h, 1, 2 * Q, False, False, "pH" + s)
+            const(h, 2, 2 * Q, False, False, "pH" + s)
+            for eh in range(2):
+                mm(pH[:, blk(eh, Q)], T.WK[0:96, eh:256:2], g3, False, False, rd, ["pH" + s], 128, Q)
+            const(h, 3, 2 * Q, False, True, "pH" + s)
+            tag("O")
+            ts(B("O", c)[:], h, 4095.0, None, ALU.min, None, ["pH" + s], ["O" + s], 2 * Q)
+        if t == RO - 1:
+            tag("N")
+            mm(pH[blk(c), 256:292], T.ID[:, 64:64 + Q], NR[:], True, False, ["ID", "NRa" + s, "NRb" + s, "N" + s], ["pH" + s], Q, 36)
+            changes(pH[blk(c), 256:292], "pH" + s, RO - 1, True)
+            for m in range(2):
+                act(lab(NB, m)[0], pH[blk(c), 256 + 18 * m:272 + 18 * m], ["pH" + s], [lab(NB, m)[1]])
+        if 0 < t < RO - 1:
+            tag("SG")
+            mm(pH[:, 128:128 + Q], T.SG[0:96, :], g3, True, True, ["SG", "G3" + s], ["pH" + s], 128, Q)
+            tag("NV")
+            act(B("NV", c)[:], pH[:, 128:128 + Q], ["pH" + s], ["NV" + s], Q)
+            tag("X")
+            cp(X[:].indirect(OG[:, blk(1, QH)]), B("NV", c)[:], ["NV" + s, "OG" + s], Xr, dur=sc(Q))
+            gcp(X[0:32, blk(16, Q)], X[0:32, blk(0, Q)], ["X" + s], ["Xa" + s])
+            gcp(X[32:64, blk(1, Q)], X[32:64, blk(17, Q)], ["X" + s], ["Xb" + s])
         cur[0] = None
-        R, DU, V = T["R" + nm], T["DU" + nm], T.VN[:]
-        DF, DB, DX, DY, DZ = T.DF, T.DB, T.DX, T.DY, T.DZ
-        DO = DX[:, 2 * w:3 * w]
-        for r in range(N):
-            a, b = 32 * r, 32 * r + 32
-            if r == rho:
-                cp(DX[a:b, 2 * w:3 * w], T.OG[a:b, 6 * t0 - 6:6 * t0 - 6 + w], og(t0, n), ["DO%d" % r])
-            else:
-                cp(DX[a:b, 2 * w:3 * w], R[a:b, w * r:w * r + w], ["R%s%d" % (nm, r)], ["DO%d" % r])
-        do = ["DO%d" % r for r in range(N)]
-        for k, v in enumerate((960.0, 896.0)):
-            ts(DX[:, k * w:k * w + w], DO, v, None, ALU.add, None, do, ["DX%d" % k])
-        ts(DF[:, 0:w], DO, 1088.0, 1536.0, ALU.is_ge, ALU.mult, do, ["DF"])
-        tt(DB[:, 0:w], DF[:, 0:w], T.BS2[:, 0:w], ALU.add, ["DF", "BS2"], ["DB"])
-        ts(DY[:, 0:3 * w], DX[:, 0:3 * w], 6, 15, ALU.arith_shift_right, ALU.bitwise_and, ["DX0", "DX1"] + do, ["DY"], 3 * w)
-        tt(DZ[:, 0:w], DY[:, 0:w], DB[:, 0:w], ALU.add, ["DY", "DB"], ["DZ0"])
-        tt(DZ[:, w:3 * w], DY[:, w:3 * w], T.BS2[:, 0:2 * w], ALU.add, ["DY", "BS2"], ["DZ1"], w)
-        cp(DU[:, 0:3 * w], DZ[:, 0:3 * w], ["DZ0", "DZ1"], ["DU" + nm], 3 * w)
-        for u in range(n):
-            o = [DU[:, k * w + 6 * u:k * w + 6 * u + 6] for k in range(3)]
-            rd = ["V", "Vj", "DU" + nm]
-            (act if t0 < RO else cp)(T.RA[:], V.indirect(o[0]), rd, ["RA"], dur=ga(96))
-            act(T.RC[:], V.indirect(o[2]), rd, ["RC"], dur=ga(96))
-            tt(T.RB[:], V.indirect(o[1]), T.RA[:], ALU.subtract, rd + ["RA"], ["RB"], dur=ga(96))
-            tt(V.indirect(o[0]), T.RB[:], T.RC[:], ALU.add, ["RB", "RC", "DU" + nm], ["V", "Vj"], dur=sc(96))
 
-    for t in range(1, RO + 1):
+    def publish(k, w, r):
+        send("o%d" % k, far + near, lambda _: B("M", k)[:, 0:w], B("R", k)[:, blk(rho, w)], r, lambda x: "R%d%d" % (k, x), LB[k])
+
+    def replay(k, n, ws, c0, c1):
+        w, co, base, bk = n * QH * (c1 - c0), QH * c0, VS * c0, "pY" if c0 == 0 else "pT"
+        Y, DU = T[bk], B("DU", k)
+
+        def row(a, b, st, sp):
+            mm(Y[:, 0:54], T.ON[0:1, blk(a, 128)], T.CW[0:1, blk(b, 54)], st, sp, ["ONa", "CW"], [bk], 128, 54)
+
+        def slots(lhs):
+            for r in [rho, rnear] + rfar:
+                src, sn = (B("M", k)[:, 0:w], "M%d" % k) if r == rho else (B("R", k)[:, ws * r:ws * r + w], "R%d%d" % (k, r))
+                for ty in range(3):
+                    mm(Y[blk(r), 18 * ty + co:18 * ty + co + w], T[lhs[ty]][:, blk(r)], src, False, False, [lhs[ty], sn], [bk], 32, w)
+        row(0, 0, True, False)
+        slots(("NI", "IS", "NI"))
+        row(6, 3, False, False)
+        row(7, 3, False, False)
+        slots(("ID", "ID", "ID"))
+        row(0, 1, False, False)
+        row(1, 2, False, True)
+        ts(DU[:], Y[:, 0:54], PF(11), -float(base), ALU.add, ALU.add, [bk, "F8"], ["DU%d" % k])
+        V = T.VN[:, VS * c0:VS * c1]
+        Vn = ["V%d" % x for x in range(c0, c1)] + ["Vj%d" % x for x in range(c0, c1)]
+        a, b = Q * c0, Q * c1
+        nm = lambda x: [x + str(y) for y in range(c0, c1)]
+        o = lambda ty, u: DU[:, 18 * ty + 6 * u + co:18 * ty + 6 * u + QH * c1]
+        rd = Vn + ["DU%d" % k]
+
+        def old(u):
+            act(B("RA", u % 2)[:, a:b], V.indirect(o(1, u)), rd, nm("RA%d" % (u % 2)), dur=ga(b - a))
+        old(0)
+        for u in range(n):
+            (act if u else cp)(T.RC[:, a:b], V.indirect(o(2, u)), rd, nm("RC"), dur=ga(b - a))
+            tt(T.RB[:, a:b], V.indirect(o(0, u)), B("RA", u % 2)[:, a:b], ALU.subtract, rd + nm("RA%d" % (u % 2)), nm("RB"), dur=ga(b - a))
+            if u + 1 < n:
+                old(u + 1)
+            tt(V.indirect(o(1, u)), T.RB[:, a:b], T.RC[:, a:b], ALU.add, nm("RB") + nm("RC") + ["DU%d" % k], Vn, dur=sc(b - a))
+
+    for t in range(RO + 1):
         for c in range(NC):
             step(c, t)
+            if t == RO and c >= NC - 2:
+                k = NB + c - NC + 2
+                publish(k, 40, ["M%d" % k] + ["L%d_%d%d" % (k, x, m) for x in range(NC) for m in range(2)])
         for k, (t0, n) in enumerate(BATCH):
             if t == t0 + n - 1:
-                send("o%d" % k, lambda r, t0=t0, n=n: T.OG[:, 6 * t0 - 6:6 * (t0 + n) - 6],
-                     T["R%d" % k][:, 6 * n * rho:6 * n * rho + 6 * n], og(t0, n), lambda r, k=k: "R%d%d" % (k, r),
-                     5000.0 if t < RO else 3000.0)
-    send("n", lambda r: T.N1[:], T.RN[:, 64 * rho:64 * rho + 64], ["N10", "N11", "N1c"], lambda r: "RN%d" % r, 3000.0)
+                act(B("M", k)[:, 0:6 * n], T.pT[:, 6 * t0 - 6:6 * (t0 + n) - 6], ["pT"], ["M%d" % k], scale=1.0 / Q)
+                publish(k, 6 * n, ["M%d" % k])
     for k, (t0, n) in enumerate(BATCH):
-        replay(str(k), t0, n)
-    dma("sync", T.yv[:], T.VN[:, 0:1536], ["V"], [], 393216)
-    for r in range(N):
-        for c in range(NC):
-            src = T.N1[0:65, 32 * c:32 * c + 32] if r == rho else T.RN[0:65, 64 * r + 32 * c:64 * r + 32 * c + 32]
-            mm(T.pH0[32 * r:32 * r + 32, Q * c:Q * c + Q], src, T.IQ[0:65, :], True, True,
-               ["IQ", "IQc"] + (["N10", "N11", "N1c"] if r == rho else ["RN%d" % r]), ["pH0"], 32, Q)
-    tt(T.YI[:], T.pH0[:, 0:96], T.CAP[:], ALU.min, ["pH0", "CAP"], ["YI"], 96)
-    dma("act", T.yi[:], T.YI[:], ["YI"], [], 49152)
+        replay(k, n, 6 * n, 0, NC)
+    for k, c0, c1 in ((NB, 0, NC - 1), (NB + 1, NC - 1, NC)):
+        replay(k, 1, 40, c0, c1)
+        for c in range(c0, c1):
+            dma("sync", T.yv[:, blk(c, VW)], T.VN[:, VS * c:VS * c + VW], ["V%d" % c], [], 256 * VW)
+    for r in [rho, rnear] + rfar:
+        for k in (NB, NB + 1):
+            src, nm = B("R", k)[:, 40 * r + 8:40 * r + 40], ["R%d%d" % (k, r)]
+            if r == rho:
+                src, nm = B("M", k)[:, 8:40], ["L%d_%d%d" % (k, x, m) for x in range(NC) for m in range(2)]
+            mm(T.pK0[blk(r), 0:96], src, T.ID[:, 0:96], k == NB, k > NB, ["ID"] + nm, ["pK0"], 32, 96)
+    tt(T.YI[:], T.pK0[:, 0:96], T.CAP[:], ALU.min, ["pK0", "CAP"], ["YI"], 96)
+    dma("act", T.yi[:], T.YI[:], ["YI"], [], 49152 * YF)
     return ops
 
 
 def schedule(ops):
     n = len(ops)
+    named = {}
+    for i, o in enumerate(ops):
+        named.setdefault((o["q"], o["ch"]), []).append(i)
+    for q, names in ROUND.items():
+        seq = [i for h in range(-4, NC * RO + 8) for nm, d in names for i in named.get((q, (nm, h + d)), [])]
+        for a, b in zip(seq, seq[1:]):
+            ops[b]["order"].add(a)
     succ = [[] for _ in range(n)]
     for i, o in enumerate(ops):
         for j in o["deps"] | o["order"]:
             succ[j].append(i)
+    left = [len(o["deps"] | o["order"]) for o in ops]
+    sequence = [i for i in range(n) if left[i] == 0]
+    for i in sequence:
+        for j in succ[i]:
+            left[j] -= 1
+            if left[j] == 0:
+                sequence.append(j)
+    assert len(sequence) == n
     prio = [0.0] * n
-    for i in range(n - 1, -1, -1):
+    for i in reversed(sequence):
         o = ops[i]
         best = 0.0
         for j in succ[i]:
             best = max(best, prio[j] + (o["lat"] + HOP if i in ops[j]["deps"] else 0.0))
         prio[i] = max(best, o["lat"]) + o["dur"]
-    x = SEED
     for i, o in enumerate(ops):
-        x = (x * 1103515245 + 12345) % 2147483648
-        prio[i] += (BIAS if o["ch"] == 0 else 0.0) + JIT * x / 2147483648.0
+        prio[i] -= BIAS * (o["ch"][1] % NC) if o["ch"] else 0.0
     left = [len(o["deps"] | o["order"]) for o in ops]
     ready_at = [0.0] * n
     pool = [i for i in range(n) if left[i] == 0]
@@ -446,14 +541,13 @@ def schedule(ops):
         o = ops[i]
         free[o["q"]] = start[i] + o["dur"]
         end[i] = start[i] + o["dur"] + o["lat"]
-        o["t"] = start[i]
         order.append(i)
         for j in succ[i]:
             ready_at[j] = max(ready_at[j], end[i] + HOP if i in ops[j]["deps"] else start[i] + o["dur"])
             left[j] -= 1
             if left[j] == 0:
                 pool.append(j)
-    return order, max(end)
+    return order
 
 
 def emit(g, T, ops, order):
@@ -508,5 +602,4 @@ def rank_program(g, core, T, topo):
     if T.rank_of(core) is None:
         return
     ops = build(g, core, T, topo)
-    order, _ = schedule(ops)
-    emit(g, T, ops, order)
+    emit(g, T, ops, schedule(ops))

@@ -7,44 +7,47 @@ ROWS = 19
 CR = 402653184.0
 LOW = -67108864.0
 VW, VS = 16 * Q, 32 * Q + 16
-CUT = [0, 768, 1024]
-PIECES = [("A1", 0, 24), ("g1", 24, 32), ("g2", 32, 40), ("A2", 40, 64)]
+CUT = [(0, 0, 128), (0, 128, 1024), (1, 0, 640), (2, 0, 1024), (1, 640, 1024)]
+STAGE = [(0, 0, 128), (0, 128, 1024), (1, 0, 1024), (2, 0, 1024)]
+LATE = 4
+PIECES_ONE = [("A1", 0, 48), ("g1", 48, 96), ("A2", 96, 144), ("g2", 144, 192)]
+PIECES = [("A1", 0, 22), ("g1", 22, 32), ("g2", 32, 42), ("A2", 42, 64)]
 PIECES_END = [("A1", 0, 16), ("g1", 16, 32), ("g2", 32, 48), ("A2", 48, 64)]
 ROUND = {
     "dve": [("OG", -2), ("g1", 0), ("G3", -2), ("SC", -1), ("g2", 0), ("E", -1), ("O", -2), ("X", -3), ("DL", -2)],
-    "act": [("A1", 0), ("NV", -3), ("A2", 0)],
-    "pe": [("k3", -1), ("k4", -1), ("SG", -3), ("D", -2), ("H", -2), ("z", -2), ("k0", 0), ("pH", -2), ("k1", 0), ("pT", -1),
+    "act": [("A1", 0), ("NV", -3), ("A2", 0), ("M", -2), ("N", -3)],
+    "pe": [("k3", -1), ("k4", -1), ("SG", -3), ("N", -3), ("D", -2), ("H", -2), ("z", -2), ("k0", 0), ("pH", -2), ("k1", 0), ("pT", -1),
            ("k2", 0)],
 }
-BATCH = [(1, 2), (3, 2), (5, 1)]
+BATCH = [(1, 2), (3, 2)]
 NB = len(BATCH)
-LB = [4000.0, 4000.0, 3500.0, 3500.0, 3500.0]
-HOP, WIN, YF, BIAS = 210.0, 60.0, 8, 0.0
+LB = [4000.0, 4000.0, 3200.0, 3500.0]
+HOP, WIN, YF, BIAS = 210.0, 60.0, 8, 1000.0
 GAM, SIG, CYC, PEC = 1.35, 3.3, 0.86, 0.47
-LAT, RATE = 1200.0, 250.0
-LW, LF, LN = 5000.0, [8000.0, 9000.0], 5000.0
-ACTC = [1, 1, 1]
+LAT, RATE = 1200.0, 400.0
+LZ, LF = [3800.0, 3000.0], [5000.0, 5000.0, 5500.0, 4500.0, 4500.0]
+ACTC = [1, 2, 2, 1, 2]
 
 SCRATCH = {}
-for _d, _l in (("bfloat16", "TB 4096 SB 3072 LD 4096 VN 3120 VO 1536 VR 1536 G 3072 RP 128 RN 36 WS 32 WA 128 WK 512 KS 96 CN 96 "
-                            "AT 256 SM 192 SG 128 SR 36 ID 128 NI 128 IS 128 FQ 96 SO 2 ON 1024 CK 64 CW 216 "
-                            "RA0 96 RA1 96 RB 96 RC 96 M0 18 M1 18 M2 18 M3 40 M4 40 R0 72 R1 72 R2 72 R3 160 R4 160"),
-               ("int32", "IV 96 SU 96 SU2 96 PI 1 PJ 6 I1 38 I2 38 I3 38 J128 128 JK 36 JJ 128"),
-               ("float32", "CA 96 CB 96 CAP 96 YI 96 PF 26 JX 128 RZ 36"),
-               ("uint16", "IU 38 DU0 54 DU1 54 DU2 54 DU3 54 DU4 54")):
+for _d, _l in (("bfloat16", "TB 4096 SB 3072 LD 4096 VN 3120 VR 1536 G 3072 RP 128 IP 144 WS 36 WA 128 WK 512 WO 512 KS 96 CA 96 CB 96 CN 96 "
+                            "AT 256 SM 384 SG 128 SR 36 ID 128 NI 128 IS 128 BO 128 DM 96 P1 96 FQ 96 E 24 SO 2 ON 1024 CK 192 CW 312 "
+                            "RA0 96 RA1 96 RB 96 RC 96 M0 18 M1 18 M2 40 M3 40 R0 72 R1 72 R2 160 R3 160"),
+               ("int32", "IV 96 SU 96 SU2 96 PI 1 PJ 6 I1 38 I2 38 I3 38 J128 128 JK 36 JJ 128 JL 96 JG 128"),
+               ("float32", "CAP 96 YI 96 PF 40 JX 128 RZ 36 MK 8 SK 96 XD 96 XS 96 SEL 96 LF 144"),
+               ("uint16", "L1 6 OW 192 MS 108 LP 160 IU 38 DU0 54 DU1 54 DU2 54 DU3 54")):
     _l = _l.split()
     for _k in range(0, len(_l), 2):
         SCRATCH[_l[_k]] = ("sbuf", [128, int(_l[_k + 1])], _d)
 for _c in range(NC):
     for _n, _s, _d in (("X", ROWS * Q, "bfloat16"), ("O", 2 * Q, "uint16"), ("OG", 2 * QH, "uint16"),
-                       ("G3", Q, "bfloat16"), ("NV", Q, "bfloat16"), ("E", 8, "bfloat16"),
+                       ("G3", Q, "bfloat16"), ("NV", Q, "bfloat16"),
                        ("SC", 36, "float32"), ("DL", 36 * RO, "bfloat16"), ("NR", 36, "bfloat16")):
         SCRATCH["%s%d" % (_n, _c)] = ("sbuf", [128, _s], _d)
 for _n in ("pK0", "pK1", "pK2", "pH0", "pH1", "pH2", "pT", "pY"):
     SCRATCH[_n] = ("psum", [128, 512], "float32")
 
-SEMAPHORES = (["q_pe", "q_dve", "q_act", "q_g", "ls"] + ["d%d" % k for k in range(32)]
-              + ["a%s%d" % (n, r) for n in ("w", "t0", "t1", "t2", "tn", "o0", "o1", "o2", "o3", "o4") for r in range(N)])
+SEMAPHORES = (["q_pe", "q_dve", "q_act", "q_g", "ls"] + ["d%d" % k for k in range(40)]
+              + ["a%s%d" % (n, r) for n in ("z", "t0", "t1", "t2", "t3", "t4", "t5", "o0", "o1", "o2", "o3") for r in range(N)])
 
 
 def _engine_sets(topo, cores, src):
@@ -161,17 +164,19 @@ def build(g, core, T, topo):
     def gcp(out, a, r, w):
         add("g", lambda: g.affine_select(out, a, [[0, Q]], ALU.is_ge, 0.0, 0, 0), r, w, 170.0 + 2 * Q * CYC)
 
-    def send(name, peers, src, dst, r, w_in, lat):
+    def send(name, peers, src, dst, r, w_in, lat, alone=False):
+        use = {c: list(topo.engines(core, c)) if alone else eng[c] for c in peers}
+
         def fn():
             trs = []
             for c in peers:
                 rid, pid = topo.addr(c, core)
-                trs.append(RemoteDMATransfer(dst_ids=[DstId(rid=rid, pnc=pid)], dma_engine_mask=sum(1 << e for e in eng[c]),
+                trs.append(RemoteDMATransfer(dst_ids=[DstId(rid=rid, pnc=pid)], dma_engine_mask=sum(1 << e for e in use[c]),
                                              remote_sem=T.sem["a%s%d" % (name, rho)], src=src(rk[c]), dst=dst))
             return g.remote_dma_fused(trs, local_sem=T.sem["ls"])
-        i = add("g", fn, r, [], 800.0, kind="send", cnt=sum(len(eng[c]) for c in peers), fixed=True)
+        i = add("g", fn, r, [], 800.0, kind="send", cnt=sum(len(use[c]) for c in peers), fixed=True)
         for c in sorted(peers, key=lambda c: c in far):
-            k = len(_engine_sets(topo, cores, c)[2][core])
+            k = len(topo.engines(c, core) if alone else _engine_sets(topo, cores, c)[2][core])
             j = add("rx", None, [], [w_in(rk[c])], 0.0, lat=lat * (0.8 if c in near else 1.0), kind="rx",
                     sem="a%s%d" % (name, rk[c]), cnt=k)
             ops[j]["order"].add(i)
@@ -179,56 +184,44 @@ def build(g, core, T, topo):
     def blk(r, n=32):
         return slice(n * r, n * r + n)
 
-    NP = len(CUT) - 1
-    peers = rfar + [rnear]
-    TBall = ["TB%d_%d_%d" % (r, k, j) for r in peers for k in range(4) for j in range(NP)] + ["TBo"]
-    SBn = lambda r: ["SB%d_%d" % (r, k) for k in range(4)]
+    def retag(nm):
+        cur[0] = cur[0] and (nm, cur[0][1])
 
-    def stage(r):
-        for k in range(4):
-            dma(("sync", "act")[k % 2], T.SB[blk(k), blk(peers.index(r), 1024)], T.dem[blk(r), blk(k, 1024)], [],
-                [SBn(r)[k]], 65536, True)
+    order = sorted(far, key=lambda c: topo.die(c) != topo.die(core)) + near
+    peers = [rk[c] for c in order]
+    TBall = ["TB%d_%d" % (j, x) for j in range(len(CUT)) for x in range(4)] + ["TBo"]
 
-    dma("act", T.WS[:], T.wt[:], [], ["WS"], 8192, True)
-    for r in rfar:
-        stage(r)
-    dma("sync", T.VO[0:32, :], T.v[blk(rho), :], [], ["VO"], 98304, True)
+    def stage(k, a, b):
+        for x in range(4):
+            dma("act" if (k, a, x % 2) == (0, 0, 1) else "sync", T.SB[blk(x), 1024 * k + a:1024 * k + b], T.dem[blk(peers[k]), 1024 * x + a:1024 * x + b], [],
+                ["SB%d_%d_%d" % (k, a, x)], 64 * (b - a), True)
+
+    def piece(j):
+        k, a, b = CUT[j]
+        send("t%d" % j, [order[k]], lambda r: T.SB[:, 1024 * k + a:1024 * k + b], T.LD[:, 1024 * rho + a:1024 * rho + b],
+             ["SB%d_%d_%d" % (k, lo, x) for kk, lo, hi in STAGE if kk == k and lo <= a < hi for x in range(4)],
+             lambda r: "LD%d" % j, LF[j], alone=k < 2)
+
+    stage(*STAGE[0])
     dma("act", T.IV[:], T.inv[:], [], ["IV"], 49152, True)
-    stage(rnear)
-    dma("act", T.SU[0:32, :], T.sup[blk(rho), :], [], ["SUa"], 12288, True)
-    dma("act", T.SU[32:64, :], T.sup[blk(rho), :], [], ["SUb"], 12288, True)
-    dma("sync", T.TB[blk(rho), :], T.dem[blk(rho), :], SBn(rnear), ["TBo"], 262144 * 5)
+    dma("act", T.WS[:, 0:32], T.wt[:], [], ["WS"], 8192, True)
+    for c in range(NC):
+        dma("act", T.VN[:, VS * c:VS * c + VW], T.v[:, blk(c, VW)], [], ["V%d" % c], 256 * VW, True)
+    dma("act", T.TB[:], T.dem[:], [], TBall, 1048576, True)
+    for a in STAGE[1:]:
+        stage(*a)
+    dma("sync", T.SU[0:32, :], T.sup[blk(rho), :], [], ["SUa"], 12288, True)
+    dma("sync", T.SU[32:64, :], T.sup[blk(rho), :], [], ["SUb"], 12288, True)
     iota(T.PI[:], [[0, 1]], 0, 1, ["PI"], 1, False)
     iota(T.J128[:], [[1, 128]], 0, 0, ["J128"], 128, False)
+    iota(T.CW[0:1, 216:312], [[4 * VS, NC], [64, Q]], 0, 0, ["BR"], 96, True)
+    iota(T.JK[:], [[32, 2], [1, 18]], 0, 0, ["JK"], 36, False)
+    piece(0)
     iota(T.I1[:], [[1, ROWS], [0, QH]], 15, 0, ["I1"], ROWS * QH, False)
     iota(T.I2[:], [[0, ROWS], [256, QH]], 0, 0, ["I2"], ROWS * QH, False)
-    iota(T.JK[:], [[32, 2], [1, 18]], 0, 0, ["JK"], 36, False)
-    send("w", far + near, lambda r: T.WS[:], T.WA[:, blk(rho)], ["WS"], lambda r: "WA%d" % r, LW)
     iota(T.JX[:], [[0, 4], [1000, 2], [1, 16]], 0, 0, ["JX"], 128, True)
-    for j in range(NP):
-        a, b = CUT[j], CUT[j + 1]
-        send("t%d" % j, far, lambda r, a=a, b=b: T.SB[:, 1024 * peers.index(r) + a:1024 * peers.index(r) + b],
-             T.LD[:, 1024 * rho + a:1024 * rho + b], SBn(rfar[0]) + SBn(rfar[1]), lambda r, j=j: "LD%d_%d" % (r, j), LF[j])
-    send("tn", near, lambda r: T.SB[:, 2048:3072], T.LD[:, blk(rho, 1024)], SBn(rnear), lambda r: "LDn", LN)
-    u4 = 64 // Q
-    for ty, (st, b) in enumerate(((u4, 38), (-64, -34 * Q), (u4, 30))):
-        iota(T.CW[0:1, blk(ty, 18)], [[0, 18 // QH], [st, QH]], b, 0, ["CW"], 18, True)
-    iota(T.CW[0:1, 54:108], [[4, 3], [0, 18 // QH], [-u4, QH]], -8, 0, ["CW"], 54, True)
-    iota(T.CW[0:1, 108:162], [[0, 9], [VS // 16, NC], [16, QH]], 0, 0, ["CW"], 54, True)
-    iota(T.CW[0:1, 162:216], [[0, 54]], 1, 0, ["CW"], 54, True)
-    iota(T.CW[0:1, 180:198], [[0, 18]], Q, 0, ["CW"], 18, True)
-    for c in range(NC):
-        dma("sync", T.VN[:, VS * c:VS * c + VW], T.v[:, blk(c, VW)], ["LD%d_%d" % (r, NP - 1) for r in rfar], ["V%d" % c], 256 * VW * (c + 1))
-
-    def unfold(r, a, b, src, names, nact):
-        for k in range(4):
-            f, n = (act, b - a) if k < nact else (cp, (b - a) // 2)
-            f(T.TB[blk(r), 1024 * k + a:1024 * k + b], T.LD[blk(k), 1024 * r + a:1024 * r + b], [src], names(k), n)
-
-    unfold(rnear, 0, 1024, "LDn", lambda k: ["TB%d_%d_%d" % (rnear, k, j) for j in range(NP)], ACTC[0])
-    for j in range(NP):
-        for r in rfar:
-            unfold(r, CUT[j], CUT[j + 1], "LD%d_%d" % (r, j), lambda k: ["TB%d_%d_%d" % (r, k, j)], ACTC[1 + j])
+    for j in range(1, LATE):
+        piece(j)
 
     PF = lambda k, a=0, b=128: T.PF[a:b, k:k + 1]
     cp(PF(0), T.PI[:], ["PI"], ["F0"])
@@ -237,60 +230,75 @@ def build(g, core, T, topo):
         ts(T.PJ[:, k:k + 1], T.PI[:], v, None, op, None, ["PI"], ["J%d" % k])
     cp(T.PF[:, 1:7], T.PJ[:], ["J%d" % k for k in range(6)], ["F1"])
     ts(T.JJ[:], T.J128[:], 31, None, ALU.bitwise_and, None, ["J128"], ["JJ"], 128)
-    ts(PF(24), PF(1), PF(6), None, ALU.add, None, ["F1"], ["F24"])
-    ts(PF(7), PF(0), float(-32 * rho), None, ALU.add, None, ["F0"], ["F4"])
+    ts(T.JL[:], T.J128[:, 0:96], 15, None, ALU.bitwise_and, None, ["J128"], ["JL"], 96)
+    ts(T.JG[:], T.J128[:], 4, None, ALU.arith_shift_right, None, ["J128"], ["JG"], 128)
+    ts(T.MK[:], T.J128[:, 0:8], PF(3), None, ALU.is_equal, None, ["J128", "F1"], ["MK"])
+    act(PF(24), PF(1), ["F1"], ["F24"], bias=PF(6))
+    act(PF(27), PF(0), ["F0"], ["F27"], bias=-96.0)
+    act(PF(7), PF(0), ["F0"], ["F4"], bias=-32.0 * rho)
+    act(PF(9), PF(5), ["F1"], ["F6"], scale=-2.0, bias=1.0)
+    act(PF(26), PF(5), ["F1"], ["F26"], scale=2.0, bias=-1.0)
+    act(PF(11), PF(2), ["F1"], ["F8"], scale=16.0)
+    act(PF(15), PF(0), ["F0"], ["F15"], bias=-64.0)
+    act(PF(17), PF(5), ["F1"], ["F170"], scale=1000.0, bias=PF(4))
+    act(PF(18), PF(17), ["F170"], ["F171"], bias=-16.0)
     ms(PF(8, 0, 32), 1.0, ["F5a"]); ms(PF(8, 32, 64), -1.0, ["F5b"]); ms(PF(8, 64, 128), 0.0, ["F5c"])
-    F5 = ["F5a", "F5b", "F5c"]
-    ms(PF(9, 0, 64), 1.0, ["F6a"]); ms(PF(9, 64, 128), -1.0, ["F6b"])
-    F6 = ["F6a", "F6b"]
-    ts(PF(10), PF(0), 113.0, float(Q), ALU.is_equal, ALU.mult, ["F0"], ["F7"])
-    ts(PF(11), PF(2), 16.0, None, ALU.mult, None, ["F1"], ["F8"])
+    F5, F6 = ["F5a", "F5b", "F5c"], ["F6"]
     ms(PF(14, 0, 32), -65536.0, ["F11a"]); ms(PF(14, 32, 64), -512.0, ["F11b"])
-    ts(PF(15), PF(0), -64.0, None, ALU.add, None, ["F0"], ["F15"])
     ts(PF(16), PF(0), 112.0, None, ALU.is_equal, None, ["F0"], ["F16"])
-    for nm, v in (("ID", 1.0), ("NI", -1.0), ("IS", float(Q))):
-        ts(T[nm][:], T.J128[:], PF(0), v, ALU.is_equal, ALU.mult, ["J128", "F0"], [nm], 128)
+    ts(PF(10), PF(0), 113.0, float(Q), ALU.is_equal, ALU.mult, ["F0"], ["F10"])
+    ts(T.ID[:], T.J128[:], PF(0), None, ALU.is_equal, None, ["J128", "F0"], ["ID"], 128)
+    act(T.NI[:], T.ID[:], ["ID"], ["NI"], 128, scale=-1.0)
+    act(T.IS[:], T.ID[:], ["ID"], ["IS"], 128, scale=float(Q))
+    act(T.SEL[:], T.ID[:, 0:96], ["ID"], ["SEL"], 96, scale=512.0)
     for k, v in enumerate((0.25, 16.0, 31.5, 2.0 ** 29, -2.0 ** 29, 0.0, 1.5 * 2.0 ** 27, -1.5 * 2.0 ** 27)):
-        ms(T.ON[0:1, blk(k, 128)], v, ["ONc" if 1 < k < 6 else "ONa"])
+        ms(T.ON[0:1, blk(k, 128)], v, ["ON%d" % k])
     ms(T.CK[0:1, :], 65.0, ["CK"])
-    ms(T.RZ[:], 0.0, ["RZ"])
-    for a, v in ((slice(16, 36, 18), CR), (slice(17, 36, 18), -CR), (slice(18, 19), 4 * LOW)):
-        ms(T.RZ[:, a], v, ["RZ"])
-    ts(PF(23), PF(5), 1000.0, PF(4), ALU.mult, ALU.add, ["F1"], ["F23"])
+    ms(T.RZ[:], 0.0, ["RZ0", "RZ1", "RZ2"])
+    for k, (a, v) in enumerate(((slice(16, 36, 18), CR), (slice(17, 36, 18), -CR), (slice(18, 19), 4 * LOW))):
+        ms(T.RZ[:, a], v, ["RZ%d" % k])
     for qh in range(QH):
-        ts(PF(17 + qh), PF(23), -16.0 * qh, None, ALU.add, None, ["F23"], ["F17%d" % qh])
-        ts(PF(20 + qh), PF(16), 9.0 * Q + 16 * qh, None, ALU.mult, None, ["F16"], ["F20%d" % qh])
-        ts(T.AT[:, blk(qh, 128)], T.JX[:], PF(17 + qh), float(Q), ALU.is_equal, ALU.mult, ["JX", "F17%d" % qh], ["A%d" % qh], 128)
-        ts(T.AT[96:128, blk(qh, 128)], T.AT[96:128, blk(qh, 128)], PF(20 + qh, 96), None, ALU.add, None,
-           ["A%d" % qh, "F20%d" % qh], ["A%d" % qh], 64)
-        for k in range(2):
-            a = slice(128 * qh + 32 * k, 128 * qh + 32 * k + 32)
-            ts(T.AT[96:128, a], T.AT[96:128, a], PF(10, 96), None, (ALU.subtract, ALU.add)[k], None, ["A%d" % qh, "F7"], ["A%d" % qh])
-    ts(T.FQ[:], T.J128[:, 0:96], PF(0), 16.0, ALU.is_equal, ALU.mult, ["J128", "F0"], ["FQ"], 96)
-    ts(PF(22), PF(16), -120.0, None, ALU.mult, None, ["F16"], ["F22"])
-    ts(T.FQ[96:128, :], T.FQ[96:128, :], PF(22, 96), None, ALU.add, None, ["FQ", "F22"], ["FQ"])
+        ts(T.AT[0:96, blk(qh, 128)], T.JX[0:96, :], PF(17 + qh, 0, 96), float(Q), ALU.is_equal, ALU.mult, ["JX", "F17%d" % qh], ["A%d" % qh], 128)
+        for k, (a, b) in enumerate(((0, 32), (32, 64), (64, 128))):
+            x = 32 + 3 * qh + k
+            ts(PF(x, 96), PF(16, 96), 9.0 * Q + 16 * qh, PF(10, 96) if k < 2 else 0.0, ALU.mult, (ALU.subtract, ALU.add, ALU.add)[k],
+               ["F16", "F10"], ["F%d" % x])
+            act(T.AT[96:128, 128 * qh + a:128 * qh + b], T.ID[96:128, 0:b - a], ["ID", "F%d" % x], ["A%d_%d" % (qh, k)], bias=PF(x, 96))
+    act(T.FQ[0:96, :], T.ID[0:96, 0:96], ["ID"], ["FQ"], 96, scale=16.0)
+    act(PF(22, 96), PF(16, 96), ["F16"], ["F22"], scale=-120.0)
+    act(T.FQ[96:128, :], T.ID[96:128, 0:96], ["ID", "F22"], ["FQc"], 96, bias=PF(22, 96))
     for m in range(2):
-        ts(PF(12 + m), PF(3), float(2 * rho + m), None, ALU.is_equal, None, ["F1"], ["F9%d" % m])
-        ts(T.SO[:, m:m + 1], PF(12 + m), -1.0, None, ALU.mult, None, ["F9%d" % m], ["SO%d" % m])
-        ts(T.SM[:, blk(m, 96)], T.JJ[:, 0:96], PF(7), PF(12 + m), ALU.is_equal, ALU.mult, ["JJ", "F4", "F9%d" % m], ["SM%d" % m], 96)
-    ts(T.RP[0:32, :], T.JJ[0:32, :], PF(1, 0, 32), None, ALU.is_equal, None, ["JJ", "F1"], ["RP"], 128)
-    ts(PF(25), PF(12), PF(13), None, ALU.add, None, ["F90", "F91"], ["F25"])
-    ts(T.RN[:], T.JK[:], PF(24), PF(25), ALU.is_equal, ALU.mult, ["JK", "F24", "F25"], ["RN"])
+        mask = T.MK[:, 2 * rho + m:2 * rho + m + 1]
+        act(T.SO[:, m:m + 1], mask, ["MK"], ["SO%d" % m], scale=-1.0)
+        ts(T.SM[:, blk(m, 96)], T.JJ[:, 0:96], PF(7), mask, ALU.is_equal, ALU.mult, ["JJ", "F4", "MK"], ["SM%d" % m], 96)
+        ts(T.SM[:, blk(2 + m, 96)], T.JJ[:, 0:96], PF(27), T.MK[:, 6 + m:7 + m], ALU.is_equal, ALU.mult, ["JJ", "F27", "MK"], ["SM%d" % (2 + m)], 96)
+    ts(T.RP[:], T.JJ[:], PF(7), None, ALU.is_equal, None, ["JJ", "F4"], ["RP"], 128)
+    for k, r in enumerate(peers + [rho]):
+        act(PF(28 + k), T.MK[:, 2 * r:2 * r + 1], ["MK"], ["F28%d" % k], bias=T.MK[:, 2 * r + 1:2 * r + 2])
+        ts(T.IP[:, blk(k, 36)], T.JK[:], PF(24), PF(28 + k), ALU.is_equal, ALU.mult, ["JK", "F24", "F28%d" % k], ["IP%d" % k])
+    ts(T.BO[:], T.JG[:], PF(3), -1.0, ALU.is_equal, ALU.mult, ["JG", "F1"], ["BO"], 128)
+    ts(T.DM[:], T.JL[:], PF(2), None, ALU.is_equal, None, ["JL", "F1"], ["DM"], 96)
+    ts(T.SK[:], T.JL[:], 0.0, None, ALU.not_equal, None, ["JL"], ["SK"], 96)
+    ms(T.WS[:, 32:36], 0.0, ["WSz"])
+    ms(T.WA[:], 0.0, ["WA%d" % r for r in range(N)], 128)
     ts(T.SG[:], T.JJ[:], PF(1), PF(9), ALU.is_equal, ALU.mult, ["JJ", "F1"] + F6, ["SG"], 128)
     ts(T.SR[:], T.JK[:], PF(24), 512.0, ALU.is_equal, ALU.mult, ["JK", "F24"], ["SR"])
     for k in (NB, NB + 1):
         ms(T["M%d" % k][:], 0.0, ["M%d" % k] + ["L%d_%d%d" % (k, c, m) for c in range(NC) for m in range(2)])
+    ms(T.E[0:64, :], 0.0, ["E%d_%d_0" % (c, t) for c in range(NC) for t in range(RO + 1)])
+    ms(T.E[64:128, :], 1.0, ["Ec"] + ["E%d_%d_1" % (c, t) for c in range(NC) for t in range(RO + 1)])
+    ts(T.KS[64:128, :], T.JJ[64:128, 0:96], PF(15, 64), PF(16, 64), ALU.is_equal, ALU.max, ["JJ", "F15", "F16"], ["KSc"], 96)
+    ts(T.NR0[0:64, :], T.JK[0:64, :], PF(24, 0, 64), PF(14, 0, 64), ALU.is_equal, ALU.mult, ["JK", "F24", "F11a", "F11b"], ["NRa0"])
+    for m in range(2):
+        ts(T.NR0[96:128, 18 * m:18 * m + 16], T.JK[96:128, 0:16], -32.0, 472.0, ALU.mult, ALU.add, ["JK"], ["NRb%d" % m])
+        ms(T.NR0[96:128, 18 * m + 16:18 * m + 18], LOW, ["NRc%d" % m])
     for c in range(NC):
         s = str(c)
-        E, NR = T["E" + s], T["NR" + s]
-        ms(E[0:64, :], 0.0, ["E%d_%d_0" % (c, t) for t in range(RO + 1)])
-        ms(E[64:128, :], 1.0, ["Ec" + s] + ["E%d_%d_1" % (c, t) for t in range(RO + 1)])
-        ms(T["DL" + s][0:Q, :], 0.0, ["DL%s_%d%d" % (s, t, m) for t in range(1, RO + 1) for m in range(2)], 36 * RO)
-        ts(NR[0:64, :], T.JK[0:64, :], PF(24, 0, 64), PF(14, 0, 64), ALU.is_equal, ALU.mult, ["JK", "F24", "F11a", "F11b"], ["NRa" + s])
-        for m in range(2):
-            ts(NR[96:128, blk(m, 18)], T.JK[96:128, 0:18], -32.0, 472.0, ALU.mult, ALU.add, ["JK"], ["NRb" + s])
-            ms(NR[96:128, 18 * m + 16:18 * m + 18], LOW, ["NRb" + s])
-        ts(T.KS[64:128, blk(c, Q)], T.J128[64:128, 0:Q], PF(15, 64), PF(16, 64), ALU.is_equal, ALU.max, ["J128", "F15", "F16"], ["KSc" + s])
+        if c:
+            act(T["NR" + s][0:64, :], T.NR0[0:64, :], ["NRa0"], ["NRa" + s])
+            act(T["NR" + s][96:128, :], T.NR0[96:128, :], ["NRb0", "NRb1", "NRc0", "NRc1"], ["NRd" + s])
+        for k in range(2):
+            ms(T["DL" + s][0:Q, 16 + k::18], 0.0, ["DLz%s%d" % (s, k)])
         ms(T.VN[:, VS * c + VW:VS * c + VS], 0.0, ["Vj" + s], VW)
     Vall = ["V%d" % c for c in range(NC)] + ["Vj%d" % c for c in range(NC)]
     ts(T.SU2[0:32, :], T.SU[0:32, :], 7, None, ALU.arith_shift_right, None, ["SUa"], ["S2a"], 96)
@@ -306,18 +314,82 @@ def build(g, core, T, topo):
     ts(T.IU[:], T.I3[:], PF(11), None, ALU.add, None, ["I3", "F8"], ["IU"])
     for c in range(NC):
         s, f = str(c), (act, cp, act)[c]
-        mm(T["pH" + s][:], T.RP[0:32, :], T.VO[0:32, blk(c, VW)], True, True, ["RP", "VO"], ["pH" + s], 128, VW)
-        f(T.VR[:, blk(c, VW)], T["pH" + s][:], ["pH" + s], ["VR" + s], VW)
-        f(T["X" + s][:], T.VR[:, blk(c, VW)].indirect(T.IU[:]), ["VR" + s, "IU"], ["X" + s], dur=ga(ROWS * Q))
-    for r in [rho, rnear] + rfar:
-        src, nm = (T.WS[:], "WS") if r == rho else (T.WA[:, blk(r)], "WA%d" % r)
-        for m in range(2):
-            mm(T.pY[0:96, blk(2 * r + m)], T.SM[:, blk(m, 96)], src, True, True, ["SM%d" % m, nm], ["pY"], 96, 32)
-    act(T.WK[0:96, 0:256], T.pY[0:96, 0:256], ["pY"] + F6, ["WK"], 256, scale=PF(9, 0, 96))
-    ts(T.WK[0:96, 256:512], T.pY[0:96, 0:256], PF(9, 0, 96), -1.0, ALU.mult, ALU.mult, ["pY"] + F6, ["WN"], 256)
+        mm(T["pK" + s][:], T.RP[:], T.VN[:, VS * c:VS * c + VW], True, True, ["RP", "V" + s], ["pK" + s], 128, VW)
+        f(T.VR[:, blk(c, VW)], T["pK" + s][:], ["pK" + s], ["VR" + s], VW)
 
-    def const(out, k, n, st, sp, bk):
-        mm(out, T.ON[0:1, blk(2 + k, 128)], T.CK[0:1, 0:n], st, sp, ["ONc", "CK"], [bk], 128, n)
+    def places(O, W, p, n, rd, bk, nO):
+        K, h = p.shape[0], T[bk][:, 0:2 * n]
+
+        def const(k, st, sp):
+            mm(h, T.ON[0:1, blk(2 + k, 128)], T.CK[0:1, 0:2 * n], st, sp, ["ON%d" % (2 + k), "CK"], [bk], 128, 2 * n)
+        retag("z")
+        const(0, True, False)
+        retag("pH")
+        for eh in range(2):
+            mm(T[bk][:, blk(eh, n)], W[0:K, 256 + eh:512:2], p, False, False, rd, [bk], 128, n)
+        const(1, False, False)
+        const(2, False, False)
+        for eh in range(2):
+            mm(T[bk][:, blk(eh, n)], W[0:K, eh:256:2], p, False, False, rd, [bk], 128, n)
+        const(3, False, True)
+        retag("O")
+        ts(O, h, 4095.0, None, ALU.min, None, [bk], [nO], 2 * n)
+
+    mm(T.pY[:, 0:96], T.ON[0:1, 0:128], T.CW[0:1, 216:312], True, False, ["ON0", "BR"], ["pY"], 128, 96)
+    mm(T.pY[:, 0:96], T.BO[:], T.CA[:], False, False, ["BO", "CA"], ["pY"], 128, 96)
+    mm(T.pY[:, 0:96], T.BO[:], T.CB[:], False, True, ["BO", "CB"], ["pY"], 128, 96)
+    tt(T.XD[:], T.pY[:, 0:96], T.DM[:], ALU.mult, ["pY", "DM"], ["XD"], 96)
+    add("dve", lambda: V_.tensor_tensor_scan(T.XS[:], T.SK[:], T.XD[:], 0.0, ALU.mult, ALU.add), ["SK", "XD"], ["XS"], vcost(96))
+    ts(T.L1[:], T.XS[:, 15::16], 8.0, None, ALU.add, None, ["XS"], ["L1"])
+    cp(T.P1[:], T.VN[:].indirect(T.L1[:]), Vall + ["L1"], ["P1"], dur=ga(96))
+    for k in range(8):
+        act(T.WO[:, blk(k)], T.WS[:, 0:32], ["WS", "MK"], ["WO%d" % k], scale=T.MK[:, k:k + 1])
+    act(T.WO[:, 256:512], T.WO[:, 0:256], ["WO%d" % k for k in range(8)], ["WO"], 256, scale=-1.0)
+    places(T.OW[:], T.WO, T.P1[:], 96, ["WO", "P1"], "pH0", "OW")
+    Gn = lambda a, b: ["G%d_%d" % (x // (2 * Q), x % (2 * Q)) for x in range(a, b, 2)]
+    for nm, a, b in PIECES_ONE:
+        (cp if nm[0] == "g" else act)(T.G[:, 16 * a:16 * b], T.TB[:].indirect(T.OW[:, a:b]), TBall + ["OW"], Gn(a, b), dur=ga(16 * (b - a)))
+    for k in range(3):
+        bk = "pH%d" % (1 + k // 2)
+        mm(T[bk][96:128, blk(k % 2, 36)], T.ID[:, blk(peers[k])], T.WS[:], True, True, ["ID", "WS", "WSz"], [bk], 32, 36)
+    for eh in range(2):
+        for h in range(2):
+            for el in range(16):
+                mm(T["pH%d" % (1 + h)][0:96, 0:72], T.G[:, 1536 * eh + el:1536 * eh + 1536:16], T.IP[:, blk(h, 72)],
+                   eh == 0 and el == 0, eh == 1 and el == 15, ["IP%d" % (2 * h), "IP%d" % (2 * h + 1)] + Gn(96 * eh, 96 * eh + 96),
+                   ["pH%d" % (1 + h)], 96, 72)
+    cp(T.MS[:, 0:72], T.pH1[:, 0:72], ["pH1"], ["MSf"], 72)
+    cp(T.MS[:, 72:108], T.pH2[:, 0:36], ["pH2"], ["MSn"])
+    cp(T.LF[0:96, blk(rho, 36)], T.pH2[0:96, 36:72], ["pH2"], ["LF%d" % rho])
+    for ps, nm, lat in ((far, "MSf", LZ[0]), (near, "MSn", LZ[1])):
+        send("z", ps, lambda r: T.MS[:, blk(peers.index(r), 36)], T.LP[:, 40 * rho:40 * rho + 36], [nm], lambda r: "LP%d" % r, lat)
+    for j in range(LATE, len(CUT)):
+        piece(j)
+    u4 = 64 // Q
+    for ty, (st, b) in enumerate(((u4, 38), (-64, -34 * Q), (u4, 30))):
+        iota(T.CW[0:1, blk(ty, 18)], [[0, 18 // QH], [st, QH]], b, 0, ["CW"], 18, True)
+    iota(T.CW[0:1, 54:108], [[4, 3], [0, 18 // QH], [-u4, QH]], -8, 0, ["CW"], 54, True)
+    iota(T.CW[0:1, 108:162], [[0, 54 // QH], [16, QH]], 0, 0, ["CW"], 54, True)
+    iota(T.CW[0:1, 162:216], [[0, 54]], 1, 0, ["CW"], 54, True)
+    iota(T.CW[0:1, 180:198], [[0, 18]], Q, 0, ["CW"], 18, True)
+    for c in range(NC):
+        s = str(c)
+        (act, cp, act)[c](T["X" + s][:], T.VR[:, blk(c, VW)].indirect(T.IU[:]), ["VR" + s, "IU"] + (["MSf", "MSn", "LF%d" % rho] if c == 1 else Gn(0, 192)), ["X" + s], dur=ga(ROWS * Q))
+    for j, (k, a, b) in enumerate(CUT):
+        r = peers[k]
+        for x in range(4):
+            f, n = (act, b - a) if x < ACTC[j] else (cp, (b - a) // 2)
+            f(T.TB[blk(r), 1024 * x + a:1024 * x + b], T.LD[blk(x), 1024 * r + a:1024 * r + b], ["LD%d" % j], ["TB%d_%d" % (j, x)], n)
+    for r in [rho, rnear] + rfar:
+        src, nm, a = T.WS[:, 0:32], "WS", 0
+        if r != rho:
+            cp(T.LF[:, blk(r, 36)], T.LP[:, 40 * r:40 * r + 36], ["LP%d" % r], ["LF%d" % r])
+            cp(T.WA[96:128, blk(r)], T.LF[96:128, 36 * r:36 * r + 32], ["LF%d" % r], ["WA%d" % r])
+            src, nm, a = T.WA[:, blk(r)], "WA%d" % r, 2
+        for m in range(2):
+            mm(T.pY[0:96, blk(2 * r + m)], T.SM[:, blk(a + m, 96)], src, True, True, ["SM%d" % (a + m), nm], ["pY"], 96, 32)
+    ts(T.WK[0:96, 256:512], T.pY[0:96, 0:256], PF(26, 0, 96), None, ALU.mult, None, ["pY", "F26"], ["WN"], 256)
+    ts(T.WK[0:96, 0:256], T.pY[0:96, 0:256], PF(9, 0, 96), None, ALU.mult, None, ["pY"] + F6, ["WK"], 256)
 
     def B(n, c):
         return T["%s%d" % (n, c)]
@@ -327,7 +399,9 @@ def build(g, core, T, topo):
 
         def tag(nm):
             cur[0] = (nm, NC * t + c) if t else None
-        E, X, SC, DL, OG, NR = B("E", c), B("X", c), B("SC", c), B("DL", c), B("OG", c), B("NR", c)
+        X, SC, DL, OG, NR = B("X", c), B("SC", c), B("DL", c), B("OG", c), B("NR", c)
+        E = lambda p, u: T.E[p, 8 * c + u:8 * c + u + 1]
+        NRn = ["NRa" + s, "N" + s] + (["NRd" + s] if c else ["NRb0", "NRb1", "NRc0", "NRc1"])
         pK, pH = B("pK", c), B("pH", c)
         En = lambda u: ["E%d_%d_%d" % (c, u, m) for m in range(2)]
         mk = lambda m: slice(64 * m, 64 * m + Q)
@@ -337,22 +411,25 @@ def build(g, core, T, topo):
         def changes(out, bk, upto, sp):
             for u in range(1, upto + 1):
                 mm(out, T.ID[0:Q, 0:Q], DL[0:Q, blk(u - 1, 36)], False, sp and u == upto,
-                   ["ID", "DL%s_%d0" % (s, u), "DL%s_%d1" % (s, u)], [bk], Q, 36)
+                   ["ID", "DLz%s0" % s, "DLz%s1" % s, "DL%s_%d0" % (s, u), "DL%s_%d1" % (s, u)], [bk], Q, 36)
         if t == 0:
-            mm(key, T.CN[:, blk(c, Q)], T.RN[:], True, True, ["CN", "RN"], ["pK" + s], Q, 36)
+            mm(key, T.CN[:, blk(c, Q)], T.IP[:, blk(3, 36)], True, True, ["CN", "IP3"], ["pK" + s], Q, 36)
             mm(pK[0:Q, 64:66], T.CN[:, blk(c, Q)], T.SO[:], True, True, ["CN", "SO0", "SO1"], ["pK" + s], Q, 2)
             for m in range(2):
-                act(E[mk(m), 0:1], pK[0:Q, 64 + m:65 + m], ["pK" + s], [En(0)[m]])
+                act(E(mk(m), 0), pK[0:Q, 64 + m:65 + m], ["pK" + s], [En(0)[m]])
             act(NR[mk(1), :], key, ["pK" + s], ["N" + s], bias=8.0)
         else:
-            for nm, a, b in PIECES_END if (t == 1 and c == 0) or (t == RO and c == NC - 1) else PIECES:
+            for nm, a, b in [] if t == 1 else PIECES_END if (t == 2 and c == 0) or (t == RO and c == NC - 1) else PIECES:
                 tag(nm)
                 (cp if nm[0] == "g" else act)(T.G[:, g0 + 16 * a:g0 + 16 * b], T.TB[:].indirect(B("O", c)[:, a:b]),
                                               TBall + ["O" + s], ["G%s_%d" % (s, x) for x in range(a, b, 2)], dur=ga(16 * (b - a)))
             tag("k0")
-            mm(key, T.KS[0:113, blk(c, Q)], NR[0:113, :], True, False, ["KS", "KSc" + s, "NRa" + s, "NRb" + s, "N" + s], ["pK" + s], Q, 36)
+            mm(key, T.KS[0:113, blk(c, Q)], NR[0:113, :], True, False, ["KS", "KSc"] + NRn, ["pK" + s], Q, 36)
             changes(key, "pK" + s, t - 1, False)
-            for eh in range(2):
+            for r in [rho, rnear] + rfar if t == 1 else []:
+                tag("k4")
+                mm(key, T.SEL[0:96, blk(c, Q)], T.LF[0:96, blk(r, 36)], False, r == rfar[-1], ["SEL", "LF%d" % r], ["pK" + s], Q, 144)
+            for eh in range(2 if t > 1 else 0):
                 a = g0 + 16 * Q * eh
                 for el in range(16):
                     tag("k%d" % (2 * eh + el // 8 + 1))
@@ -360,17 +437,17 @@ def build(g, core, T, topo):
                        ["SR"] + ["G%s_%d" % (s, x) for x in range(Q * eh, Q * eh + Q, 2)], ["pK" + s], Q, 36)
             tag("SC")
             add("dve", lambda: V_.tensor_tensor_scan(SC[0:Q, :], T.RZ[0:Q, :], key, LOW, ALU.add, ALU.max),
-                ["RZ", "pK" + s], ["SC" + s], vcost(36))
+                ["RZ0", "RZ1", "RZ2", "pK" + s], ["SC" + s], vcost(36))
             tag("E")
             for m in range(2):
-                ts(E[mk(m), t:t + 1], SC[0:Q, 18 * m + 15:18 * m + 16], SC[0:Q, 18 * m + 17:18 * m + 18],
+                ts(E(mk(m), t), SC[0:Q, 18 * m + 15:18 * m + 16], SC[0:Q, 18 * m + 17:18 * m + 18],
                    -8.0 if t == 1 else pK[mk(m), 65:66], ALU.subtract, ALU.max, ["SC" + s, "pK" + s], [En(t)[m]])
 
         def rows(out, a, K, bk):
             for qh in range(QH):
-                mm(out[:, a + qh:a + qh + 1], T.AT[0:K, blk(qh, 128)], E[0:K, t:t + 1], True, True,
-                   ["A%d" % qh, "Ec" + s] + En(t), [bk], 128, 1)
-        if t < RO:
+                mm(out[:, a + qh:a + qh + 1], T.AT[0:K, blk(qh, 128)], E(slice(0, K), t), True, True,
+                   ["A%d" % qh, "Ec"] + ["A%d_%d" % (qh, k) for k in range(3)] + En(t), [bk], 128, 1)
+        if 0 < t < RO:
             tag("pT")
             rows(pK, 72, 113, "pK" + s)
             if t < RO - 1:
@@ -382,10 +459,10 @@ def build(g, core, T, topo):
             tag("H")
             rows(T.pT, 6 * (t - 1) + QH * c, 113, "pT")
             tag("D")
-            mm(pK[0:96, 64:65], T.ID[0:96, 0:96], E[0:96, t - 1:t], True, False, ["ID"] + En(t - 1), ["pK" + s], 96, 1)
-            mm(pK[0:96, 64:65], T.NI[0:96, 0:96], E[0:96, t:t + 1], False, True, ["NI"] + En(t), ["pK" + s], 96, 1)
+            mm(pK[0:96, 64:65], T.ID[0:96, 0:96], E(slice(0, 96), t - 1), True, False, ["ID"] + En(t - 1), ["pK" + s], 96, 1)
+            mm(pK[0:96, 64:65], T.NI[0:96, 0:96], E(slice(0, 96), t), False, True, ["NI"] + En(t), ["pK" + s], 96, 1)
             if t < RO:
-                mm(pK[0:96, 65:66], T.FQ[0:113, :], E[0:113, t:t + 1], True, True, ["FQ", "Ec" + s] + En(t), ["pK" + s], 96, 1)
+                mm(pK[0:96, 65:66], T.FQ[0:113, :], E(slice(0, 113), t), True, True, ["FQ", "FQc", "Ec"] + En(t), ["pK" + s], 96, 1)
             tag("DL")
             lab = lambda k, m: (B("M", k)[blk(c), 8 + 16 * m:24 + 16 * m], "L%d_%d%d" % (k, c, m))
             for m in range(2):
@@ -393,30 +470,19 @@ def build(g, core, T, topo):
                 out, nm = (DL[0:Q, a:a + 16], "DL%s_%d%d" % (s, t, m)) if t < RO else lab(NB + 1, m)
                 ts(out, pK[0:Q, gd(m)], SC[0:Q, 18 * m + 15:18 * m + 16], pK[mk(m), 64:65],
                    ALU.is_equal, ALU.mult, ["pK" + s, "SC" + s], [nm])
-        if t == RO and c >= NC - 2:
+        if t == RO and c in (0, NC - 1):
             tag("M")
-            k, a = (NB, 0) if c == NC - 2 else (NB + 1, QH * c)
-            act(B("M", k)[:, 0:QH * (c + 1) - a], T.pT[:, 30 + a:30 + QH * (c + 1)], ["pT"], ["M%d" % k], scale=1.0 / Q)
-        if t < RO:
+            k, a, b = (NB, 24, 30 + QH) if c == 0 else (NB + 1, 30 + QH, 36)
+            act(B("M", k)[:, 0:b - a], T.pT[:, a:b], ["pT"], ["M%d" % k], scale=1.0 / Q)
+        if 0 < t < RO:
             Xr = ["X" + s, "Xa" + s, "Xb" + s]
             tag("G3")
-            cp(B("G3", c)[:], X[:].indirect(OG[:, blk(0 if t else 1, QH)]), Xr + ["OG" + s], ["G3" + s], dur=ga(Q))
-            g3, rd, h = B("G3", c)[0:96, :], ["WK", "WN", "G3" + s], pH[:, 0:2 * Q]
-            tag("z")
-            const(h, 0, 2 * Q, True, False, "pH" + s)
-            tag("pH")
-            for eh in range(2):
-                mm(pH[:, blk(eh, Q)], T.WK[0:96, 256 + eh:512:2], g3, False, False, rd, ["pH" + s], 128, Q)
-            const(h, 1, 2 * Q, False, False, "pH" + s)
-            const(h, 2, 2 * Q, False, False, "pH" + s)
-            for eh in range(2):
-                mm(pH[:, blk(eh, Q)], T.WK[0:96, eh:256:2], g3, False, False, rd, ["pH" + s], 128, Q)
-            const(h, 3, 2 * Q, False, True, "pH" + s)
-            tag("O")
-            ts(B("O", c)[:], h, 4095.0, None, ALU.min, None, ["pH" + s], ["O" + s], 2 * Q)
+            cp(B("G3", c)[:], X[:].indirect(OG[:, 0:QH]), Xr + ["OG" + s], ["G3" + s], dur=ga(Q))
+            g3 = B("G3", c)[0:96, :]
+            places(B("O", c)[:], T.WK, g3, Q, ["WK", "WN", "G3" + s], "pH" + s, "O" + s)
         if t == RO - 1:
             tag("N")
-            mm(pH[blk(c), 256:292], T.ID[:, 64:64 + Q], NR[:], True, False, ["ID", "NRa" + s, "NRb" + s, "N" + s], ["pH" + s], Q, 36)
+            mm(pH[blk(c), 256:292], T.ID[:, 64:64 + Q], NR[:], True, False, ["ID"] + NRn, ["pH" + s], Q, 36)
             changes(pH[blk(c), 256:292], "pH" + s, RO - 1, True)
             for m in range(2):
                 act(lab(NB, m)[0], pH[blk(c), 256 + 18 * m:272 + 18 * m], ["pH" + s], [lab(NB, m)[1]])
@@ -434,12 +500,13 @@ def build(g, core, T, topo):
     def publish(k, w, r):
         send("o%d" % k, far + near, lambda _: B("M", k)[:, 0:w], B("R", k)[:, blk(rho, w)], r, lambda x: "R%d%d" % (k, x), LB[k])
 
-    def replay(k, n, ws, c0, c1):
-        w, co, base, bk = n * QH * (c1 - c0), QH * c0, VS * c0, "pY" if c0 == 0 else "pT"
+    def offsets(k, w, ws, co):
+        bk = "pT" if co else "pY"
         Y, DU = T[bk], B("DU", k)
+        cur[0] = "replay" if k < NB else None
 
         def row(a, b, st, sp):
-            mm(Y[:, 0:54], T.ON[0:1, blk(a, 128)], T.CW[0:1, blk(b, 54)], st, sp, ["ONa", "CW"], [bk], 128, 54)
+            mm(Y[:, 0:54], T.ON[0:1, blk(a, 128)], T.CW[0:1, blk(b, 54)], st, sp, ["ON%d" % a, "CW"], [bk], 128, 54)
 
         def slots(lhs):
             for r in [rho, rnear] + rfar:
@@ -453,40 +520,49 @@ def build(g, core, T, topo):
         slots(("ID", "ID", "ID"))
         row(0, 1, False, False)
         row(1, 2, False, True)
-        ts(DU[:], Y[:, 0:54], PF(11), -float(base), ALU.add, ALU.add, [bk, "F8"], ["DU%d" % k])
-        V = T.VN[:, VS * c0:VS * c1]
-        Vn = ["V%d" % x for x in range(c0, c1)] + ["Vj%d" % x for x in range(c0, c1)]
-        a, b = Q * c0, Q * c1
-        nm = lambda x: [x + str(y) for y in range(c0, c1)]
-        o = lambda ty, u: DU[:, 18 * ty + 6 * u + co:18 * ty + 6 * u + QH * c1]
-        rd = Vn + ["DU%d" % k]
+        ts(DU[:], Y[:, 0:54], PF(11), None, ALU.add, None, [bk, "F8"], ["DU%d" % k])
+        cur[0] = None
 
-        def old(u):
-            act(B("RA", u % 2)[:, a:b], V.indirect(o(1, u)), rd, nm("RA%d" % (u % 2)), dur=ga(b - a))
+    def replay(steps, c):
+        V, Vn = T.VN[:, blk(c, VS)], ["V%d" % c, "Vj%d" % c]
+        a, b = Q * c, Q * c + Q
+        nm = lambda x: [x + str(c)]
+        o = lambda ty, j: B("DU", steps[j][0])[:, blk(9 * ty + 3 * steps[j][1] + c, QH)]
+        rd = lambda j: Vn + ["DU%d" % steps[j][0]]
+
+        def old(j):
+            act(B("RA", j % 2)[:, a:b], V.indirect(o(1, j)), rd(j), nm("RA%d" % (j % 2)), dur=ga(b - a))
         old(0)
-        for u in range(n):
-            (act if u else cp)(T.RC[:, a:b], V.indirect(o(2, u)), rd, nm("RC"), dur=ga(b - a))
-            tt(T.RB[:, a:b], V.indirect(o(0, u)), B("RA", u % 2)[:, a:b], ALU.subtract, rd + nm("RA%d" % (u % 2)), nm("RB"), dur=ga(b - a))
-            if u + 1 < n:
-                old(u + 1)
-            tt(V.indirect(o(1, u)), T.RB[:, a:b], T.RC[:, a:b], ALU.add, nm("RB") + nm("RC") + ["DU%d" % k], Vn, dur=sc(b - a))
+        for j in range(len(steps)):
+            (act if j else cp)(T.RC[:, a:b], V.indirect(o(2, j)), rd(j), nm("RC"), dur=ga(b - a))
+            tt(T.RB[:, a:b], V.indirect(o(0, j)), B("RA", j % 2)[:, a:b], ALU.subtract, rd(j) + nm("RA%d" % (j % 2)), nm("RB"), dur=ga(b - a))
+            if j + 1 < len(steps):
+                old(j + 1)
+            tt(V.indirect(o(1, j)), T.RB[:, a:b], T.RC[:, a:b], ALU.add, nm("RB") + nm("RC") + rd(j), Vn, dur=sc(b - a))
 
     for t in range(RO + 1):
         for c in range(NC):
             step(c, t)
-            if t == RO and c >= NC - 2:
-                k = NB + c - NC + 2
+            if t == RO and c in (0, NC - 1):
+                k = NB + (c > 0)
                 publish(k, 40, ["M%d" % k] + ["L%d_%d%d" % (k, x, m) for x in range(NC) for m in range(2)])
         for k, (t0, n) in enumerate(BATCH):
             if t == t0 + n - 1:
+                cur[0] = ("M", NC * t + NC - 1)
                 act(B("M", k)[:, 0:6 * n], T.pT[:, 6 * t0 - 6:6 * (t0 + n) - 6], ["pT"], ["M%d" % k], scale=1.0 / Q)
+                cur[0] = None
                 publish(k, 6 * n, ["M%d" % k])
     for k, (t0, n) in enumerate(BATCH):
-        replay(k, n, 6 * n, 0, NC)
-    for k, c0, c1 in ((NB, 0, NC - 1), (NB + 1, NC - 1, NC)):
-        replay(k, 1, 40, c0, c1)
-        for c in range(c0, c1):
-            dma("sync", T.yv[:, blk(c, VW)], T.VN[:, VS * c:VS * c + VW], ["V%d" % c], [], 256 * VW)
+        offsets(k, 6 * n, 6 * n, 0)
+    offsets(NB, 6 + QH, 40, 0)
+    for c in range(NC):
+        replay([(k, u) for k, (t0, n) in enumerate(BATCH) for u in range(n)], c)
+        replay([(NB, 0)] + [(NB, 1)] * (c == 0), c)
+    offsets(NB + 1, 6 - QH, 40, QH)
+    for c in range(NC):
+        if c:
+            replay([(NB + 1, 0)], c)
+        dma("sync", T.yv[:, blk(c, VW)], T.VN[:, VS * c:VS * c + VW], ["V%d" % c], [], 256 * VW)
     for r in [rho, rnear] + rfar:
         for k in (NB, NB + 1):
             src, nm = B("R", k)[:, 40 * r + 8:40 * r + 40], ["R%d%d" % (k, r)]
@@ -527,7 +603,7 @@ def schedule(ops):
             best = max(best, prio[j] + (o["lat"] + HOP if i in ops[j]["deps"] else 0.0))
         prio[i] = max(best, o["lat"]) + o["dur"]
     for i, o in enumerate(ops):
-        prio[i] -= BIAS * (o["ch"][1] % NC) if o["ch"] else 0.0
+        prio[i] += BIAS if o["ch"] == "replay" else 0.0
     left = [len(o["deps"] | o["order"]) for o in ops]
     ready_at = [0.0] * n
     pool = [i for i in range(n) if left[i] == 0]

@@ -7,30 +7,30 @@ ROWS = 19
 CR = 402653184.0
 LOW = -67108864.0
 VW, VS = 16 * Q, 32 * Q + 16
-CUT = [(0, 0, 128), (0, 128, 1024), (1, 0, 640), (2, 0, 1024), (1, 640, 1024)]
-STAGE = [(0, 0, 128), (0, 128, 1024), (1, 0, 1024), (2, 0, 1024)]
+CUT = [(0, 0, 512), (0, 512, 4096), (1, 0, 1536), (2, 0, 4096), (1, 1536, 3584), (1, 3584, 4096)]
 LATE = 4
 PIECES_ONE = [("A1", 0, 48), ("g1", 48, 96), ("A2", 96, 144), ("g2", 144, 192)]
-PIECES = [("A1", 0, 22), ("g1", 22, 32), ("g2", 32, 42), ("A2", 42, 64)]
+PIECES = [("A1", 0, 24), ("g1", 24, 32), ("g2", 32, 42), ("A2", 42, 64)]
 PIECES_END = [("A1", 0, 16), ("g1", 16, 32), ("g2", 32, 48), ("A2", 48, 64)]
 ROUND = {
-    "dve": [("OG", -2), ("g1", 0), ("G3", -2), ("SC", -1), ("g2", 0), ("E", -1), ("O", -2), ("X", -3), ("DL", -2)],
-    "act": [("A1", 0), ("NV", -3), ("A2", 0), ("M", -2), ("N", -3)],
-    "pe": [("k3", -1), ("k4", -1), ("SG", -3), ("N", -3), ("D", -2), ("H", -2), ("z", -2), ("k0", 0), ("pH", -2), ("k1", 0), ("pT", -1),
-           ("k2", 0)],
+    "dve": [("OS", -3), ("L0", -3), ("OG", -2), ("g1", 0), ("G3", -2), ("DU", 0), ("SC", -1), ("g2", 0), ("E", -1), ("L1", -2), ("O", -2),
+            ("X", -3)],
+    "act": [("A2", 0), ("M", -2), ("N", -3), ("A1", 1), ("NV", -2)],
+    "pe": [("k3", -1), ("k4", -1), ("SG", -3), ("D", -2), ("N", -3), ("z", -2), ("k0", 0), ("pH", -2), ("k1", 0), ("H", -2),
+           ("dc", 0), ("pT", -1), ("k2", 0)],
 }
 BATCH = [(1, 2), (3, 2)]
-NB = len(BATCH)
-LB = [4000.0, 4000.0, 3200.0, 3500.0]
-HOP, WIN, YF, BIAS = 210.0, 60.0, 8, 1000.0
+NB, FIRST = len(BATCH), 14
+LB = [4000.0, 4000.0, 2800.0, 2800.0]
+HOP, WIN, YF, BIAS = 210.0, 60.0, 8, 2000.0
 GAM, SIG, CYC, PEC = 1.35, 3.3, 0.86, 0.47
-LAT, RATE = 1200.0, 400.0
-LZ, LF = [3800.0, 3000.0], [5000.0, 5000.0, 5500.0, 4500.0, 4500.0]
-ACTC = [1, 2, 2, 1, 2]
+LAT, RATE = 1200.0, 450.0
+LZ, LF = [3300.0, 3000.0], [5000.0, 5000.0, 5000.0, 4500.0, 3200.0, 3300.0]
+ACTC = [0, 0, 4, 0, 2, 1]
 
 SCRATCH = {}
 for _d, _l in (("bfloat16", "TB 4096 SB 3072 LD 4096 VN 3120 VR 1536 G 3072 RP 128 IP 144 WS 36 WA 128 WK 512 WO 512 KS 96 CA 96 CB 96 CN 96 "
-                            "AT 256 SM 384 SG 128 SR 36 ID 128 NI 128 IS 128 BO 128 DM 96 P1 96 FQ 96 E 24 SO 2 ON 1024 CK 192 CW 312 "
+                            "AT 256 SM 384 SG 128 SR 36 ID 128 NI 128 IS 128 BO 128 DM 96 P1 288 FQ 96 E 24 SO 2 ON 1024 CK 192 CW 312 "
                             "RA0 96 RA1 96 RB 96 RC 96 M0 18 M1 18 M2 40 M3 40 R0 72 R1 72 R2 160 R3 160"),
                ("int32", "IV 96 SU 96 SU2 96 PI 1 PJ 6 I1 38 I2 38 I3 38 J128 128 JK 36 JJ 128 JL 96 JG 128"),
                ("float32", "CAP 96 YI 96 PF 40 JX 128 RZ 36 MK 8 SK 96 XD 96 XS 96 SEL 96 LF 144"),
@@ -40,7 +40,7 @@ for _d, _l in (("bfloat16", "TB 4096 SB 3072 LD 4096 VN 3120 VR 1536 G 3072 RP 1
         SCRATCH[_l[_k]] = ("sbuf", [128, int(_l[_k + 1])], _d)
 for _c in range(NC):
     for _n, _s, _d in (("X", ROWS * Q, "bfloat16"), ("O", 2 * Q, "uint16"), ("OG", 2 * QH, "uint16"),
-                       ("G3", Q, "bfloat16"), ("NV", Q, "bfloat16"),
+                       ("G3", 3 * Q, "bfloat16"), ("NV", Q, "bfloat16"),
                        ("SC", 36, "float32"), ("DL", 36 * RO, "bfloat16"), ("NR", 36, "bfloat16")):
         SCRATCH["%s%d" % (_n, _c)] = ("sbuf", [128, _s], _d)
 for _n in ("pK0", "pK1", "pK2", "pH0", "pH1", "pH2", "pT", "pY"):
@@ -191,25 +191,29 @@ def build(g, core, T, topo):
     peers = [rk[c] for c in order]
     TBall = ["TB%d_%d" % (j, x) for j in range(len(CUT)) for x in range(4)] + ["TBo"]
 
-    def stage(k, a, b):
-        for x in range(4):
-            dma("act" if (k, a, x % 2) == (0, 0, 1) else "sync", T.SB[blk(x), 1024 * k + a:1024 * k + b], T.dem[blk(peers[k]), 1024 * x + a:1024 * x + b], [],
-                ["SB%d_%d_%d" % (k, a, x)], 64 * (b - a), True)
+
+    def stage(j):
+        k, a, b = CUT[j]
+        if k != 1:
+            dma("sync", T.SB[:, 1024 * k + a // 4:1024 * k + b // 4], T.dem[blk(peers[k]), a:b], [],
+                ["SB%d_%d" % (j, x) for x in range(4)], 64 * (b - a), True)
+        for x in range(4 * (k == 1 and a == 0)):
+            dma("sync", T.SB[blk(x), blk(k, 1024)], T.dem[blk(peers[k]), blk(x, 1024)], [],
+                ["SB%d_%d" % (i, x) for i in range(len(CUT)) if CUT[i][0] == k], 65536, True)
 
     def piece(j):
         k, a, b = CUT[j]
-        send("t%d" % j, [order[k]], lambda r: T.SB[:, 1024 * k + a:1024 * k + b], T.LD[:, 1024 * rho + a:1024 * rho + b],
-             ["SB%d_%d_%d" % (k, lo, x) for kk, lo, hi in STAGE if kk == k and lo <= a < hi for x in range(4)],
-             lambda r: "LD%d" % j, LF[j], alone=k < 2)
+        send("t%d" % j, [order[k]], lambda r: T.SB[:, 1024 * k + a // 4:1024 * k + b // 4], T.LD[:, 1024 * rho + a // 4:1024 * rho + b // 4],
+             ["SB%d_%d" % (j, x) for x in range(4)], lambda r: "LD%d" % j, LF[j], alone=k < 2)
 
-    stage(*STAGE[0])
+    stage(0)
     dma("act", T.IV[:], T.inv[:], [], ["IV"], 49152, True)
     dma("act", T.WS[:, 0:32], T.wt[:], [], ["WS"], 8192, True)
     for c in range(NC):
-        dma("act", T.VN[:, VS * c:VS * c + VW], T.v[:, blk(c, VW)], [], ["V%d" % c], 256 * VW, True)
-    dma("act", T.TB[:], T.dem[:], [], TBall, 1048576, True)
-    for a in STAGE[1:]:
-        stage(*a)
+        dma("sync" if c < 2 else "act", T.VN[:, VS * c:VS * c + VW], T.v[:, blk(c, VW)], [], ["V%d" % c], 256 * VW, True)
+    dma("sync", T.TB[:], T.dem[:], [], TBall, 1048576, True)
+    for j in range(1, len(CUT)):
+        stage(j)
     dma("sync", T.SU[0:32, :], T.sup[blk(rho), :], [], ["SUa"], 12288, True)
     dma("sync", T.SU[32:64, :], T.sup[blk(rho), :], [], ["SUb"], 12288, True)
     iota(T.PI[:], [[0, 1]], 0, 1, ["PI"], 1, False)
@@ -317,8 +321,8 @@ def build(g, core, T, topo):
         mm(T["pK" + s][:], T.RP[:], T.VN[:, VS * c:VS * c + VW], True, True, ["RP", "V" + s], ["pK" + s], 128, VW)
         f(T.VR[:, blk(c, VW)], T["pK" + s][:], ["pK" + s], ["VR" + s], VW)
 
-    def places(O, W, p, n, rd, bk, nO):
-        K, h = p.shape[0], T[bk][:, 0:2 * n]
+    def places(O, W, P, K, n, rd, bk, nO):
+        p, h = P[0:K, n:2 * n], T[bk][:, 0:2 * n]
 
         def const(k, st, sp):
             mm(h, T.ON[0:1, blk(2 + k, 128)], T.CK[0:1, 0:2 * n], st, sp, ["ON%d" % (2 + k), "CK"], [bk], 128, 2 * n)
@@ -330,8 +334,7 @@ def build(g, core, T, topo):
         const(1, False, False)
         const(2, False, False)
         for eh in range(2):
-            mm(T[bk][:, blk(eh, n)], W[0:K, eh:256:2], p, False, False, rd, [bk], 128, n)
-        const(3, False, True)
+            mm(h, W[0:K, eh:256:2], P[0:K, n - n * eh:3 * n - n * eh], False, eh == 1, rd, [bk], 128, 2 * n)
         retag("O")
         ts(O, h, 4095.0, None, ALU.min, None, [bk], [nO], 2 * n)
 
@@ -341,11 +344,14 @@ def build(g, core, T, topo):
     tt(T.XD[:], T.pY[:, 0:96], T.DM[:], ALU.mult, ["pY", "DM"], ["XD"], 96)
     add("dve", lambda: V_.tensor_tensor_scan(T.XS[:], T.SK[:], T.XD[:], 0.0, ALU.mult, ALU.add), ["SK", "XD"], ["XS"], vcost(96))
     ts(T.L1[:], T.XS[:, 15::16], 8.0, None, ALU.add, None, ["XS"], ["L1"])
-    cp(T.P1[:], T.VN[:].indirect(T.L1[:]), Vall + ["L1"], ["P1"], dur=ga(96))
+    ms(T.P1[:, 0:96], 0.0, ["P1a"]); ms(T.P1[:, 192:288], 0.0, ["P1b"])
+    for c in range(NC):
+        ms(T["G3%d" % c][:, 0:Q], 0.0, ["G3a%d" % c]); ms(T["G3%d" % c][:, 2 * Q:3 * Q], 0.0, ["G3b%d" % c])
+    cp(T.P1[:, 96:192], T.VN[:].indirect(T.L1[:]), Vall + ["L1"], ["P1"], dur=ga(96))
     for k in range(8):
         act(T.WO[:, blk(k)], T.WS[:, 0:32], ["WS", "MK"], ["WO%d" % k], scale=T.MK[:, k:k + 1])
     act(T.WO[:, 256:512], T.WO[:, 0:256], ["WO%d" % k for k in range(8)], ["WO"], 256, scale=-1.0)
-    places(T.OW[:], T.WO, T.P1[:], 96, ["WO", "P1"], "pH0", "OW")
+    places(T.OW[:], T.WO, T.P1, 128, 96, ["WO", "P1", "P1a", "P1b"], "pH0", "OW")
     Gn = lambda a, b: ["G%d_%d" % (x // (2 * Q), x % (2 * Q)) for x in range(a, b, 2)]
     for nm, a, b in PIECES_ONE:
         (cp if nm[0] == "g" else act)(T.G[:, 16 * a:16 * b], T.TB[:].indirect(T.OW[:, a:b]), TBall + ["OW"], Gn(a, b), dur=ga(16 * (b - a)))
@@ -376,10 +382,13 @@ def build(g, core, T, topo):
         s = str(c)
         (act, cp, act)[c](T["X" + s][:], T.VR[:, blk(c, VW)].indirect(T.IU[:]), ["VR" + s, "IU"] + (["MSf", "MSn", "LF%d" % rho] if c == 1 else Gn(0, 192)), ["X" + s], dur=ga(ROWS * Q))
     for j, (k, a, b) in enumerate(CUT):
-        r = peers[k]
-        for x in range(4):
-            f, n = (act, b - a) if x < ACTC[j] else (cp, (b - a) // 2)
-            f(T.TB[blk(r), 1024 * x + a:1024 * x + b], T.LD[blk(x), 1024 * r + a:1024 * r + b], ["LD%d" % j], ["TB%d_%d" % (j, x)], n)
+        r, w = peers[k], (b - a) // 4
+        cols = slice(1024 * r + a // 4, 1024 * r + b // 4)
+        if k != 1:
+            dma("sync", T.TB[blk(r), a:b], T.LD[:, cols], ["LD%d" % j], TBall[4 * j:4 * j + 4], 64 * (b - a))
+        for x in range(4 * (k == 1)):
+            f, n = (act, w) if x < ACTC[j] else (cp, w // 2)
+            f(T.TB[blk(r), 1024 * x + a // 4:1024 * x + b // 4], T.LD[blk(x), cols], ["LD%d" % j], ["TB%d_%d" % (j, x)], n)
     for r in [rho, rnear] + rfar:
         src, nm, a = T.WS[:, 0:32], "WS", 0
         if r != rho:
@@ -389,7 +398,7 @@ def build(g, core, T, topo):
         for m in range(2):
             mm(T.pY[0:96, blk(2 * r + m)], T.SM[:, blk(a + m, 96)], src, True, True, ["SM%d" % (a + m), nm], ["pY"], 96, 32)
     ts(T.WK[0:96, 256:512], T.pY[0:96, 0:256], PF(26, 0, 96), None, ALU.mult, None, ["pY", "F26"], ["WN"], 256)
-    ts(T.WK[0:96, 0:256], T.pY[0:96, 0:256], PF(9, 0, 96), None, ALU.mult, None, ["pY"] + F6, ["WK"], 256)
+    act(T.WK[0:96, 0:256], T.WK[0:96, 256:512], ["WN"], ["WK"], 256, scale=-1.0)
 
     def B(n, c):
         return T["%s%d" % (n, c)]
@@ -398,7 +407,7 @@ def build(g, core, T, topo):
         s = str(c)
 
         def tag(nm):
-            cur[0] = (nm, NC * t + c) if t else None
+            cur[0] = (nm, NC * t + c) if t > 1 else None
         X, SC, DL, OG, NR = B("X", c), B("SC", c), B("DL", c), B("OG", c), B("NR", c)
         E = lambda p, u: T.E[p, 8 * c + u:8 * c + u + 1]
         NRn = ["NRa" + s, "N" + s] + (["NRd" + s] if c else ["NRb0", "NRb1", "NRc0", "NRc1"])
@@ -450,11 +459,11 @@ def build(g, core, T, topo):
         if 0 < t < RO:
             tag("pT")
             rows(pK, 72, 113, "pK" + s)
-            if t < RO - 1:
-                rows(pK, 72 + QH, 114, "pK" + s)
             tag("OG")
-            w = 2 * QH if t < RO - 1 else QH
-            ts(OG[:, 0:w], pK[:, 72:72 + w], PF(2), None, ALU.add, None, ["pK" + s, "F1"], ["OG" + s])
+            ts(OG[:, 0:QH], pK[:, 72:72 + QH], PF(2), None, ALU.add, None, ["pK" + s, "F1"], ["OG" + s])
+        if 0 < t < RO - 1:
+            tag("D")
+            rows(pK, 72 + QH, 114, "pK" + s)
         if t > 0:
             tag("H")
             rows(T.pT, 6 * (t - 1) + QH * c, 113, "pT")
@@ -464,8 +473,12 @@ def build(g, core, T, topo):
             if t < RO:
                 mm(pK[0:96, 65:66], T.FQ[0:113, :], E(slice(0, 113), t), True, True, ["FQ", "FQc", "Ec"] + En(t), ["pK" + s], 96, 1)
             tag("DL")
+            if t < RO - 1:
+                tag("OS")
+                ts(OG[:, blk(1, QH)], pK[:, 72 + QH:72 + 2 * QH], PF(2), None, ALU.add, None, ["pK" + s, "F1"], ["OS" + s])
             lab = lambda k, m: (B("M", k)[blk(c), 8 + 16 * m:24 + 16 * m], "L%d_%d%d" % (k, c, m))
             for m in range(2):
+                tag("L%d" % m)
                 a = 36 * (t - 1) + 18 * m
                 out, nm = (DL[0:Q, a:a + 16], "DL%s_%d%d" % (s, t, m)) if t < RO else lab(NB + 1, m)
                 ts(out, pK[0:Q, gd(m)], SC[0:Q, 18 * m + 15:18 * m + 16], pK[mk(m), 64:65],
@@ -477,9 +490,9 @@ def build(g, core, T, topo):
         if 0 < t < RO:
             Xr = ["X" + s, "Xa" + s, "Xb" + s]
             tag("G3")
-            cp(B("G3", c)[:], X[:].indirect(OG[:, 0:QH]), Xr + ["OG" + s], ["G3" + s], dur=ga(Q))
-            g3 = B("G3", c)[0:96, :]
-            places(B("O", c)[:], T.WK, g3, Q, ["WK", "WN", "G3" + s], "pH" + s, "O" + s)
+            cp(B("G3", c)[:, Q:2 * Q], X[:].indirect(OG[:, 0:QH]), Xr + ["OG" + s], ["G3" + s], dur=ga(Q))
+            g3 = B("G3", c)[0:96, Q:2 * Q]
+            places(B("O", c)[:], T.WK, B("G3", c), 96, Q, ["WK", "WN", "G3" + s, "G3a" + s, "G3b" + s], "pH" + s, "O" + s)
         if t == RO - 1:
             tag("N")
             mm(pH[blk(c), 256:292], T.ID[:, 64:64 + Q], NR[:], True, False, ["ID"] + NRn, ["pH" + s], Q, 36)
@@ -492,7 +505,7 @@ def build(g, core, T, topo):
             tag("NV")
             act(B("NV", c)[:], pH[:, 128:128 + Q], ["pH" + s], ["NV" + s], Q)
             tag("X")
-            cp(X[:].indirect(OG[:, blk(1, QH)]), B("NV", c)[:], ["NV" + s, "OG" + s], Xr, dur=sc(Q))
+            cp(X[:].indirect(OG[:, blk(1, QH)]), B("NV", c)[:], ["NV" + s, "OS" + s], Xr, dur=sc(Q))
             gcp(X[0:32, blk(16, Q)], X[0:32, blk(0, Q)], ["X" + s], ["Xa" + s])
             gcp(X[32:64, blk(1, Q)], X[32:64, blk(17, Q)], ["X" + s], ["Xb" + s])
         cur[0] = None
@@ -504,6 +517,7 @@ def build(g, core, T, topo):
         bk = "pT" if co else "pY"
         Y, DU = T[bk], B("DU", k)
         cur[0] = "replay" if k < NB else None
+        i0 = len(ops)
 
         def row(a, b, st, sp):
             mm(Y[:, 0:54], T.ON[0:1, blk(a, 128)], T.CW[0:1, blk(b, 54)], st, sp, ["ON%d" % a, "CW"], [bk], 128, 54)
@@ -520,6 +534,10 @@ def build(g, core, T, topo):
         slots(("ID", "ID", "ID"))
         row(0, 1, False, False)
         row(1, 2, False, True)
+        if k == 0:
+            for i in range(i0, len(ops)):
+                ops[i]["ch"] = ("dc", FIRST + (i - i0) // 8)
+            cur[0] = ("DU", FIRST + 4)
         ts(DU[:], Y[:, 0:54], PF(11), None, ALU.add, None, [bk, "F8"], ["DU%d" % k])
         cur[0] = None
 

from concourse.bass import DstId, RemoteDMATransfer
from concourse.mybir import AluOpType as ALU, AxisListType as AX, ActivationFunctionType as AF

N, Q, NC, RO = 4, 32, 3, 6
QH = Q // 16
ROWS = 19
CR = 402653184.0
LOW = -67108864.0
VW, VS = 16 * Q, 32 * Q + 16
CUT = [(0, 0, 512), (0, 512, 4096), (1, 0, 1536), (2, 0, 4096), (1, 1536, 3584), (1, 3584, 4096)]
LATE = 4
PIECES_ONE = [("A1", 0, 48), ("g1", 48, 96), ("A2", 96, 144), ("g2", 144, 192)]
PIECES = [("A1", 0, 24), ("g1", 24, 32), ("g2", 32, 42), ("A2", 42, 64)]
PIECES_END = [("A1", 0, 16), ("g1", 16, 32), ("g2", 32, 48), ("A2", 48, 64)]
ROUND = {
    "dve": [("OS", -3), ("L0", -3), ("OG", -2), ("g1", 0), ("G3", -2), ("DU", 0), ("SC", -1), ("g2", 0), ("E", -1), ("L1", -2), ("O", -2),
            ("X", -3)],
    "act": [("A2", 0), ("M", -2), ("N", -3), ("A1", 1), ("NV", -2)],
    "pe": [("k3", -1), ("k4", -1), ("SG", -3), ("D", -2), ("N", -3), ("z", -2), ("k0", 0), ("pH", -2), ("k1", 0), ("H", -2),
           ("dc", 0), ("pT", -1), ("k2", 0)],
}
BATCH = [(1, 2), (3, 2)]
NB, FIRST = len(BATCH), 14
LB = [4000.0, 4000.0, 2800.0, 2800.0]
HOP, WIN, YF, BIAS = 210.0, 60.0, 8, 2000.0
GAM, SIG, CYC, PEC = 1.35, 3.3, 0.86, 0.47
LAT, RATE = 1200.0, 450.0
LZ, LF = [3300.0, 3000.0], [5000.0, 5000.0, 5000.0, 4500.0, 3200.0, 3300.0]
ACTC = [0, 0, 4, 0, 2, 1]

SCRATCH = {}
for _d, _l in (("bfloat16", "TB 4096 SB 3072 LD 4096 VN 3120 VR 1536 G 3072 RP 128 IP 144 WS 36 WA 128 WK 512 WO 512 KS 96 CA 96 CB 96 CN 96 "
                            "AT 256 SM 384 SG 128 SR 36 ID 128 NI 128 IS 128 BO 128 DM 96 P1 288 FQ 96 E 24 SO 2 ON 1024 CK 192 CW 312 "
                            "RA0 96 RA1 96 RB 96 RC 96 M0 18 M1 18 M2 40 M3 40 R0 72 R1 72 R2 160 R3 160"),
               ("int32", "IV 96 SU 96 SU2 96 PI 1 PJ 6 I1 38 I2 38 I3 38 J128 128 JK 36 JJ 128 JL 96 JG 128"),
               ("float32", "CAP 96 YI 96 PF 40 JX 128 RZ 36 MK 8 SK 96 XD 96 XS 96 SEL 96 LF 144"),
               ("uint16", "L1 6 OW 192 MS 108 LP 160 IU 38 DU0 54 DU1 54 DU2 54 DU3 54")):
    _l = _l.split()
    for _k in range(0, len(_l), 2):
        SCRATCH[_l[_k]] = ("sbuf", [128, int(_l[_k + 1])], _d)
for _c in range(NC):
    for _n, _s, _d in (("X", ROWS * Q, "bfloat16"), ("O", 2 * Q, "uint16"), ("OG", 2 * QH, "uint16"),
                       ("G3", 3 * Q, "bfloat16"), ("NV", Q, "bfloat16"),
                       ("SC", 36, "float32"), ("DL", 36 * RO, "bfloat16"), ("NR", 36, "bfloat16")):
        SCRATCH["%s%d" % (_n, _c)] = ("sbuf", [128, _s], _d)
for _n in ("pK0", "pK1", "pK2", "pH0", "pH1", "pH2", "pT", "pY"):
    SCRATCH[_n] = ("psum", [128, 512], "float32")

SEMAPHORES = (["q_pe", "q_dve", "q_act", "q_g", "ls"] + ["d%d" % k for k in range(40)]
              + ["a%s%d" % (n, r) for n in ("z", "t0", "t1", "t2", "t3", "t4", "t5", "o0", "o1", "o2", "o3") for r in range(N)])


def _engine_sets(topo, cores, src):
    peers = [c for c in cores if c != src]
    every = {c: list(topo.engines(src, c)) for c in peers}
    few = min(len(e) for e in every.values())
    far = [c for c in peers if len(every[c]) == few]
    near = [c for c in peers if c not in far]
    out, used = {}, []
    share = few // len(far)
    for k, c in enumerate(far):
        out[c] = every[c][k * share:(k + 1) * share]
        used += out[c]
    for c in near:
        out[c] = [e for e in every[c] if e not in used]
        used += out[c]
    return far, near, out


def build(g, core, T, topo):
    rho = T.rank_of(core)
    cores = list(T.cores)
    far, near, eng = _engine_sets(topo, cores, core)
    rk = {c: T.rank_of(c) for c in cores}
    rfar, rnear = [rk[c] for c in far], rk[near[0]]
    ops = []
    last_w, readers, bank = {}, {}, {}
    prev_fixed = {}
    ndma, load = [0], [0.0]
    cur = [None]

    def add(q, fn, r, w, dur, lat=0.0, kind="c", sem=None, cnt=0, fixed=False):
        i = len(ops)
        deps = set()
        for x in list(r) + list(w):
            if x[0] == "p":
                for j in bank.get(x, []):
                    if ops[j]["q"] != q:
                        deps.add(j)
        for x in r:
            if x in last_w:
                deps.add(last_w[x])
        for x in w:
            if x in last_w:
                deps.add(last_w[x])
            deps.update(readers.get(x, []))
        for x in r:
            readers.setdefault(x, []).append(i)
        for x in w:
            last_w[x] = i
            readers[x] = []
        for x in set(list(r) + list(w)):
            if x[0] == "p":
                old = bank.get(x, [])
                bank[x] = (old if old and ops[old[0]]["q"] == q else []) + [i]
        deps.discard(i)
        order = set()
        if q == "pe":
            order = {j for j in deps if ops[j]["q"] == "pe"}
            deps -= order
        if fixed:
            if q in prev_fixed:
                order.add(prev_fixed[q])
            prev_fixed[q] = i
        if kind == "dma":
            sem, cnt = "d%d" % ndma[0], 16
            ndma[0] += 1
        ops.append(dict(ch=cur[0], q=q, fn=fn, deps=deps, order=order, dur=dur, lat=lat, kind=kind, sem=sem, cnt=cnt))
        return i

    V_, S_, P_ = g.vector, g.scalar, g.tensor

    def vcost(n, f=1.0):
        return max(64.0, n * f) * CYC

    def ga(n):
        return 55.0 + GAM * n

    def sc(n):
        return 55.0 + SIG * n

    def ts(out, in0, s1, s2, o0, o1, r, w, n=1):
        if o1 is None:
            add("dve", lambda: V_.tensor_scalar(out, in0, s1, None, o0), r, w, vcost(n))
        else:
            add("dve", lambda: V_.tensor_scalar(out, in0, s1, s2, o0, o1), r, w, vcost(n))

    def tt(out, a, b, op, r, w, n=1, dur=None):
        add("dve", lambda: V_.tensor_tensor(out, a, b, op), r, w, dur or vcost(n))

    def cp(out, a, r, w, n=1, dur=None):
        add("dve", lambda: V_.tensor_copy(out, a), r, w, dur or vcost(n))

    def ms(ap, val, w, n=1):
        add("dve", lambda: V_.memset(ap, val), [], w, vcost(n, 0.5))

    def act(out, a, r, w, n=1, dur=None, bias=0.0, scale=1.0):
        add("act", lambda: S_.activation(out, a, AF.Identity, bias=bias, scale=scale), r, w, dur or vcost(n))

    def mm(out, l, rr, st, sp, r, w, m, n):
        add("pe", lambda: P_.matmul(out, l, rr, st, sp), r, w, max(min(64, m), n) * PEC)

    def dma(q, out, a, r, w, nbytes, first=False):
        e = {"sync": g.sync, "act": g.scalar}[q]
        load[0] = (load[0] if first else 0.0) + nbytes / RATE
        add(q, lambda: e.dma_start(out, a), r, w, 60.0, lat=LAT + load[0], kind="dma", fixed=True)

    def iota(out, pat, base, cm, w, n, flt):
        if flt:
            add("g", lambda: g.iota(out, pat, base, cm, allow_small_or_imprecise_dtypes=True), [], w, 130.0 + 2 * n * CYC, fixed=True)
        else:
            add("g", lambda: g.iota(out, pat, base, cm), [], w, 130.0 + 2 * n * CYC, fixed=True)

    def gcp(out, a, r, w):
        add("g", lambda: g.affine_select(out, a, [[0, Q]], ALU.is_ge, 0.0, 0, 0), r, w, 170.0 + 2 * Q * CYC)

    def send(name, peers, src, dst, r, w_in, lat, alone=False):
        use = {c: list(topo.engines(core, c)) if alone else eng[c] for c in peers}

        def fn():
            trs = []
            for c in peers:
                rid, pid = topo.addr(c, core)
                trs.append(RemoteDMATransfer(dst_ids=[DstId(rid=rid, pnc=pid)], dma_engine_mask=sum(1 << e for e in use[c]),
                                             remote_sem=T.sem["a%s%d" % (name, rho)], src=src(rk[c]), dst=dst))
            return g.remote_dma_fused(trs, local_sem=T.sem["ls"])
        i = add("g", fn, r, [], 800.0, kind="send", cnt=sum(len(use[c]) for c in peers), fixed=True)
        for c in sorted(peers, key=lambda c: c in far):
            k = len(topo.engines(c, core) if alone else _engine_sets(topo, cores, c)[2][core])
            j = add("rx", None, [], [w_in(rk[c])], 0.0, lat=lat * (0.8 if c in near else 1.0), kind="rx",
                    sem="a%s%d" % (name, rk[c]), cnt=k)
            ops[j]["order"].add(i)

    def blk(r, n=32):
        return slice(n * r, n * r + n)

    def retag(nm):
        cur[0] = cur[0] and (nm, cur[0][1])

    order = sorted(far, key=lambda c: topo.die(c) != topo.die(core)) + near
    peers = [rk[c] for c in order]
    TBall = ["TB%d_%d" % (j, x) for j in range(len(CUT)) for x in range(4)] + ["TBo"]


    def stage(j):
        k, a, b = CUT[j]
        if k != 1:
            dma("sync", T.SB[:, 1024 * k + a // 4:1024 * k + b // 4], T.dem[blk(peers[k]), a:b], [],
                ["SB%d_%d" % (j, x) for x in range(4)], 64 * (b - a), True)
        for x in range(4 * (k == 1 and a == 0)):
            dma("sync", T.SB[blk(x), blk(k, 1024)], T.dem[blk(peers[k]), blk(x, 1024)], [],
                ["SB%d_%d" % (i, x) for i in range(len(CUT)) if CUT[i][0] == k], 65536, True)

    def piece(j):
        k, a, b = CUT[j]
        send("t%d" % j, [order[k]], lambda r: T.SB[:, 1024 * k + a // 4:1024 * k + b // 4], T.LD[:, 1024 * rho + a // 4:1024 * rho + b // 4],
             ["SB%d_%d" % (j, x) for x in range(4)], lambda r: "LD%d" % j, LF[j], alone=k < 2)

    stage(0)
    dma("act", T.IV[:], T.inv[:], [], ["IV"], 49152, True)
    dma("act", T.WS[:, 0:32], T.wt[:], [], ["WS"], 8192, True)
    for c in range(NC):
        dma("sync" if c < 2 else "act", T.VN[:, VS * c:VS * c + VW], T.v[:, blk(c, VW)], [], ["V%d" % c], 256 * VW, True)
    dma("sync", T.TB[:], T.dem[:], [], TBall, 1048576, True)
    for j in range(1, len(CUT)):
        stage(j)
    dma("sync", T.SU[0:32, :], T.sup[blk(rho), :], [], ["SUa"], 12288, True)
    dma("sync", T.SU[32:64, :], T.sup[blk(rho), :], [], ["SUb"], 12288, True)
    iota(T.PI[:], [[0, 1]], 0, 1, ["PI"], 1, False)
    iota(T.J128[:], [[1, 128]], 0, 0, ["J128"], 128, False)
    iota(T.CW[0:1, 216:312], [[4 * VS, NC], [64, Q]], 0, 0, ["BR"], 96, True)
    iota(T.JK[:], [[32, 2], [1, 18]], 0, 0, ["JK"], 36, False)
    piece(0)
    iota(T.I1[:], [[1, ROWS], [0, QH]], 15, 0, ["I1"], ROWS * QH, False)
    iota(T.I2[:], [[0, ROWS], [256, QH]], 0, 0, ["I2"], ROWS * QH, False)
    iota(T.JX[:], [[0, 4], [1000, 2], [1, 16]], 0, 0, ["JX"], 128, True)
    for j in range(1, LATE):
        piece(j)

    PF = lambda k, a=0, b=128: T.PF[a:b, k:k + 1]
    cp(PF(0), T.PI[:], ["PI"], ["F0"])
    for k, (v, op) in enumerate(((31, ALU.bitwise_and), (15, ALU.bitwise_and), (4, ALU.arith_shift_right), (63, ALU.bitwise_and),
                                 (6, ALU.arith_shift_right), (16, ALU.bitwise_and))):
        ts(T.PJ[:, k:k + 1], T.PI[:], v, None, op, None, ["PI"], ["J%d" % k])
    cp(T.PF[:, 1:7], T.PJ[:], ["J%d" % k for k in range(6)], ["F1"])
    ts(T.JJ[:], T.J128[:], 31, None, ALU.bitwise_and, None, ["J128"], ["JJ"], 128)
    ts(T.JL[:], T.J128[:, 0:96], 15, None, ALU.bitwise_and, None, ["J128"], ["JL"], 96)
    ts(T.JG[:], T.J128[:], 4, None, ALU.arith_shift_right, None, ["J128"], ["JG"], 128)
    ts(T.MK[:], T.J128[:, 0:8], PF(3), None, ALU.is_equal, None, ["J128", "F1"], ["MK"])
    act(PF(24), PF(1), ["F1"], ["F24"], bias=PF(6))
    act(PF(27), PF(0), ["F0"], ["F27"], bias=-96.0)
    act(PF(7), PF(0), ["F0"], ["F4"], bias=-32.0 * rho)
    act(PF(9), PF(5), ["F1"], ["F6"], scale=-2.0, bias=1.0)
    act(PF(26), PF(5), ["F1"], ["F26"], scale=2.0, bias=-1.0)
    act(PF(11), PF(2), ["F1"], ["F8"], scale=16.0)
    act(PF(15), PF(0), ["F0"], ["F15"], bias=-64.0)
    act(PF(17), PF(5), ["F1"], ["F170"], scale=1000.0, bias=PF(4))
    act(PF(18), PF(17), ["F170"], ["F171"], bias=-16.0)
    ms(PF(8, 0, 32), 1.0, ["F5a"]); ms(PF(8, 32, 64), -1.0, ["F5b"]); ms(PF(8, 64, 128), 0.0, ["F5c"])
    F5, F6 = ["F5a", "F5b", "F5c"], ["F6"]
    ms(PF(14, 0, 32), -65536.0, ["F11a"]); ms(PF(14, 32, 64), -512.0, ["F11b"])
    ts(PF(16), PF(0), 112.0, None, ALU.is_equal, None, ["F0"], ["F16"])
    ts(PF(10), PF(0), 113.0, float(Q), ALU.is_equal, ALU.mult, ["F0"], ["F10"])
    ts(T.ID[:], T.J128[:], PF(0), None, ALU.is_equal, None, ["J128", "F0"], ["ID"], 128)
    act(T.NI[:], T.ID[:], ["ID"], ["NI"], 128, scale=-1.0)
    act(T.IS[:], T.ID[:], ["ID"], ["IS"], 128, scale=float(Q))
    act(T.SEL[:], T.ID[:, 0:96], ["ID"], ["SEL"], 96, scale=512.0)
    for k, v in enumerate((0.25, 16.0, 31.5, 2.0 ** 29, -2.0 ** 29, 0.0, 1.5 * 2.0 ** 27, -1.5 * 2.0 ** 27)):
        ms(T.ON[0:1, blk(k, 128)], v, ["ON%d" % k])
    ms(T.CK[0:1, :], 65.0, ["CK"])
    ms(T.RZ[:], 0.0, ["RZ0", "RZ1", "RZ2"])
    for k, (a, v) in enumerate(((slice(16, 36, 18), CR), (slice(17, 36, 18), -CR), (slice(18, 19), 4 * LOW))):
        ms(T.RZ[:, a], v, ["RZ%d" % k])
    for qh in range(QH):
        ts(T.AT[0:96, blk(qh, 128)], T.JX[0:96, :], PF(17 + qh, 0, 96), float(Q), ALU.is_equal, ALU.mult, ["JX", "F17%d" % qh], ["A%d" % qh], 128)
        for k, (a, b) in enumerate(((0, 32), (32, 64), (64, 128))):
            x = 32 + 3 * qh + k
            ts(PF(x, 96), PF(16, 96), 9.0 * Q + 16 * qh, PF(10, 96) if k < 2 else 0.0, ALU.mult, (ALU.subtract, ALU.add, ALU.add)[k],
               ["F16", "F10"], ["F%d" % x])
            act(T.AT[96:128, 128 * qh + a:128 * qh + b], T.ID[96:128, 0:b - a], ["ID", "F%d" % x], ["A%d_%d" % (qh, k)], bias=PF(x, 96))
    act(T.FQ[0:96, :], T.ID[0:96, 0:96], ["ID"], ["FQ"], 96, scale=16.0)
    act(PF(22, 96), PF(16, 96), ["F16"], ["F22"], scale=-120.0)
    act(T.FQ[96:128, :], T.ID[96:128, 0:96], ["ID", "F22"], ["FQc"], 96, bias=PF(22, 96))
    for m in range(2):
        mask = T.MK[:, 2 * rho + m:2 * rho + m + 1]
        act(T.SO[:, m:m + 1], mask, ["MK"], ["SO%d" % m], scale=-1.0)
        ts(T.SM[:, blk(m, 96)], T.JJ[:, 0:96], PF(7), mask, ALU.is_equal, ALU.mult, ["JJ", "F4", "MK"], ["SM%d" % m], 96)
        ts(T.SM[:, blk(2 + m, 96)], T.JJ[:, 0:96], PF(27), T.MK[:, 6 + m:7 + m], ALU.is_equal, ALU.mult, ["JJ", "F27", "MK"], ["SM%d" % (2 + m)], 96)
    ts(T.RP[:], T.JJ[:], PF(7), None, ALU.is_equal, None, ["JJ", "F4"], ["RP"], 128)
    for k, r in enumerate(peers + [rho]):
        act(PF(28 + k), T.MK[:, 2 * r:2 * r + 1], ["MK"], ["F28%d" % k], bias=T.MK[:, 2 * r + 1:2 * r + 2])
        ts(T.IP[:, blk(k, 36)], T.JK[:], PF(24), PF(28 + k), ALU.is_equal, ALU.mult, ["JK", "F24", "F28%d" % k], ["IP%d" % k])
    ts(T.BO[:], T.JG[:], PF(3), -1.0, ALU.is_equal, ALU.mult, ["JG", "F1"], ["BO"], 128)
    ts(T.DM[:], T.JL[:], PF(2), None, ALU.is_equal, None, ["JL", "F1"], ["DM"], 96)
    ts(T.SK[:], T.JL[:], 0.0, None, ALU.not_equal, None, ["JL"], ["SK"], 96)
    ms(T.WS[:, 32:36], 0.0, ["WSz"])
    ms(T.WA[:], 0.0, ["WA%d" % r for r in range(N)], 128)
    ts(T.SG[:], T.JJ[:], PF(1), PF(9), ALU.is_equal, ALU.mult, ["JJ", "F1"] + F6, ["SG"], 128)
    ts(T.SR[:], T.JK[:], PF(24), 512.0, ALU.is_equal, ALU.mult, ["JK", "F24"], ["SR"])
    for k in (NB, NB + 1):
        ms(T["M%d" % k][:], 0.0, ["M%d" % k] + ["L%d_%d%d" % (k, c, m) for c in range(NC) for m in range(2)])
    ms(T.E[0:64, :], 0.0, ["E%d_%d_0" % (c, t) for c in range(NC) for t in range(RO + 1)])
    ms(T.E[64:128, :], 1.0, ["Ec"] + ["E%d_%d_1" % (c, t) for c in range(NC) for t in range(RO + 1)])
    ts(T.KS[64:128, :], T.JJ[64:128, 0:96], PF(15, 64), PF(16, 64), ALU.is_equal, ALU.max, ["JJ", "F15", "F16"], ["KSc"], 96)
    ts(T.NR0[0:64, :], T.JK[0:64, :], PF(24, 0, 64), PF(14, 0, 64), ALU.is_equal, ALU.mult, ["JK", "F24", "F11a", "F11b"], ["NRa0"])
    for m in range(2):
        ts(T.NR0[96:128, 18 * m:18 * m + 16], T.JK[96:128, 0:16], -32.0, 472.0, ALU.mult, ALU.add, ["JK"], ["NRb%d" % m])
        ms(T.NR0[96:128, 18 * m + 16:18 * m + 18], LOW, ["NRc%d" % m])
    for c in range(NC):
        s = str(c)
        if c:
            act(T["NR" + s][0:64, :], T.NR0[0:64, :], ["NRa0"], ["NRa" + s])
            act(T["NR" + s][96:128, :], T.NR0[96:128, :], ["NRb0", "NRb1", "NRc0", "NRc1"], ["NRd" + s])
        for k in range(2):
            ms(T["DL" + s][0:Q, 16 + k::18], 0.0, ["DLz%s%d" % (s, k)])
        ms(T.VN[:, VS * c + VW:VS * c + VS], 0.0, ["Vj" + s], VW)
    Vall = ["V%d" % c for c in range(NC)] + ["Vj%d" % c for c in range(NC)]
    ts(T.SU2[0:32, :], T.SU[0:32, :], 7, None, ALU.arith_shift_right, None, ["SUa"], ["S2a"], 96)
    ts(T.SU2[32:64, :], T.SU[32:64, :], 127, None, ALU.bitwise_and, None, ["SUb"], ["S2b"], 96)
    cp(T.KS[0:64, :], T.SU2[0:64, :], ["S2a", "S2b"], ["KS"], 96)
    ts(T.CA[:], T.IV[:], 0.0, 17.0, ALU.is_lt, ALU.mult, ["IV"], ["CA"], 96)
    ts(T.CB[:], T.IV[:], -8.0, None, ALU.add, None, ["IV"], ["CB"], 96)
    tt(T.CN[:], T.CA[:], T.CB[:], ALU.add, ["CA", "CB"], ["CN"], 192)
    ts(T.CAP[:], T.CA[:], -6.0, 101.0, ALU.mult, ALU.add, ["CA"], ["CAP"], 96)
    ts(T.I3[:], T.I1[:], PF(8), None, ALU.add, None, ["I1"] + F5, ["I3"])
    ts(T.I1[:], T.I3[:], 15, None, ALU.bitwise_and, None, ["I3"], ["I1"])
    tt(T.I3[:], T.I1[:], T.I2[:], ALU.add, ["I1", "I2"], ["I3"])
    ts(T.IU[:], T.I3[:], PF(11), None, ALU.add, None, ["I3", "F8"], ["IU"])
    for c in range(NC):
        s, f = str(c), (act, cp, act)[c]
        mm(T["pK" + s][:], T.RP[:], T.VN[:, VS * c:VS * c + VW], True, True, ["RP", "V" + s], ["pK" + s], 128, VW)
        f(T.VR[:, blk(c, VW)], T["pK" + s][:], ["pK" + s], ["VR" + s], VW)

    def places(O, W, P, K, n, rd, bk, nO):
        p, h = P[0:K, n:2 * n], T[bk][:, 0:2 * n]

        def const(k, st, sp):
            mm(h, T.ON[0:1, blk(2 + k, 128)], T.CK[0:1, 0:2 * n], st, sp, ["ON%d" % (2 + k), "CK"], [bk], 128, 2 * n)
        retag("z")
        const(0, True, False)
        retag("pH")
        for eh in range(2):
            mm(T[bk][:, blk(eh, n)], W[0:K, 256 + eh:512:2], p, False, False, rd, [bk], 128, n)
        const(1, False, False)
        const(2, False, False)
        for eh in range(2):
            mm(h, W[0:K, eh:256:2], P[0:K, n - n * eh:3 * n - n * eh], False, eh == 1, rd, [bk], 128, 2 * n)
        retag("O")
        ts(O, h, 4095.0, None, ALU.min, None, [bk], [nO], 2 * n)

    mm(T.pY[:, 0:96], T.ON[0:1, 0:128], T.CW[0:1, 216:312], True, False, ["ON0", "BR"], ["pY"], 128, 96)
    mm(T.pY[:, 0:96], T.BO[:], T.CA[:], False, False, ["BO", "CA"], ["pY"], 128, 96)
    mm(T.pY[:, 0:96], T.BO[:], T.CB[:], False, True, ["BO", "CB"], ["pY"], 128, 96)
    tt(T.XD[:], T.pY[:, 0:96], T.DM[:], ALU.mult, ["pY", "DM"], ["XD"], 96)
    add("dve", lambda: V_.tensor_tensor_scan(T.XS[:], T.SK[:], T.XD[:], 0.0, ALU.mult, ALU.add), ["SK", "XD"], ["XS"], vcost(96))
    ts(T.L1[:], T.XS[:, 15::16], 8.0, None, ALU.add, None, ["XS"], ["L1"])
    ms(T.P1[:, 0:96], 0.0, ["P1a"]); ms(T.P1[:, 192:288], 0.0, ["P1b"])
    for c in range(NC):
        ms(T["G3%d" % c][:, 0:Q], 0.0, ["G3a%d" % c]); ms(T["G3%d" % c][:, 2 * Q:3 * Q], 0.0, ["G3b%d" % c])
    cp(T.P1[:, 96:192], T.VN[:].indirect(T.L1[:]), Vall + ["L1"], ["P1"], dur=ga(96))
    for k in range(8):
        act(T.WO[:, blk(k)], T.WS[:, 0:32], ["WS", "MK"], ["WO%d" % k], scale=T.MK[:, k:k + 1])
    act(T.WO[:, 256:512], T.WO[:, 0:256], ["WO%d" % k for k in range(8)], ["WO"], 256, scale=-1.0)
    places(T.OW[:], T.WO, T.P1, 128, 96, ["WO", "P1", "P1a", "P1b"], "pH0", "OW")
    Gn = lambda a, b: ["G%d_%d" % (x // (2 * Q), x % (2 * Q)) for x in range(a, b, 2)]
    for nm, a, b in PIECES_ONE:
        (cp if nm[0] == "g" else act)(T.G[:, 16 * a:16 * b], T.TB[:].indirect(T.OW[:, a:b]), TBall + ["OW"], Gn(a, b), dur=ga(16 * (b - a)))
    for k in range(3):
        bk = "pH%d" % (1 + k // 2)
        mm(T[bk][96:128, blk(k % 2, 36)], T.ID[:, blk(peers[k])], T.WS[:], True, True, ["ID", "WS", "WSz"], [bk], 32, 36)
    for eh in range(2):
        for h in range(2):
            for el in range(16):
                mm(T["pH%d" % (1 + h)][0:96, 0:72], T.G[:, 1536 * eh + el:1536 * eh + 1536:16], T.IP[:, blk(h, 72)],
                   eh == 0 and el == 0, eh == 1 and el == 15, ["IP%d" % (2 * h), "IP%d" % (2 * h + 1)] + Gn(96 * eh, 96 * eh + 96),
                   ["pH%d" % (1 + h)], 96, 72)
    cp(T.MS[:, 0:72], T.pH1[:, 0:72], ["pH1"], ["MSf"], 72)
    cp(T.MS[:, 72:108], T.pH2[:, 0:36], ["pH2"], ["MSn"])
    cp(T.LF[0:96, blk(rho, 36)], T.pH2[0:96, 36:72], ["pH2"], ["LF%d" % rho])
    for ps, nm, lat in ((far, "MSf", LZ[0]), (near, "MSn", LZ[1])):
        send("z", ps, lambda r: T.MS[:, blk(peers.index(r), 36)], T.LP[:, 40 * rho:40 * rho + 36], [nm], lambda r: "LP%d" % r, lat)
    for j in range(LATE, len(CUT)):
        piece(j)
    u4 = 64 // Q
    for ty, (st, b) in enumerate(((u4, 38), (-64, -34 * Q), (u4, 30))):
        iota(T.CW[0:1, blk(ty, 18)], [[0, 18 // QH], [st, QH]], b, 0, ["CW"], 18, True)
    iota(T.CW[0:1, 54:108], [[4, 3], [0, 18 // QH], [-u4, QH]], -8, 0, ["CW"], 54, True)
    iota(T.CW[0:1, 108:162], [[0, 54 // QH], [16, QH]], 0, 0, ["CW"], 54, True)
    iota(T.CW[0:1, 162:216], [[0, 54]], 1, 0, ["CW"], 54, True)
    iota(T.CW[0:1, 180:198], [[0, 18]], Q, 0, ["CW"], 18, True)
    for c in range(NC):
        s = str(c)
        (act, cp, act)[c](T["X" + s][:], T.VR[:, blk(c, VW)].indirect(T.IU[:]), ["VR" + s, "IU"] + (["MSf", "MSn", "LF%d" % rho] if c == 1 else Gn(0, 192)), ["X" + s], dur=ga(ROWS * Q))
    for j, (k, a, b) in enumerate(CUT):
        r, w = peers[k], (b - a) // 4
        cols = slice(1024 * r + a // 4, 1024 * r + b // 4)
        if k != 1:
            dma("sync", T.TB[blk(r), a:b], T.LD[:, cols], ["LD%d" % j], TBall[4 * j:4 * j + 4], 64 * (b - a))
        for x in range(4 * (k == 1)):
            f, n = (act, w) if x < ACTC[j] else (cp, w // 2)
            f(T.TB[blk(r), 1024 * x + a // 4:1024 * x + b // 4], T.LD[blk(x), cols], ["LD%d" % j], ["TB%d_%d" % (j, x)], n)
    for r in [rho, rnear] + rfar:
        src, nm, a = T.WS[:, 0:32], "WS", 0
        if r != rho:
            cp(T.LF[:, blk(r, 36)], T.LP[:, 40 * r:40 * r + 36], ["LP%d" % r], ["LF%d" % r])
            cp(T.WA[96:128, blk(r)], T.LF[96:128, 36 * r:36 * r + 32], ["LF%d" % r], ["WA%d" % r])
            src, nm, a = T.WA[:, blk(r)], "WA%d" % r, 2
        for m in range(2):
            mm(T.pY[0:96, blk(2 * r + m)], T.SM[:, blk(a + m, 96)], src, True, True, ["SM%d" % (a + m), nm], ["pY"], 96, 32)
    ts(T.WK[0:96, 256:512], T.pY[0:96, 0:256], PF(26, 0, 96), None, ALU.mult, None, ["pY", "F26"], ["WN"], 256)
    act(T.WK[0:96, 0:256], T.WK[0:96, 256:512], ["WN"], ["WK"], 256, scale=-1.0)

    def B(n, c):
        return T["%s%d" % (n, c)]

    def step(c, t):
        s = str(c)

        def tag(nm):
            cur[0] = (nm, NC * t + c) if t > 1 else None
        X, SC, DL, OG, NR = B("X", c), B("SC", c), B("DL", c), B("OG", c), B("NR", c)
        E = lambda p, u: T.E[p, 8 * c + u:8 * c + u + 1]
        NRn = ["NRa" + s, "N" + s] + (["NRd" + s] if c else ["NRb0", "NRb1", "NRc0", "NRc1"])
        pK, pH = B("pK", c), B("pH", c)
        En = lambda u: ["E%d_%d_%d" % (c, u, m) for m in range(2)]
        mk = lambda m: slice(64 * m, 64 * m + Q)
        gd = lambda m: slice(18 * m, 18 * m + 16)
        key, g0 = pK[0:Q, 0:36], 32 * Q * c

        def changes(out, bk, upto, sp):
            for u in range(1, upto + 1):
                mm(out, T.ID[0:Q, 0:Q], DL[0:Q, blk(u - 1, 36)], False, sp and u == upto,
                   ["ID", "DLz%s0" % s, "DLz%s1" % s, "DL%s_%d0" % (s, u), "DL%s_%d1" % (s, u)], [bk], Q, 36)
        if t == 0:
            mm(key, T.CN[:, blk(c, Q)], T.IP[:, blk(3, 36)], True, True, ["CN", "IP3"], ["pK" + s], Q, 36)
            mm(pK[0:Q, 64:66], T.CN[:, blk(c, Q)], T.SO[:], True, True, ["CN", "SO0", "SO1"], ["pK" + s], Q, 2)
            for m in range(2):
                act(E(mk(m), 0), pK[0:Q, 64 + m:65 + m], ["pK" + s], [En(0)[m]])
            act(NR[mk(1), :], key, ["pK" + s], ["N" + s], bias=8.0)
        else:
            for nm, a, b in [] if t == 1 else PIECES_END if (t == 2 and c == 0) or (t == RO and c == NC - 1) else PIECES:
                tag(nm)
                (cp if nm[0] == "g" else act)(T.G[:, g0 + 16 * a:g0 + 16 * b], T.TB[:].indirect(B("O", c)[:, a:b]),
                                              TBall + ["O" + s], ["G%s_%d" % (s, x) for x in range(a, b, 2)], dur=ga(16 * (b - a)))
            tag("k0")
            mm(key, T.KS[0:113, blk(c, Q)], NR[0:113, :], True, False, ["KS", "KSc"] + NRn, ["pK" + s], Q, 36)
            changes(key, "pK" + s, t - 1, False)
            for r in [rho, rnear] + rfar if t == 1 else []:
                tag("k4")
                mm(key, T.SEL[0:96, blk(c, Q)], T.LF[0:96, blk(r, 36)], False, r == rfar[-1], ["SEL", "LF%d" % r], ["pK" + s], Q, 144)
            for eh in range(2 if t > 1 else 0):
                a = g0 + 16 * Q * eh
                for el in range(16):
                    tag("k%d" % (2 * eh + el // 8 + 1))
                    mm(key, T.G[:, a + el:a + 16 * Q:16], T.SR[:], False, eh == 1 and el == 15,
                       ["SR"] + ["G%s_%d" % (s, x) for x in range(Q * eh, Q * eh + Q, 2)], ["pK" + s], Q, 36)
            tag("SC")
            add("dve", lambda: V_.tensor_tensor_scan(SC[0:Q, :], T.RZ[0:Q, :], key, LOW, ALU.add, ALU.max),
                ["RZ0", "RZ1", "RZ2", "pK" + s], ["SC" + s], vcost(36))
            tag("E")
            for m in range(2):
                ts(E(mk(m), t), SC[0:Q, 18 * m + 15:18 * m + 16], SC[0:Q, 18 * m + 17:18 * m + 18],
                   -8.0 if t == 1 else pK[mk(m), 65:66], ALU.subtract, ALU.max, ["SC" + s, "pK" + s], [En(t)[m]])

        def rows(out, a, K, bk):
            for qh in range(QH):
                mm(out[:, a + qh:a + qh + 1], T.AT[0:K, blk(qh, 128)], E(slice(0, K), t), True, True,
                   ["A%d" % qh, "Ec"] + ["A%d_%d" % (qh, k) for k in range(3)] + En(t), [bk], 128, 1)
        if 0 < t < RO:
            tag("pT")
            rows(pK, 72, 113, "pK" + s)
            tag("OG")
            ts(OG[:, 0:QH], pK[:, 72:72 + QH], PF(2), None, ALU.add, None, ["pK" + s, "F1"], ["OG" + s])
        if 0 < t < RO - 1:
            tag("D")
            rows(pK, 72 + QH, 114, "pK" + s)
        if t > 0:
            tag("H")
            rows(T.pT, 6 * (t - 1) + QH * c, 113, "pT")
            tag("D")
            mm(pK[0:96, 64:65], T.ID[0:96, 0:96], E(slice(0, 96), t - 1), True, False, ["ID"] + En(t - 1), ["pK" + s], 96, 1)
            mm(pK[0:96, 64:65], T.NI[0:96, 0:96], E(slice(0, 96), t), False, True, ["NI"] + En(t), ["pK" + s], 96, 1)
            if t < RO:
                mm(pK[0:96, 65:66], T.FQ[0:113, :], E(slice(0, 113), t), True, True, ["FQ", "FQc", "Ec"] + En(t), ["pK" + s], 96, 1)
            tag("DL")
            if t < RO - 1:
                tag("OS")
                ts(OG[:, blk(1, QH)], pK[:, 72 + QH:72 + 2 * QH], PF(2), None, ALU.add, None, ["pK" + s, "F1"], ["OS" + s])
            lab = lambda k, m: (B("M", k)[blk(c), 8 + 16 * m:24 + 16 * m], "L%d_%d%d" % (k, c, m))
            for m in range(2):
                tag("L%d" % m)
                a = 36 * (t - 1) + 18 * m
                out, nm = (DL[0:Q, a:a + 16], "DL%s_%d%d" % (s, t, m)) if t < RO else lab(NB + 1, m)
                ts(out, pK[0:Q, gd(m)], SC[0:Q, 18 * m + 15:18 * m + 16], pK[mk(m), 64:65],
                   ALU.is_equal, ALU.mult, ["pK" + s, "SC" + s], [nm])
        if t == RO and c in (0, NC - 1):
            tag("M")
            k, a, b = (NB, 24, 30 + QH) if c == 0 else (NB + 1, 30 + QH, 36)
            act(B("M", k)[:, 0:b - a], T.pT[:, a:b], ["pT"], ["M%d" % k], scale=1.0 / Q)
        if 0 < t < RO:
            Xr = ["X" + s, "Xa" + s, "Xb" + s]
            tag("G3")
            cp(B("G3", c)[:, Q:2 * Q], X[:].indirect(OG[:, 0:QH]), Xr + ["OG" + s], ["G3" + s], dur=ga(Q))
            g3 = B("G3", c)[0:96, Q:2 * Q]
            places(B("O", c)[:], T.WK, B("G3", c), 96, Q, ["WK", "WN", "G3" + s, "G3a" + s, "G3b" + s], "pH" + s, "O" + s)
        if t == RO - 1:
            tag("N")
            mm(pH[blk(c), 256:292], T.ID[:, 64:64 + Q], NR[:], True, False, ["ID"] + NRn, ["pH" + s], Q, 36)
            changes(pH[blk(c), 256:292], "pH" + s, RO - 1, True)
            for m in range(2):
                act(lab(NB, m)[0], pH[blk(c), 256 + 18 * m:272 + 18 * m], ["pH" + s], [lab(NB, m)[1]])
        if 0 < t < RO - 1:
            tag("SG")
            mm(pH[:, 128:128 + Q], T.SG[0:96, :], g3, True, True, ["SG", "G3" + s], ["pH" + s], 128, Q)
            tag("NV")
            act(B("NV", c)[:], pH[:, 128:128 + Q], ["pH" + s], ["NV" + s], Q)
            tag("X")
            cp(X[:].indirect(OG[:, blk(1, QH)]), B("NV", c)[:], ["NV" + s, "OS" + s], Xr, dur=sc(Q))
            gcp(X[0:32, blk(16, Q)], X[0:32, blk(0, Q)], ["X" + s], ["Xa" + s])
            gcp(X[32:64, blk(1, Q)], X[32:64, blk(17, Q)], ["X" + s], ["Xb" + s])
        cur[0] = None

    def publish(k, w, r):
        send("o%d" % k, far + near, lambda _: B("M", k)[:, 0:w], B("R", k)[:, blk(rho, w)], r, lambda x: "R%d%d" % (k, x), LB[k])

    def offsets(k, w, ws, co):
        bk = "pT" if co else "pY"
        Y, DU = T[bk], B("DU", k)
        cur[0] = "replay" if k < NB else None
        i0 = len(ops)

        def row(a, b, st, sp):
            mm(Y[:, 0:54], T.ON[0:1, blk(a, 128)], T.CW[0:1, blk(b, 54)], st, sp, ["ON%d" % a, "CW"], [bk], 128, 54)

        def slots(lhs):
            for r in [rho, rnear] + rfar:
                src, sn = (B("M", k)[:, 0:w], "M%d" % k) if r == rho else (B("R", k)[:, ws * r:ws * r + w], "R%d%d" % (k, r))
                for ty in range(3):
                    mm(Y[blk(r), 18 * ty + co:18 * ty + co + w], T[lhs[ty]][:, blk(r)], src, False, False, [lhs[ty], sn], [bk], 32, w)
        row(0, 0, True, False)
        slots(("NI", "IS", "NI"))
        row(6, 3, False, False)
        row(7, 3, False, False)
        slots(("ID", "ID", "ID"))
        row(0, 1, False, False)
        row(1, 2, False, True)
        if k == 0:
            for i in range(i0, len(ops)):
                ops[i]["ch"] = ("dc", FIRST + (i - i0) // 8)
            cur[0] = ("DU", FIRST + 4)
        ts(DU[:], Y[:, 0:54], PF(11), None, ALU.add, None, [bk, "F8"], ["DU%d" % k])
        cur[0] = None

    def replay(steps, c):
        V, Vn = T.VN[:, blk(c, VS)], ["V%d" % c, "Vj%d" % c]
        a, b = Q * c, Q * c + Q
        nm = lambda x: [x + str(c)]
        o = lambda ty, j: B("DU", steps[j][0])[:, blk(9 * ty + 3 * steps[j][1] + c, QH)]
        rd = lambda j: Vn + ["DU%d" % steps[j][0]]

        def old(j):
            act(B("RA", j % 2)[:, a:b], V.indirect(o(1, j)), rd(j), nm("RA%d" % (j % 2)), dur=ga(b - a))
        old(0)
        for j in range(len(steps)):
            (act if j else cp)(T.RC[:, a:b], V.indirect(o(2, j)), rd(j), nm("RC"), dur=ga(b - a))
            tt(T.RB[:, a:b], V.indirect(o(0, j)), B("RA", j % 2)[:, a:b], ALU.subtract, rd(j) + nm("RA%d" % (j % 2)), nm("RB"), dur=ga(b - a))
            if j + 1 < len(steps):
                old(j + 1)
            tt(V.indirect(o(1, j)), T.RB[:, a:b], T.RC[:, a:b], ALU.add, nm("RB") + nm("RC") + rd(j), Vn, dur=sc(b - a))

    for t in range(RO + 1):
        for c in range(NC):
            step(c, t)
            if t == RO and c in (0, NC - 1):
                k = NB + (c > 0)
                publish(k, 40, ["M%d" % k] + ["L%d_%d%d" % (k, x, m) for x in range(NC) for m in range(2)])
        for k, (t0, n) in enumerate(BATCH):
            if t == t0 + n - 1:
                cur[0] = ("M", NC * t + NC - 1)
                act(B("M", k)[:, 0:6 * n], T.pT[:, 6 * t0 - 6:6 * (t0 + n) - 6], ["pT"], ["M%d" % k], scale=1.0 / Q)
                cur[0] = None
                publish(k, 6 * n, ["M%d" % k])
    for k, (t0, n) in enumerate(BATCH):
        offsets(k, 6 * n, 6 * n, 0)
    offsets(NB, 6 + QH, 40, 0)
    for c in range(NC):
        replay([(k, u) for k, (t0, n) in enumerate(BATCH) for u in range(n)], c)
        replay([(NB, 0)] + [(NB, 1)] * (c == 0), c)
    offsets(NB + 1, 6 - QH, 40, QH)
    for c in range(NC):
        if c:
            replay([(NB + 1, 0)], c)
        dma("sync", T.yv[:, blk(c, VW)], T.VN[:, VS * c:VS * c + VW], ["V%d" % c], [], 256 * VW)
    for r in [rho, rnear] + rfar:
        for k in (NB, NB + 1):
            src, nm = B("R", k)[:, 40 * r + 8:40 * r + 40], ["R%d%d" % (k, r)]
            if r == rho:
                src, nm = B("M", k)[:, 8:40], ["L%d_%d%d" % (k, x, m) for x in range(NC) for m in range(2)]
            mm(T.pK0[blk(r), 0:96], src, T.ID[:, 0:96], k == NB, k > NB, ["ID"] + nm, ["pK0"], 32, 96)
    tt(T.YI[:], T.pK0[:, 0:96], T.CAP[:], ALU.min, ["pK0", "CAP"], ["YI"], 96)
    dma("act", T.yi[:], T.YI[:], ["YI"], [], 49152 * YF)
    return ops


def schedule(ops):
    n = len(ops)
    named = {}
    for i, o in enumerate(ops):
        named.setdefault((o["q"], o["ch"]), []).append(i)
    for q, names in ROUND.items():
        seq = [i for h in range(-4, NC * RO + 8) for nm, d in names for i in named.get((q, (nm, h + d)), [])]
        for a, b in zip(seq, seq[1:]):
            ops[b]["order"].add(a)
    succ = [[] for _ in range(n)]
    for i, o in enumerate(ops):
        for j in o["deps"] | o["order"]:
            succ[j].append(i)
    left = [len(o["deps"] | o["order"]) for o in ops]
    sequence = [i for i in range(n) if left[i] == 0]
    for i in sequence:
        for j in succ[i]:
            left[j] -= 1
            if left[j] == 0:
                sequence.append(j)
    assert len(sequence) == n
    prio = [0.0] * n
    for i in reversed(sequence):
        o = ops[i]
        best = 0.0
        for j in succ[i]:
            best = max(best, prio[j] + (o["lat"] + HOP if i in ops[j]["deps"] else 0.0))
        prio[i] = max(best, o["lat"]) + o["dur"]
    for i, o in enumerate(ops):
        prio[i] += BIAS if o["ch"] == "replay" else 0.0
    left = [len(o["deps"] | o["order"]) for o in ops]
    ready_at = [0.0] * n
    pool = [i for i in range(n) if left[i] == 0]
    free, order, end = {}, [], [0.0] * n
    while pool:
        start = {i: max(ready_at[i], free.get(ops[i]["q"], 0.0)) for i in pool}
        first = min(pool, key=lambda i: (start[i], -prio[i]))
        cand = [i for i in pool if ops[i]["q"] == ops[first]["q"] and start[i] <= start[first] + WIN]
        i = max(cand, key=lambda k: (prio[k], -k))
        pool.remove(i)
        o = ops[i]
        free[o["q"]] = start[i] + o["dur"]
        end[i] = start[i] + o["dur"] + o["lat"]
        order.append(i)
        for j in succ[i]:
            ready_at[j] = max(ready_at[j], end[i] + HOP if i in ops[j]["deps"] else start[i] + o["dur"])
            left[j] -= 1
            if left[j] == 0:
                pool.append(j)
    return order


def emit(g, T, ops, order):
    queue = {"pe": g.tensor, "dve": g.vector, "act": g.scalar, "g": g, "sync": g.sync}
    pos = {i: k for k, i in enumerate(order)}
    needed = set()
    for o in ops:
        last = {}
        for j in o["deps"]:
            key = ops[j]["q"] if ops[j]["kind"] == "c" else j
            if key not in last or pos[j] > pos[last[key]]:
                last[key] = j
        o["deps"] = set(last.values())
        needed |= o["deps"]
    known = {q: {} for q in queue}
    count, total, done = {}, {}, {}
    for i in order:
        o = ops[i]
        q = o["q"]
        if o["kind"] == "rx":
            done[i] = (o["sem"], o["cnt"], {})
            total[o["sem"]] = o["cnt"]
            continue
        kn = known[q]
        for j in sorted(o["deps"], key=lambda j: -pos[j]):
            s, v, clock = done[j]
            if kn.get(s, 0) < v:
                queue[q].wait_ge(T.sem[s], v)
                kn[s] = v
            for s2, v2 in clock.items():
                if kn.get(s2, 0) < v2:
                    kn[s2] = v2
        ins = o["fn"]()
        if o["kind"] == "send":
            total["ls"] = total.get("ls", 0) + o["cnt"]
        elif o["kind"] == "dma":
            ins.then_inc(T.sem[o["sem"]], 16)
            done[i] = (o["sem"], 16, dict(kn))
            total[o["sem"]] = 16
        elif i in needed:
            s = "q_" + q
            count[s] = count.get(s, 0) + 1
            ins.then_inc(T.sem[s], 1)
            done[i] = (s, count[s], dict(kn))
            total[s] = count[s]
    for s, v in total.items():
        if max(k.get(s, 0) for k in known.values()) < v:
            g.wait_ge(T.sem[s], v)


def rank_program(g, core, T, topo):
    if T.rank_of(core) is None:
        return
    ops = build(g, core, T, topo)
    emit(g, T, ops, schedule(ops))
